import numpy as np, ml_dtypes
CORES = [8,9,10,11,12,13]
N = 6
import mx_ref
BF = ml_dtypes.bfloat16
def cols(t, e):
    v = np.concatenate([t.reshape(128, -1, 4), np.zeros((128, 1, 4), BF)], axis=1)
    return np.ascontiguousarray(v[:, e]).reshape(128, -1)
def decode(q):
    o = []
    for b in range(4):
        e = np.zeros((128, 128, 4), np.float32); e[np.arange(128), np.arange(128), b] = 1
        o.append(mx_ref.matmul(mx_ref.quantize(e.reshape(128, 512).astype(BF)), q))
    return np.stack(o, axis=2).reshape(128, -1)
def f(rng, *shape):
    return mx_ref.flush((rng.standard_normal(shape, dtype=np.float32) * np.exp2(rng.integers(-2, 3, shape[:-1] + (1,)))).astype(BF))
def wide(rng, *shape, cols=0):
    v = rng.standard_normal(shape, dtype=np.float32) * np.exp2(rng.integers(-12, 13, shape)).astype(np.float32)
    if cols: v *= np.repeat(np.exp2(rng.integers(-cols, cols + 1, shape[:-2] + (1, shape[-1] // 4))) * (rng.random(shape[:-2] + (1, shape[-1] // 4)) > 0.0625), 4, axis=-1).astype(np.float32)
    return mx_ref.flush(v.astype(BF))
K = 512
def plant(t, k, v):
    o = t.astype(np.float32).reshape(128, -1, 4); o[:, k] = v
    return o.reshape(128, -1).astype(BF)
def setup_inputs(rng):
    return {"x": f(rng, N, 128, 512), "c1": f(rng, N, 128, 4 * K), "c2": f(rng, N, 128, 4 * K)}
def setup_inputs_last(rng):
    d = setup_inputs(rng); u = f(rng, 128, 4).astype(np.float32).reshape(128, 1, 4); x = []
    s = np.exp2(np.where(np.arange(128) < 120, 2, 0) + np.arange(128) % 2).astype(np.float32).reshape(1, 128, 1)
    for r in range(N):
        x.append(plant(d["x"][r], rng.permutation(128), u * s))
    d["x"] = np.stack(x)
    for c in ("c1", "c2"):
        d[c] = np.stack([plant(d[c][q], [K - 1], np.float32(2) * u) if q == N - 1 else d[c][q] for q in range(N)])
    return d
def setup_inputs_negative(rng):
    d = setup_inputs(rng)
    for c, s in (("x", 1), ("c1", -1), ("c2", -1)):
        d[c] = (np.abs(d[c].astype(np.float32)) * np.float32(s * 2.0 ** 20)).astype(BF)
    return d
def setup_inputs_own(rng):
    d = setup_inputs(rng)
    for c, s in (("c1", 2), ("c2", -2)):
        d[c] = np.stack([plant(d[c][r], rng.permutation(K)[:128], np.float32(s) * d["x"][r].astype(np.float32).reshape(128, -1, 4)) for r in range(N)])
    return d
def setup_inputs_spread(rng):
    d = setup_inputs(rng); d["x"] = wide(rng, N, 128, 512, cols=8)
    for c in ("c1", "c2"): d[c] = wide(rng, N, 128, 4 * K, cols=2)
    return d
def setup_inputs_ties(rng):
    d = setup_inputs(rng)
    d["x"] = np.stack([plant(d["x"][r], rng.permutation(128)[:1], np.zeros((128, 1, 4), np.float32)) for r in range(N)])
    for c in ("c1", "c2"):
        a = f(rng, N, 128, K)
        d[c] = np.stack([cols(np.concatenate([a[q], a[q], a[(q + 1) % N], a[(q + 2) % N]], axis=1), rng.permutation(K)) for q in range(N)])
    return d
def check_inputs(d):
    b = []
    for c in ("x", "c1", "c2"):
        a = np.abs(d[c].astype(np.float32))
        if not (np.isfinite(a) & ((a == 0) | ((a >= 2.0 ** -30) & (a <= 2.0 ** 30)))).all(): b.append(c)
    return b
def winners(v, book):
    s = np.concatenate([mx_ref.matmul(v, q) for q in book], axis=1)
    w = np.argmax(s + np.float32(0), axis=1)
    return w, s[np.arange(128), w]
def chosen(t, e):
    return t.reshape(128, -1, 4)[:, e].reshape(128, -1)
def reference(x, c1, c2):
    q1 = [mx_ref.quantize(c1[q]) for q in range(N)]
    q2 = [mx_ref.quantize(c2[q]) for q in range(N)]
    d1 = np.concatenate([decode(q) for q in q1], axis=1)
    d2 = np.concatenate([decode(q) for q in q2], axis=1)
    y = np.zeros((N, 128, 512), np.float32); no = np.zeros((N, 4, 128), np.float32)
    for r in range(N):
        w1, s1 = winners(mx_ref.quantize(x[r]), q1)
        R = (x[r].astype(np.float32) - chosen(d1, w1)).astype(BF)
        w2, s2 = winners(mx_ref.quantize(R), q2)
        y[r] = R.astype(np.float32) - chosen(d2, w2)
        no[r, 0] = w1; no[r, 1] = w2; no[r, 2] = s1; no[r, 3] = s2
    return {"y": y, "no": no}

@@ -1,0 +1,630 @@
+from concourse.bass import DstId, RemoteDMATransfer
+from concourse.mybir import dt, AluOpType, AxisListType, ActivationFunctionType
+
+N = 6
+K = 512
+A = AluOpType
+F = ActivationFunctionType
+CW = 384
+
+SCRATCH = {
+    "xt": ("sbuf", [128, 512], "bfloat16"),
+    "ones": ("sbuf", [128, 516], "bfloat16"),
+    "zt": ("sbuf", [128, 516], "bfloat16"),
+    "eq": ("sbuf", [128, 512], "float8_e4m3fn_x4"),
+    "ep": ("sbuf", [128, 512], "uint8"),
+    "neg": ("sbuf", [128, 512], "float32"),
+    "bm": ("sbuf", [128, 32], "float32"),
+    "mask": ("sbuf", [128, 32], "float32"),
+    "pi": ("sbuf", [128, 8], "int32"),
+    "p3": ("sbuf", [128, 8], "int32"),
+    "acol": ("sbuf", [128, 8], "float32"),
+    "aw": ("sbuf", [128, 8], "float32"),
+    "sl": ("sbuf", [128, 16], "float32"),
+    "wt": ("sbuf", [128, 8], "float32"),
+    "q512": ("sbuf", [128, 8], "float32"),
+    "lx": ("sbuf", [128, 16, 32], "float32"),
+    "lt": ("sbuf", [128, 16, 32], "float32"),
+    "ly": ("sbuf", [128, 16, 16], "float32"),
+    "lz": ("sbuf", [128, 16, 8], "float32"),
+    "ls": ("sbuf", [128, 16, 16], "float32"),
+    "off": ("sbuf", [128, 16, 32], "uint16"),
+    "sb": ("psum", [128, 2048], "float32"),
+    "up": ("psum", [128, 2048], "float32"),
+}
+for _h in range(2):
+    SCRATCH["rt%d" % _h] = ("sbuf", [128, 512], "bfloat16")
+    SCRATCH["yt%d" % _h] = ("sbuf", [128, 256], "float32")
+for _s in (1, 2):
+    SCRATCH["ct%d" % _s] = ("sbuf", [128, 4 * K], "bfloat16")
+    SCRATCH["cq%d" % _s] = ("sbuf", [128, K], "float8_e4m3fn_x4")
+    SCRATCH["cp%d" % _s] = ("sbuf", [128, K], "uint8")
+    SCRATCH["xq%d" % _s] = ("sbuf", [128, 896], "float8_e4m3fn_x4")
+    SCRATCH["xp%d" % _s] = ("sbuf", [128, 896], "uint8")
+    SCRATCH["dc%d" % _s] = ("sbuf", [128, 56], "float32")
+    for _h in range(2):
+        SCRATCH["wq%d_%d" % (_s, _h)] = ("sbuf", [128, 448], "float8_e4m3fn_x4")
+        SCRATCH["wp%d_%d" % (_s, _h)] = ("sbuf", [128, 448], "uint8")
+        SCRATCH["win%d_%d" % (_s, _h)] = ("sbuf", [128, 4 * CW], "bfloat16")
+        SCRATCH["sc%d_%d" % (_s, _h)] = ("sbuf", [128, 4 * N], "float32")
+        for _t in range(3):
+            _n = (_s, _h, _t)
+            SCRATCH["rm%d_%d_%d" % _n] = ("sbuf", [128, 516], "float32")
+            SCRATCH["jk%d_%d_%d" % _n] = ("sbuf", [128, 512], "bfloat16")
+            SCRATCH["gt%d_%d_%d" % _n] = ("sbuf", [128, 512], "bfloat16")
+            if _t < 2:
+                SCRATCH["oq%d_%d_%d" % _n] = ("sbuf", [128, 128], "float8_e4m3fn_x4")
+                SCRATCH["op%d_%d_%d" % _n] = ("sbuf", [128, 128], "uint8")
+
+SEMAPHORES = ["cv", "cs", "cp", "cg", "sent", "ld_x", "ld_c1", "ld_c2", "st_no"]
+for _s in (1, 2):
+    for _h in range(2):
+        SEMAPHORES += ["pair%d_%d" % (_s, _h), "wa%d_%d" % (_s, _h), "st_y%d_%d" % (_s - 1, _h)]
+for _r in range(N):
+    SEMAPHORES += ["xa1_%d" % _r, "xa2_0_%d" % _r, "xa2_1_%d" % _r]
+
+CSEM = {"V": "cv", "S": "cs", "P": "cp", "G": "cg"}
+
+
+def estimate(f, hop, rem, wake):
+    return {"v": 0.00083 * f, "s0": 0.024 * f, "s": 0.00083 * f, "sg": 0.00126 * f, "mm": 0.00076 * f, "g0": 0.13 * f,
+            "g": 0.0015 * f, "wake": wake, "rem": rem, "hop": 2.2 + hop, "hopx": 3.0 + hop, "hopr": 2.8 + hop, "dma": 2.0,
+            "dmai": 0.08, "bias": 0.25}
+
+
+SETS = [estimate(1.2, 0.0, 0.3, 0.08), estimate(1.0, -0.4, 0.25, 0.06), estimate(1.5, 0.3, 0.3, 0.08), estimate(1.2, 0.8, 0.6, 0.1)]
+STEPS = 15000
+LEAD = 2
+_memo = {}
+
+
+def chain(c):
+    turn = lambda p: sorted([r for r in range(N) if r % 2 == p and r != c], key=lambda r: (r - c) % N)
+    o, s = turn(1 - c % 2), turn(c % 2)
+    return [o[0], s[0], o[1], s[1], o[2]]
+
+
+def left(r, h):
+    return (r % 2 == 0) == (h == 0)
+
+
+def own(r, h):
+    return (64, 1) if left(r, h) else (768, 0)
+
+
+def place(r, h, q):
+    return (q - r - 1) % N if left(r, h) else (q - r) % N
+
+
+def lands(r, h):
+    return (0, 320) if left(r, h) else (128, 0)
+
+
+def build(topo, cores, E):
+    ops = []
+    now = [0]
+    got = {}
+    sent = {}
+    arr = []
+    R = range(N)
+
+    def op(c, q, dur, deps, emit, kind="c", sem=None, lat=0.0):
+        ops.append({"c": c, "q": q, "dur": dur, "deps": [d for d in deps if d is not None], "emit": emit, "kind": kind,
+                    "sem": sem, "lat": lat, "bias": E["bias"] * now[0]})
+        return len(ops) - 1
+
+    def V(c, n, deps, emit, fast=False):
+        return op(c, "V", max(64, n * (0.5 if fast else 1)) * E["v"], deps, emit)
+
+    def S(c, n, deps, emit):
+        return op(c, "S", E["s0"] + max(64, n) * E["s"], deps, emit)
+
+    def X(c, n, deps, ev, es, ind=False):
+        i = op(c, "V", 0.0, deps, None)
+        dv, ds = max(64, n) * E["v"], E["s0"] + max(64, n) * E["s"]
+        if ind:
+            dv, ds = 0.05 + n * E["sg"], 0.065 + n * E["sg"]
+        ops[i]["alt"] = {"V": (dv, ev), "S": (ds, es)}
+        return i
+
+    def G(c, n, deps, emit):
+        return op(c, "G", E["g0"] + n * E["g"], deps, emit)
+
+    def MM(c, n, deps, emit):
+        return op(c, "P", (n + 16) * E["mm"], deps, emit)
+
+    def D(c, q, deps, emit, sem, total=16, more=0.0):
+        return op(c, q, E["dmai"], deps, emit, "d", (sem, total), E["dma"] + more)
+
+    def QZ(c, n, deps, emit):
+        return op(c, "V", 0.015 + 4 * n * 0.00034 * E["v"] / 0.001, deps, emit)
+
+    def send(c, parts, deps):
+        share = 1
+        while share < len(parts):
+            share *= 2
+
+        def emit(g, T):
+            ts = []
+            for i, (dst, sem, src, land) in enumerate(parts):
+                eng = topo.engines(cores[c], cores[dst[0]])
+                w = len(eng) // share
+                m = 0
+                for e in eng[i * w:(i + 1) * w]:
+                    m |= 1 << e
+                ids = []
+                for d in dst:
+                    rid, pid, _ = topo.addr(cores[d])
+                    ids.append(DstId(rid=rid, pnc=pid))
+                ts.append(RemoteDMATransfer(dst_ids=ids, dma_engine_mask=m, remote_sem=T.sem[sem], srcs=[src(T)], dsts=[land(T, d) for d in dst], alu_op=0))
+            return g.remote_dma_fused(ts, local_sem=T.sem.sent)
+        for dst, sem, _, _ in parts:
+            w = len(topo.engines(cores[c], cores[dst[0]])) // share
+            for d in dst:
+                got[(d, sem)] = got.get((d, sem), 0) + w
+            sent[c] = sent.get(c, 0) + w
+        return op(c, "G", E["rem"] + 0.06 * (len(parts) - 1), deps, emit, "r")
+
+    def arrive(c, sem, deps, lat):
+        o = op(c, None, 0.0, deps, None, "a", (sem, None), lat)
+        arr.append(o)
+        return o
+
+    st = [{} for _ in R]
+    for c in R:
+        s = st[c]
+        s["ldx"] = D(c, "Y", [], lambda g, T: g.sync.dma_start(T.xt[:], T.x[:]), "ld_x")
+        s["ldc1"] = D(c, "Y", [], lambda g, T: g.sync.dma_start(T.ct1[:], T.c1[:]), "ld_c1", 16, 1.2)
+        s["qx1"] = [QZ(c, 128, [s["ldx"]], lambda g, T, a=a: g.vector.quantize_mx(T.xq1[:, a:a + 128], T.xp1[:, a:a + 128], T.xt[:])) for a in (0, 768)]
+        s["neg"] = V(c, 512, [], lambda g, T: g.vector.memset(T.neg[:], -1e29))
+        s["ones"] = V(c, 516, [], lambda g, T: g.vector.memset(T.ones[:], 1.0), True)
+        pi = G(c, 1, [], lambda g, T: g.iota(T.pi[:, 0:1], [[0, 1]], 0, 1))
+        bm = G(c, 32, [], lambda g, T: g.iota(T.bm[:], [[0, 2], [1, 4], [0, 4]], 0, 0, allow_small_or_imprecise_dtypes=True))
+        p3 = V(c, 1, [pi], lambda g, T: g.vector.tensor_scalar(T.p3[:, 0:1], T.pi[:, 0:1], 3, None, A.bitwise_and))
+        s["acol"] = V(c, 1, [p3], lambda g, T: g.vector.tensor_copy(T.acol[:, 0:1], T.p3[:, 0:1]))
+        s["mask"] = V(c, 32, [bm, s["acol"]], lambda g, T: g.vector.tensor_scalar(T.mask[:], T.bm[:], T.acol[:, 0:1], None, A.is_equal))
+        s["aw"] = V(c, 1, [s["acol"]], lambda g, T: g.vector.tensor_scalar(T.aw[:, 0:1], T.acol[:, 0:1], float(CW), None, A.mult))
+        s["qc1"] = QZ(c, 512, [s["ldc1"]], lambda g, T: g.vector.quantize_mx(T.cq1[:], T.cp1[:], T.ct1[:]))
+
+    def spread(c, stage, h, q):
+        dst = [(c + i) % N for i in range(1, N)]
+        if h is None:
+            sem, a, n, k = "xa1_%d" % c, 0, 128, 0
+        else:
+            sem, n = "xa2_%d_%d" % (h, c), 64
+            a, k = own(c, h)
+        to = lambda d: 128 + 128 * chain(d).index(c) + 64 * k
+        s1 = send(c, [(dst, sem, lambda T: T["xq%d" % stage][:, a:a + n].bitcast(dt.uint8), lambda T, d: T["xq%d" % stage][:, to(d):to(d) + n].bitcast(dt.uint8))], [q])
+        s2 = send(c, [(dst, sem, lambda T: T["xp%d" % stage][:, a:a + n], lambda T, d: T["xp%d" % stage][:, to(d):to(d) + n])], [q])
+        for d in dst:
+            o = arrive(d, sem, [s1, s2], E["hopx"] if h is None else E["hopr"])
+            for e in ((0, 1) if h is None else (h,)):
+                st[d]["x%d_%d_%d" % (stage, e, c)] = o
+
+    for c in R:
+        s = st[c]
+        spread(c, 1, None, s["qx1"][0])
+        for h in range(2):
+            s["x1_%d_%d" % (h, c)] = s["qx1"][0 if left(c, h) else 1]
+        s["zt"] = G(c, 516, [s["ones"]], lambda g, T: g.affine_select(T.zt[:], T.ones[:], [[-1, 516]], A.is_equal, 0.0, 4, 4))
+        late = [s["qx1"][0]]
+        s["wt"] = G(c, 6, late, lambda g, T: g.iota(T.wt[:, 0:N], [[-1, N]], 8, 0, allow_small_or_imprecise_dtypes=True))
+        for h in range(2):
+            m = min(c + 1, N - 1) if left(c, h) else max(c, 1)
+            s["sl%d" % h] = [G(c, z - a, late, lambda g, T, h=h, a=a, z=z, b=64 * place(c, h, a) - (0 if left(c, h) else 64): g.iota(
+                T.sl[:, 8 * h + a:8 * h + z], [[64, z - a]], b, 1, allow_small_or_imprecise_dtypes=True)) for a, z in ((0, m), (m, N))]
+        s["q512"] = G(c, 6, late, lambda g, T: g.iota(T.q512[:, 0:N], [[K, N]], 0, 0, allow_small_or_imprecise_dtypes=True))
+        s["eq"] = [QZ(c, 128, [s["zt"]], lambda g, T, b=b: g.vector.quantize_mx(T.eq[:, 128 * b:128 * b + 128], T.ep[:, 128 * b:128 * b + 128], T.zt[:, 4 - b:516 - b])) for b in range(4)]
+        s["z"] = [V(c, 256, [], lambda g, T, h=h, z=(0 if left(c, h) else 256): g.vector.memset(T["rt%d" % h][:, z:z + 256], 0.0), True) for h in range(2)]
+        s["ldc2"] = D(c, "Y", [s["qc1"]], lambda g, T: g.sync.dma_start(T.ct2[:], T.c2[:]), "ld_c2", 16, 1.5)
+        s["qc2"] = QZ(c, 512, [s["ldc2"]], lambda g, T: g.vector.quantize_mx(T.cq2[:], T.cp2[:], T.ct2[:]))
+
+    def spread_out(c, i, n, p, vals, deps):
+        sl = i if n == 1 else slice(i, i + n)
+        tr = []
+        for k in range(n):
+            m = X(c, 32, [deps[k], st[c]["mask"]], lambda g, T, k=k: g.vector.tensor_scalar(T.lx[p, i + k, :], T.mask[p, :], vals[k](T), None, A.mult),
+                  lambda g, T, k=k: g.scalar.activation(T.lx[p, i + k, :], T.mask[p, :], F.Copy, scale=vals[k](T)))
+            tr.append(V(c, 32, [m], lambda g, T, k=k: g.vector.transpose(T.lt[p, i + k, :], T.lx[p, i + k, :])))
+        y = V(c, 32 * n, tr, lambda g, T: g.vector.tensor_tensor(T.ly[p, sl, :], T.lt[p, sl, 0::2], T.lt[p, sl, 1::2], A.add))
+        return V(c, 16 * n, [y], lambda g, T: g.vector.tensor_tensor(T.lz[p, sl, :], T.ly[p, sl, 0::2], T.ly[p, sl, 1::2], A.add))
+
+    def word_list(c, i, n, vals, deps):
+        sl = slice(i, i + n)
+        z = spread_out(c, i, n, slice(0, 128), vals, deps)
+        half = []
+        for d in range(2):
+            for b in range(2):
+                for a in range(2):
+                    o, f = slice(64 * d + 32 * b, 64 * d + 32 * b + 32), slice(64 * d + 32 * a, 64 * d + 32 * a + 32)
+                    half.append(X(c, 8 * n, [z], lambda g, T, o=o, f=f, a=a: g.vector.tensor_copy(T.ls[o, sl, 8 * a:8 * a + 8], T.lz[f, sl, :]),
+                                  lambda g, T, o=o, f=f, a=a: g.scalar.activation(T.ls[o, sl, 8 * a:8 * a + 8], T.lz[f, sl, :], F.Copy)))
+        out = []
+        for h in range(2):
+            for d in range(2):
+                o, f = slice(64 * d, 64 * d + 64), slice(64 * h, 64 * h + 64)
+                out.append(V(c, 16 * n, half[4 * h:4 * h + 4] + [st[c]["acol"]], lambda g, T, o=o, f=f, h=h: g.vector.tensor_scalar(
+                    T.off[o, sl, 16 * h:16 * h + 16], T.ls[f, sl, :], 4.0, T.acol[f, 0:1], A.mult, A.add)))
+        return out
+
+    scans = [[] for _ in R]
+    slot = [0] * N
+    pairs = {(s, h): [[] for _ in R] for s in (1, 2) for h in range(2)}
+    cands = {(s, h): [[] for _ in R] for s in (1, 2) for h in range(2)}
+
+    def search(c, stage, h):
+        s = st[c]
+        ch = chain(c)
+        ot = lands(c, h)[1]
+        tiles = [(192, (ch[0], ch[1])), (448, (ch[2], ch[3])), (704, (ch[4], c))]
+        if left(c, h):
+            tiles = [(320, (ch[1], ch[2])), (576, (ch[3], ch[4])), (64, (c, ch[0]))]
+        seq = [2, 0, 1]
+        nm = lambda k: "%d_%d_%d" % (stage, h, k)
+        wq, wp, sc_ = "wq%d_%d" % (stage, h), "wp%d_%d" % (stage, h), "sc%d_%d" % (stage, h)
+        sg = {}
+        for k in seq:
+            col, who = tiles[k]
+            bank = len(scans[c]) % 4
+            prev = scans[c][-4] if len(scans[c]) >= 4 else None
+            m = MM(c, 512, [s["x%d_%d_%d" % (stage, h, r)] for r in who] + [s["qc%d" % stage], prev], lambda g, T, col=col, bank=bank: g.tensor.matmul_mx(
+                T.sb[:, 512 * bank:512 * bank + 512], T["xq%d" % stage][:, col:col + 128], T["xp%d" % stage][:, col:col + 128], T["cq%d" % stage][:], T["cp%d" % stage][:], True, True))
+            sc = V(c, 512, [m, s["neg"]], lambda g, T, k=k, bank=bank: g.vector.tensor_tensor_scan(
+                T["rm" + nm(k)][:, 0:512], T.sb[:, 512 * bank:512 * bank + 512], T.neg[:], -1e29, A.max, A.max))
+            scans[c].append(sc)
+            sg[k] = S(c, 512, [sc], lambda g, T, k=k: g.scalar.activation(
+                T["jk" + nm(k)][:], T["rm" + nm(k)][:, 0:512], F.Sign, bias=T["rm" + nm(k)][:, 511:512], scale=-1.0, accum_out=T["rm" + nm(k)][:, 512:513]))
+        o = send(c, [([r for r in tiles[k][1] if r != c], "pair%d_%d" % (stage, h), lambda T, k=k: T["rm" + nm(k)][:, 511:513],
+                      lambda T, d: T[sc_][:, 4 * c:4 * c + 2]) for k in range(3)], [sg[k] for k in range(3)])
+        for r in R:
+            if r != c:
+                pairs[(stage, h)][r].append(o)
+        pb = slice(0, 64) if left(c, h) else slice(64, 128)
+        s["own%d_%d" % (stage, h)] = V(c, 2, [sg[2]], lambda g, T: g.vector.tensor_copy(T[sc_][pb, 4 * c:4 * c + 2], T["rm" + nm(2)][pb, 511:513]))
+        i0 = slot[c]
+        slot[c] += 3
+        ls = word_list(c, i0, 3, [lambda T, k=k: T["rm" + nm(k)][:, 512:513] for k in seq], [sg[k] for k in seq])
+        qs = {}
+        for j, k in enumerate(seq):
+            i = i0 + j
+            ga = [X(c, 256, ls,
+                    lambda g, T, k=k, i=i, e=e: g.vector.tensor_copy(T["gt" + nm(k)][:, 256 * e:256 * e + 256], T["ct%d" % stage][:, 0:4 * K].indirect(T.off[:, i, 16 * e:16 * e + 16])),
+                    lambda g, T, k=k, i=i, e=e: g.scalar.activation(T["gt" + nm(k)][:, 256 * e:256 * e + 256], T["ct%d" % stage][:, 0:4 * K].indirect(T.off[:, i, 16 * e:16 * e + 16]), F.Copy), True) for e in range(2)]
+            if k == 2:
+                qs[k] = QZ(c, 128, ga, lambda g, T: g.vector.quantize_mx(T[wq][:, ot:ot + 128], T[wp][:, ot:ot + 128], T["gt" + nm(2)][:]))
+                s["w%d_%d" % (stage, h)] = qs[k]
+            else:
+                qs[k] = QZ(c, 128, ga, lambda g, T, k=k: g.vector.quantize_mx(T["oq" + nm(k)][:], T["op" + nm(k)][:], T["gt" + nm(k)][:]))
+        sem = "wa%d_%d" % (stage, h)
+        to = lambda d: lands(d, h)[0] + 64 * ((c - d - 1) % N)
+        for part in ([2], [0, 1]):
+            pc, pp = [], []
+            for k in part:
+                for e, r in enumerate(tiles[k][1]):
+                    if r != c:
+                        a, bq, bp = (ot + 64 * e, wq, wp) if k == 2 else (64 * e, "oq" + nm(k), "op" + nm(k))
+                        pc.append(([r], sem, lambda T, bq=bq, a=a: T[bq][:, a:a + 64].bitcast(dt.uint8), lambda T, d: T[wq][:, to(d):to(d) + 64].bitcast(dt.uint8)))
+                        pp.append(([r], sem, lambda T, bp=bp, a=a: T[bp][:, a:a + 64], lambda T, d: T[wp][:, to(d):to(d) + 64]))
+            s1 = send(c, pc, [qs[k] for k in part])
+            s2 = send(c, pp, [qs[k] for k in part])
+            for p in pc:
+                cands[(stage, h)][p[0][0]] += [s1, s2]
+
+    upd = [{} for _ in R]
+    joint = [{} for _ in R]
+
+    def finish(c, stage, h):
+        s = st[c]
+        dc, sc, win = "dc%d" % stage, "sc%d_%d" % (stage, h), "win%d_%d" % (stage, h)
+        pb = slice(0, 64) if left(c, h) else slice(64, 128)
+        p0 = 0 if left(c, h) else 64
+        p1 = 64 - p0
+        pa = arrive(c, "pair%d_%d" % (stage, h), pairs[(stage, h)][c], E["hop"])
+        wa = arrive(c, "wa%d_%d" % (stage, h), cands[(stage, h)][c], E["hop"])
+        col = lambda T, k: T[dc][pb, k:k + 1]
+        ow = s["own%d_%d" % (stage, h)]
+        m = V(c, 6, [pa, ow], lambda g, T: g.vector.tensor_reduce(col(T, 0), T[sc][pb, 0::4], AxisListType.X, A.max))
+        e = V(c, 6, [m], lambda g, T: g.vector.tensor_scalar(T[dc][pb, 8:8 + N], T[sc][pb, 0::4], col(T, 0), None, A.is_equal))
+        w = V(c, 6, [e, s["wt"]], lambda g, T: g.vector.tensor_tensor(T[dc][pb, 16:16 + N], T[dc][pb, 8:8 + N], T.wt[pb, 0:N], A.mult))
+        k8 = V(c, 6, [w], lambda g, T: g.vector.tensor_reduce(col(T, 1), T[dc][pb, 16:16 + N], AxisListType.X, A.max))
+        oh = V(c, 6, [k8], lambda g, T: g.vector.tensor_scalar(T[dc][pb, 24:24 + N], T[dc][pb, 16:16 + N], col(T, 1), None, A.is_equal))
+        pv = V(c, 6, [oh] + s["sl%d" % h], lambda g, T: g.vector.tensor_tensor(T[dc][pb, 40:40 + N], T[dc][pb, 24:24 + N], T.sl[pb, 8 * h:8 * h + N], A.mult))
+        v = V(c, 6, [pv], lambda g, T: g.vector.tensor_reduce(col(T, 2), T[dc][pb, 40:40 + N], AxisListType.X, A.add))
+        i = slot[c]
+        slot[c] += 1
+        z = spread_out(c, i, 1, pb, [lambda T: col(T, 2)], [v])
+        near = []
+        for b in range(2):
+            for a in range(2):
+                o, f = slice(p0 + 32 * b, p0 + 32 * b + 32), slice(p0 + 32 * a, p0 + 32 * a + 32)
+                near.append(V(c, 8, [z, s["aw"]], lambda g, T, o=o, f=f, a=a: g.vector.tensor_scalar(T.off[o, i, 8 * a:8 * a + 8], T.lz[f, i, :], 1.0, T.aw[f, 0:1], A.mult, A.add)))
+        ls = [V(c, 16, near, lambda g, T: g.vector.tensor_copy(T.off[p1:p1 + 64, i, 0:16], T.off[pb, i, 0:16]))]
+        gn = V(c, 6, [pa, ow, s["q512"]], lambda g, T: g.vector.tensor_tensor(T[dc][pb, 32:32 + N], T[sc][pb, 1::4], T.q512[pb, 0:N], A.add))
+        joint[c].setdefault(stage, []).extend([m, oh, gn])
+        of, ot = lands(c, h)
+        cps = []
+        for mine in (True, False):
+            for b in range(4):
+                a, n = (ot, 128) if mine else (of, 320)
+                f, k, o = (p0, 64, 64 * place(c, h, c)) if mine else (0, 320, 64 * place(c, h, (c + 1) % N))
+                u = MM(c, n, [s["w%d_%d" % (stage, h)] if mine else wa, s["eq"][b], upd[c].get(b)], lambda g, T, b=b, a=a, n=n: g.tensor.matmul_mx(
+                    T.up[:, 512 * b:512 * b + n], T.eq[:, 128 * b:128 * b + 128], T.ep[:, 128 * b:128 * b + 128],
+                    T["wq%d_%d" % (stage, h)][:, a:a + n], T["wp%d_%d" % (stage, h)][:, a:a + n], True, True))
+                to = lambda T, b=b, o=o, k=k: T[win][:, CW * b + o:CW * b + o + k]
+                fr = lambda T, b=b, f=f, k=k: T.up[:, 512 * b + f:512 * b + f + k]
+                cp = X(c, k, [u], lambda g, T, to=to, fr=fr: g.vector.tensor_scalar(to(T), fr(T), -1.0, None, A.mult),
+                       lambda g, T, to=to, fr=fr: g.scalar.activation(to(T), fr(T), F.Copy, scale=-1.0))
+                upd[c][b] = cp
+                cps.append(cp)
+        half = 1 if left(c, h) else 0
+        if stage == 1:
+            r = V(c, 450, cps + ls + s["z"] + [s["ldx"]], lambda g, T: g.vector.tensor_tensor(
+                T["rt%d" % h][:, 256 * half:256 * half + 256], T[win][:, 0:4 * CW].indirect(T.off[:, i, 0:16]), T.xt[:, 256 * half:256 * half + 256], A.add))
+            s["r%d" % h] = r
+            a = 0 if left(c, h) else 768
+            q2 = QZ(c, 128, [r], lambda g, T: g.vector.quantize_mx(T.xq2[:, a:a + 128], T.xp2[:, a:a + 128], T["rt%d" % h][:]))
+            s["x2_%d_%d" % (h, c)] = q2
+            spread(c, 2, h, q2)
+        else:
+            for k in range(2):
+                y = V(c, 225, cps + ls + [s["r%d" % h]], lambda g, T, k=k: g.vector.tensor_tensor(
+                    T["yt%d" % h][:, 128 * k:128 * k + 128], T[win][:, 0:4 * CW].indirect(T.off[:, i, 8 * k:8 * k + 8]), T["rt%d" % h][:, 256 * half + 128 * k:256 * half + 128 * k + 128], A.add))
+                a = 256 * half + 128 * k
+                if k == 0:
+                    D(c, "Y", [y], lambda g, T, a=a, k=k: g.sync.dma_start(T.y[:, a:a + 128], T["yt%d" % h][:, 128 * k:128 * k + 128]), "st_y%d_%d" % (k, h))
+                else:
+                    D(c, "S", [y], lambda g, T, a=a, k=k: g.scalar.dma_start(T.y[:, a:a + 128], T["yt%d" % h][:, 128 * k:128 * k + 128]), "st_y%d_%d" % (k, h))
+
+    def numbers(c, stage):
+        dc = "dc%d" % stage
+        d = joint[c][stage]
+        pr = V(c, 6, d, lambda g, T: g.vector.tensor_tensor(T[dc][:, 48:48 + N], T[dc][:, 24:24 + N], T[dc][:, 32:32 + N], A.mult))
+        nu = V(c, 6, [pr], lambda g, T: g.vector.tensor_reduce(T[dc][:, 3:4], T[dc][:, 48:48 + N], AxisListType.X, A.add))
+        for row, cc in ((stage - 1, 3), (stage + 1, 0)):
+            for h in range(2):
+                f, o = (0, 64) if left(c, h) else (64, 0)
+                D(c, "Y", [nu] if cc == 3 else d, lambda g, T, row=row, cc=cc, f=f, o=o: g.sync.dma_start(T.no[row:row + 1, o:o + 64], T[dc][f:f + 64, cc:cc + 1]), "st_no", 128)
+
+    for stage in (1, 2):
+        for h in range(2):
+            now[0] = h if stage == 1 else 1 + h
+            for c in R:
+                search(c, stage, h)
+            for c in R:
+                finish(c, stage, h)
+        for c in R:
+            numbers(c, stage)
+    for o in arr:
+        ops[o]["sem"] = (ops[o]["sem"][0], got[(ops[o]["c"], ops[o]["sem"][0])])
+    return ops, sent
+
+
+def alike(ops):
+    per = [[i for i, o in enumerate(ops) if o["c"] == c and o["kind"] != "a"] for c in range(N)]
+    calls = [[i for i in l if ops[i]["kind"] == "r"] for l in per]
+    back = {}
+    for l in calls:
+        for k, i in enumerate(l):
+            back[i] = calls[LEAD][k]
+    ids = per[LEAD] + [i for i, o in enumerate(ops) if o["c"] == LEAD and o["kind"] == "a"]
+    at = {i: k for k, i in enumerate(ids)}
+    return per, ids, [sorted(set(at[back.get(d, d)] for d in ops[i]["deps"])) for i in ids]
+
+
+def draw_up(topo, cores):
+    ops, sent = build(topo, cores, SETS[0])
+    per, ids, deps = alike(ops)
+    n = len(ids)
+    R = range(n)
+    sets = []
+    for E in SETS:
+        full = build(topo, cores, E)[0]
+        lead = [full[i] for i in ids]
+        sets.append(([{q: v[0] for q, v in o["alt"].items()} if "alt" in o else {o["q"]: o["dur"]} for o in lead], [o["lat"] for o in lead], E["wake"]))
+    lead = [ops[i] for i in ids]
+    alt = ["alt" in o for o in lead]
+    home = [o["q"] for o in lead]
+    succ = [[] for _ in R]
+    for i in R:
+        for d in deps[i]:
+            succ[d].append(i)
+    cnt = [len(d) for d in deps]
+    top = [i for i in R if cnt[i] == 0]
+    for i in top:
+        for j in succ[i]:
+            cnt[j] -= 1
+            if cnt[j] == 0:
+                top.append(j)
+    rank = [0.0] * n
+    for j in reversed(top):
+        rank[j] = min(sets[0][0][j].values()) + sets[0][1][j] + sets[0][2] + max([rank[k] for k in succ[j]] + [0.0])
+    rank = [rank[i] - lead[i]["bias"] for i in R]
+
+    def order(nudge, pin, favour):
+        dur, lat, wake = sets[0]
+        todo = [len(d) for d in deps]
+        at = [0.0] * n
+        ready = {q: [] for q in ("V", "S", "P", "G", "Y", None)}
+        free = {q: 0.0 for q in ready}
+        seq = {q: [] for q in ready}
+        qof = [None] * n
+        pr = [rank[i] + nudge[i] for i in R]
+
+        def add(i):
+            if not alt[i]:
+                ready[home[i]].append(i)
+                return
+            for q in ("V", "S"):
+                if pin[i] in (None, q):
+                    ready[q].append(i)
+        for i in R:
+            if todo[i] == 0:
+                add(i)
+        for _ in R:
+            bt, bq = 1e9, None
+            for q, l in ready.items():
+                if l:
+                    t = min([at[i] for i in l])
+                    if q and free[q] > t:
+                        t = free[q]
+                    if t < bt:
+                        bt, bq = t, q
+            i, bp = -1, -1e9
+            for j in ready[bq]:
+                if at[j] <= bt:
+                    p = pr[j] - (favour if bq == "V" and alt[j] else 0.0)
+                    if p > bp:
+                        i, bp = j, p
+            ready[bq].remove(i)
+            if alt[i]:
+                o = "S" if bq == "V" else "V"
+                if i in ready[o]:
+                    ready[o].remove(i)
+            qof[i] = bq
+            e = bt + dur[i][bq]
+            if bq:
+                free[bq] = e
+            seq[bq].append(i)
+            for k in succ[i]:
+                todo[k] -= 1
+                at[k] = max(at[k], e + lat[i] + (0.06 if bq == home[k] and not alt[k] else wake))
+                if todo[k] == 0:
+                    add(k)
+        return seq, qof
+
+    def span(seq, qof, which):
+        dur, lat, wake = sets[which]
+        todo = [len(d) for d in deps]
+        at = [0.0] * n
+        pos = {q: 0 for q in seq}
+        free = {q: 0.0 for q in seq}
+        end = 0.0
+        land = [i for i in R if qof[i] is None and todo[i] == 0]
+        moved = True
+        while moved:
+            moved = False
+            for q, l in seq.items():
+                while (land if q is None else pos[q] < len(l) and todo[l[pos[q]]] == 0):
+                    i = land.pop() if q is None else l[pos[q]]
+                    pos[q] += 1
+                    e = at[i] if q is None else max(at[i], free[q]) + dur[i][q]
+                    free[q] = e
+                    moved = True
+                    d = e + lat[i]
+                    if d > end:
+                        end = d
+                    for k in succ[i]:
+                        todo[k] -= 1
+                        a = d + (0.06 if q and qof[k] == q else wake)
+                        if a > at[k]:
+                            at[k] = a
+                        if todo[k] == 0 and qof[k] is None:
+                            land.append(k)
+        return end
+
+    seed = [12345]
+
+    def draw(m):
+        seed[0] = (seed[0] * 1103515245 + 12345) % (1 << 31)
+        return (seed[0] >> 8) % m
+
+    work = [i for i in R if home[i] in ("V", "S")]
+    both = [i for i in work if alt[i]]
+    cur = ([0.0] * n, [None] * n, 1.0)
+    kept = order(*cur)
+    base = [span(kept[0], kept[1], k) for k in range(len(SETS))]
+    now = best = 1.0
+    for step in range(STEPS):
+        nudge, pin, favour = list(cur[0]), list(cur[1]), cur[2]
+        k = draw(100)
+        if k < 60:
+            for _ in range(1 + draw(3)):
+                nudge[work[draw(len(work))]] = (draw(61) - 30) / 10.0 if draw(10) < 7 else 0.0
+        elif k < 75:
+            a, d = draw(len(work)), (draw(51) - 25) / 10.0
+            for i in work[a:a + 3 + draw(38)]:
+                nudge[i] += d
+        elif k < 97:
+            for _ in range(1 + draw(3)):
+                pin[both[draw(len(both))]] = (None, "V", "S")[draw(3)]
+        else:
+            favour = (0.0, 0.5, 1.0, 1.5, 2.0, 3.0)[draw(6)]
+        so = order(nudge, pin, favour)
+        v = sum(span(so[0], so[1], k) / base[k] for k in range(len(SETS))) / len(SETS)
+        if v <= now + 0.003 * max(0.0, 1.0 - step / (0.9 * STEPS)) * draw(1000) / 1000.0:
+            cur, now = (nudge, pin, favour), v
+            if v < best:
+                best, kept = v, so
+    seq = {}
+    for c in range(N):
+        for q, l in kept[0].items():
+            if q:
+                seq[(c, q)] = [per[c][k] for k in l]
+        for k in both:
+            o = ops[per[c][k]]
+            o["q"] = kept[1][k]
+            o["emit"] = o["alt"][o["q"]][1]
+    return ops, sent, seq, [span(kept[0], kept[1], k) for k in range(len(SETS))]
+
+
+def plan(topo, cores):
+    if "plan" not in _memo:
+        _memo["plan"] = draw_up(topo, cores)
+    return _memo["plan"]
+
+
+def rank_program(g, core, T, topo):
+    rank = T.rank_of(core)
+    if rank is None:
+        return
+    ops, sent, seq, _ = plan(topo, list(T.cores))
+    queues = {"V": g.vector, "S": g.scalar, "P": g.tensor, "G": g, "Y": g.sync}
+    num = {}
+    tot = {"sent": sent[rank]}
+    for q in CSEM:
+        k = 0
+        for i in seq.get((rank, q), []):
+            if ops[i]["kind"] == "c":
+                k += 1
+                num[i] = (CSEM[q], k)
+        tot[CSEM[q]] = k
+    known = {q: {} for q in queues}
+    snap = {}
+    pos = {q: 0 for q in queues}
+    mine = sum(len(seq.get((rank, q), [])) for q in queues)
+    while mine:
+        moved = False
+        for q in queues:
+            lst = seq.get((rank, q), [])
+            while pos[q] < len(lst) and all(ops[d]["kind"] in "ra" or d in snap for d in ops[lst[pos[q]]]["deps"]):
+                i = lst[pos[q]]
+                o = ops[i]
+                need = {}
+                for d in o["deps"]:
+                    name, cnt = num[d] if ops[d]["kind"] == "c" else ops[d]["sem"]
+                    if need.get(name, (0, None))[0] < cnt:
+                        need[name] = (cnt, snap.get(d))
+                for name in sorted(need, key=lambda t: -len(need[t][1] or {})):
+                    cnt, sn = need[name]
+                    if known[q].get(name, 0) < cnt:
+                        queues[q].wait_ge(T.sem[name], cnt)
+                        known[q][name] = cnt
+                        for k2, v2 in (sn or {}).items():
+                            known[q][k2] = max(known[q].get(k2, 0), v2)
+                ins = o["emit"](g, T)
+                if o["kind"] == "c":
+                    ins.then_inc(T.sem[num[i][0]], 1)
+                elif o["kind"] == "d":
+                    ins.then_inc(T.sem[o["sem"][0]], 16)
+                snap[i] = dict(known[q])
+                pos[q] += 1
+                mine -= 1
+                moved = True
+        if not moved:
+            raise ValueError("the plan does not close")
+    for o in ops:
+        if o["c"] == rank and o["kind"] in "da":
+            tot[o["sem"][0]] = o["sem"][1]
+    for name in SEMAPHORES:
+        if tot.get(name, 0) > known["G"].get(name, 0):
+            g.wait_ge(T.sem[name], tot[name])

@@ -5,7 +5,19 @@ N = 6
 K = 512
 A = AluOpType
 F = ActivationFunctionType
-CW = 384
+BW = 256
+
+LISTS = {1: [[0, 1, 2], [4, 5, 3]], 2: [["O", (0, 0), (0, 1)], ["F", (1, 0), (1, 1)]]}
+SENDS = {1: [[(0, 0), (0, 1)], ["F"], [(1, 0), (1, 1)]], 2: [[(0, 0), (0, 1)], ["F"], [(1, 0), (1, 1)]]}
+PIECES = {0: 2, 1: 2}
+TILES = ["O", "F", (0, 0), (0, 1), (1, 0), (1, 1)]
+SPREAD = [[1, 2], [4, 5, 3]]
+FULL = False
+if FULL:
+    BW = 768
+    LISTS = {1: [[0, 1, 2], [3, 4, 5]], 2: [[0, 1, 2], [3, 4, 5]]}
+    SENDS = {1: [[1, 2], [3, 4, 5]], 2: [[1, 2], [3, 4, 5]]}
+    TILES = list(range(N))
 
 SCRATCH = {
     "xt": ("sbuf", [128, 512], "bfloat16"),
@@ -16,105 +28,103 @@ SCRATCH = {
     "neg": ("sbuf", [128, 512], "float32"),
     "bm": ("sbuf", [128, 32], "float32"),
     "mask": ("sbuf", [128, 32], "float32"),
+    "rs": ("sbuf", [128, 192], "float32"),
     "pi": ("sbuf", [128, 8], "int32"),
-    "p3": ("sbuf", [128, 8], "int32"),
-    "acol": ("sbuf", [128, 8], "float32"),
-    "aw": ("sbuf", [128, 8], "float32"),
-    "sl": ("sbuf", [128, 16], "float32"),
-    "wt": ("sbuf", [128, 8], "float32"),
+    "pf": ("sbuf", [128, 8], "float32"),
+    "step": ("sbuf", [128, 8], "float32"),
     "q512": ("sbuf", [128, 8], "float32"),
-    "lx": ("sbuf", [128, 16, 32], "float32"),
-    "lt": ("sbuf", [128, 16, 32], "float32"),
-    "ly": ("sbuf", [128, 16, 16], "float32"),
-    "lz": ("sbuf", [128, 16, 8], "float32"),
-    "ls": ("sbuf", [128, 16, 16], "float32"),
-    "off": ("sbuf", [128, 16, 32], "uint16"),
-    "sb": ("psum", [128, 2048], "float32"),
-    "up": ("psum", [128, 2048], "float32"),
+    "rt": ("sbuf", [128, 1024], "bfloat16"),
+    "yt": ("sbuf", [128, 512], "float32"),
+    "ps": ("psum", [128, 4096], "float32"),
 }
-for _h in range(2):
-    SCRATCH["rt%d" % _h] = ("sbuf", [128, 512], "bfloat16")
-    SCRATCH["yt%d" % _h] = ("sbuf", [128, 256], "float32")
+SEMAPHORES = ["cv", "cs", "cp", "cg", "sent", "ld_x", "ld_c1_0", "ld_c1_1", "ld_c2_0", "st"]
 for _s in (1, 2):
     SCRATCH["ct%d" % _s] = ("sbuf", [128, 4 * K], "bfloat16")
     SCRATCH["cq%d" % _s] = ("sbuf", [128, K], "float8_e4m3fn_x4")
     SCRATCH["cp%d" % _s] = ("sbuf", [128, K], "uint8")
     SCRATCH["xq%d" % _s] = ("sbuf", [128, 896], "float8_e4m3fn_x4")
     SCRATCH["xp%d" % _s] = ("sbuf", [128, 896], "uint8")
-    SCRATCH["dc%d" % _s] = ("sbuf", [128, 56], "float32")
-    for _h in range(2):
-        SCRATCH["wq%d_%d" % (_s, _h)] = ("sbuf", [128, 448], "float8_e4m3fn_x4")
-        SCRATCH["wp%d_%d" % (_s, _h)] = ("sbuf", [128, 448], "uint8")
-        SCRATCH["win%d_%d" % (_s, _h)] = ("sbuf", [128, 4 * CW], "bfloat16")
-        SCRATCH["sc%d_%d" % (_s, _h)] = ("sbuf", [128, 4 * N], "float32")
-        for _t in range(3):
-            _n = (_s, _h, _t)
-            SCRATCH["rm%d_%d_%d" % _n] = ("sbuf", [128, 516], "float32")
-            SCRATCH["jk%d_%d_%d" % _n] = ("sbuf", [128, 512], "bfloat16")
-            SCRATCH["gt%d_%d_%d" % _n] = ("sbuf", [128, 512], "bfloat16")
-            if _t < 2:
-                SCRATCH["oq%d_%d_%d" % _n] = ("sbuf", [128, 128], "float8_e4m3fn_x4")
-                SCRATCH["op%d_%d_%d" % _n] = ("sbuf", [128, 128], "uint8")
-
-SEMAPHORES = ["cv", "cs", "cp", "cg", "sent", "ld_x", "ld_c1", "ld_c2", "st_no"]
-for _s in (1, 2):
-    for _h in range(2):
-        SEMAPHORES += ["pair%d_%d" % (_s, _h), "wa%d_%d" % (_s, _h), "st_y%d_%d" % (_s - 1, _h)]
+    SCRATCH["dc%d" % _s] = ("sbuf", [128, 64], "float32")
+    SCRATCH["wq%d" % _s] = ("sbuf", [128, 768], "float8_e4m3fn_x4")
+    SCRATCH["wp%d" % _s] = ("sbuf", [128, 768], "uint8")
+    SCRATCH["oq%d" % _s] = ("sbuf", [128, 640], "float8_e4m3fn_x4")
+    SCRATCH["op%d" % _s] = ("sbuf", [128, 640], "uint8")
+    SCRATCH["win%d" % _s] = ("sbuf", [128, 3072], "bfloat16")
+    SCRATCH["sc%d" % _s] = ("sbuf", [128, 4 * N], "float32")
+    SCRATCH["gt%d" % _s] = ("sbuf", [128, N * 512], "bfloat16")
+    SCRATCH["jk%d" % _s] = ("sbuf", [128, N * 512], "bfloat16")
+    SCRATCH["rm%d" % _s] = ("sbuf", [128, N * 516], "float32")
+    SCRATCH["of%d" % _s] = ("sbuf", [128, 2, 16], "uint16")
+    for _i in list(range(len(LISTS[_s]))) + [N]:
+        for _b in ("lx", "lt", "ls"):
+            SCRATCH["%s%d_%d" % (_b, _s, _i)] = ("sbuf", [128, 192], "float32")
+        if _i < N:
+            SCRATCH["off%d_%d" % (_s, _i)] = ("sbuf", [128, 192], "uint16")
+    SEMAPHORES += ["pair%d" % _s] + ["wa%d_%d" % (_s, _i) for _i in range(len(SENDS[_s]))]
 for _r in range(N):
     SEMAPHORES += ["xa1_%d" % _r, "xa2_0_%d" % _r, "xa2_1_%d" % _r]
 
 CSEM = {"V": "cv", "S": "cs", "P": "cp", "G": "cg"}
 
 
-def estimate(f, hop, rem, wake):
+def estimate(f, wake, rem, row, rate, fix):
     return {"v": 0.00083 * f, "s0": 0.024 * f, "s": 0.00083 * f, "sg": 0.00126 * f, "mm": 0.00076 * f, "g0": 0.13 * f,
-            "g": 0.0015 * f, "wake": wake, "rem": rem, "hop": 2.2 + hop, "hopx": 3.0 + hop, "hopr": 2.8 + hop, "dma": 2.0,
-            "dmai": 0.08, "bias": 0.25}
+            "g": 0.0015 * f, "q": 0.00025 * f, "wake": wake, "rem": rem, "row": row, "byte": 1.0 / rate, "fix": fix, "dmai": 0.08}
 
 
-SETS = [estimate(1.2, 0.0, 0.3, 0.08), estimate(1.0, -0.4, 0.25, 0.06), estimate(1.5, 0.3, 0.3, 0.08), estimate(1.2, 0.8, 0.6, 0.1)]
-STEPS = 15000
+SETS = [estimate(1.2, 0.08, 0.3, 0.005, 16e3, 1.6), estimate(1.0, 0.06, 0.25, 0.003, 25e3, 1.6), estimate(1.5, 0.08, 0.3, 0.005, 16e3, 1.8),
+        estimate(1.2, 0.1, 0.6, 0.01, 12e3, 1.8)]
+DRAFTS, STEPS, LOOK, SEED = 6000, 25000, 0.15, 1
 LEAD = 2
 _memo = {}
 
 
-def chain(c):
-    turn = lambda p: sorted([r for r in range(N) if r % 2 == p and r != c], key=lambda r: (r - c) % N)
-    o, s = turn(1 - c % 2), turn(c % 2)
-    return [o[0], s[0], o[1], s[1], o[2]]
+def side(r, h):
+    return (r + h) % 2
 
 
-def left(r, h):
-    return (r % 2 == 0) == (h == 0)
+def slot(r, c):
+    k = (r - c) % N
+    return k - 1 if k < N // 2 else k - 2
 
 
-def own(r, h):
-    return (64, 1) if left(r, h) else (768, 0)
+def halves(t):
+    if FULL:
+        return [(t, h) for h in range(2)]
+    if t in ("O", "F"):
+        return [(0 if t == "O" else N // 2, h) for h in range(2)]
+    return [(3 * t[1] + 1, t[0]), (3 * t[1] + 2, t[0])]
 
 
 def place(r, h, q):
-    return (q - r - 1) % N if left(r, h) else (q - r) % N
+    e = side(r, h)
+    if FULL:
+        return 128 * ((r - q) % N) + 64 * e
+    if (q - r) % (N // 2) == 0:
+        return (4 * BW if h == 0 else 0) + (0 if q == r else 128) + 64 * e
+    return (0 if h == 0 else 4 * BW) + 64 * slot(r, q)
 
 
-def lands(r, h):
-    return (0, 320) if left(r, h) else (128, 0)
+def shares(n, width):
+    w = [width]
+    while len(w) < n:
+        w = sorted(w[1:] + [w[0] // 2] * 2, reverse=True)
+    return w
 
 
 def build(topo, cores, E):
     ops = []
-    now = [0]
     got = {}
-    sent = {}
     arr = []
     R = range(N)
 
     def op(c, q, dur, deps, emit, kind="c", sem=None, lat=0.0):
         ops.append({"c": c, "q": q, "dur": dur, "deps": [d for d in deps if d is not None], "emit": emit, "kind": kind,
-                    "sem": sem, "lat": lat, "bias": E["bias"] * now[0]})
+                    "sem": sem, "lat": lat, "by": None})
         return len(ops) - 1
 
-    def V(c, n, deps, emit, fast=False):
-        return op(c, "V", max(64, n * (0.5 if fast else 1)) * E["v"], deps, emit)
+    def V(c, n, deps, emit):
+        return op(c, "V", max(64, n) * E["v"], deps, emit)
 
     def S(c, n, deps, emit):
         return op(c, "S", E["s0"] + max(64, n) * E["s"], deps, emit)
@@ -127,292 +137,303 @@ def build(topo, cores, E):
         ops[i]["alt"] = {"V": (dv, ev), "S": (ds, es)}
         return i
 
+    def copy(c, n, deps, to, fr, by=None, ind=False):
+        if by is None:
+            return X(c, n, deps, lambda g, T: g.vector.tensor_copy(to(T), fr(T)), lambda g, T: g.scalar.activation(to(T), fr(T), F.Copy), ind)
+        return X(c, n, deps, lambda g, T: g.vector.tensor_scalar(to(T), fr(T), by(T), None, A.mult), lambda g, T: g.scalar.activation(to(T), fr(T), F.Copy, scale=by(T)))
+
     def G(c, n, deps, emit):
         return op(c, "G", E["g0"] + n * E["g"], deps, emit)
 
     def MM(c, n, deps, emit):
         return op(c, "P", (n + 16) * E["mm"], deps, emit)
 
-    def D(c, q, deps, emit, sem, total=16, more=0.0):
-        return op(c, q, E["dmai"], deps, emit, "d", (sem, total), E["dma"] + more)
-
-    def QZ(c, n, deps, emit):
-        return op(c, "V", 0.015 + 4 * n * 0.00034 * E["v"] / 0.001, deps, emit)
-
-    def send(c, parts, deps):
-        share = 1
-        while share < len(parts):
-            share *= 2
-
-        def emit(g, T):
-            ts = []
-            for i, (dst, sem, src, land) in enumerate(parts):
-                eng = topo.engines(cores[c], cores[dst[0]])
-                w = len(eng) // share
-                m = 0
-                for e in eng[i * w:(i + 1) * w]:
-                    m |= 1 << e
-                ids = []
-                for d in dst:
-                    rid, pid, _ = topo.addr(cores[d])
-                    ids.append(DstId(rid=rid, pnc=pid))
-                ts.append(RemoteDMATransfer(dst_ids=ids, dma_engine_mask=m, remote_sem=T.sem[sem], srcs=[src(T)], dsts=[land(T, d) for d in dst], alu_op=0))
-            return g.remote_dma_fused(ts, local_sem=T.sem.sent)
-        for dst, sem, _, _ in parts:
-            w = len(topo.engines(cores[c], cores[dst[0]])) // share
-            for d in dst:
-                got[(d, sem)] = got.get((d, sem), 0) + w
-            sent[c] = sent.get(c, 0) + w
-        return op(c, "G", E["rem"] + 0.06 * (len(parts) - 1), deps, emit, "r")
-
-    def arrive(c, sem, deps, lat):
-        o = op(c, None, 0.0, deps, None, "a", (sem, None), lat)
+    def arrive(c, sem, deps, by=None):
+        o = op(c, None, 0.0, deps, None, "a", sem)
+        ops[o]["by"] = by
         arr.append(o)
         return o
 
+    def D(c, q, width, deps, emit, sem):
+        d = op(c, q, E["dmai"], deps, emit, "d", sem)
+        w = op(c, "D", 8 * (E["row"] + width * E["byte"]), [d], None, "w", None, E["fix"])
+        got[(c, sem)] = got.get((c, sem), 0) + 16
+        return arrive(c, sem, [w], d)
+
+    def QZ(c, n, deps, emit):
+        return op(c, "V", 0.015 + 4 * n * E["q"], deps, emit)
+
+    def send(c, width, parts, deps, more=0.0):
+        eng = topo.engines(cores[c], cores[parts[0][2][0][0]])
+        w = shares(len(parts), len(eng))
+
+        def emit(g, T):
+            ts = []
+            for i, (sem, src, to) in enumerate(parts):
+                m = 0
+                for e in eng[sum(w[:i]):sum(w[:i + 1])]:
+                    m |= 1 << e
+                ids = []
+                for d, _ in to:
+                    rid, pid, _ = topo.addr(cores[d])
+                    ids.append(DstId(rid=rid, pnc=pid))
+                ts.append(RemoteDMATransfer(dst_ids=ids, dma_engine_mask=m, remote_sem=T.sem[sem], srcs=[src(T)], dsts=[land(T) for _, land in to], alu_op=0))
+            return g.remote_dma_fused(ts, local_sem=T.sem.sent)
+        for i, (sem, _, to) in enumerate(parts):
+            for d, _ in to:
+                got[(d, sem)] = got.get((d, sem), 0) + w[i]
+            got[(c, "sent")] = got.get((c, "sent"), 0) + w[i]
+        r = op(c, "G", E["rem"] + 0.06 * (len(parts) - 1) + more, deps, emit, "r")
+        t = max(128 * len(p[2]) / w[i] * (E["row"] + width * E["byte"]) for i, p in enumerate(parts))
+        return op(c, "D", t, [r], None, "w", None, E["fix"])
+
+    def send_mx(c, n, parts, deps, more=0.0, which=(1, 4)):
+        words = lambda b, a: lambda T: T[b[0]][:, a:a + n].bitcast(dt.uint8)
+        plane = lambda b, a: lambda T: T[b[1]][:, a:a + n]
+        return [send(c, k * n, [(sem, f(b, a), [(d, f(b2, a2)) for d, b2, a2 in to]) for sem, b, a, to in parts], deps, more)
+                for k, f in ((1, plane), (4, words)) if k in which]
+
+    XQ = lambda s: ("xq%d" % s, "xp%d" % s)
+    WQ = lambda s: ("wq%d" % s, "wp%d" % s)
+    OQ = lambda s: ("oq%d" % s, "op%d" % s)
+    quant = lambda b, a, n, fr: lambda g, T: g.vector.quantize_mx(T[b[0]][:, a:a + n], T[b[1]][:, a:a + n], fr(T))
+    acol = lambda T, p: T.pf[p, 0:1]
     st = [{} for _ in R]
     for c in R:
         s = st[c]
-        s["ldx"] = D(c, "Y", [], lambda g, T: g.sync.dma_start(T.xt[:], T.x[:]), "ld_x")
-        s["ldc1"] = D(c, "Y", [], lambda g, T: g.sync.dma_start(T.ct1[:], T.c1[:]), "ld_c1", 16, 1.2)
-        s["qx1"] = [QZ(c, 128, [s["ldx"]], lambda g, T, a=a: g.vector.quantize_mx(T.xq1[:, a:a + 128], T.xp1[:, a:a + 128], T.xt[:])) for a in (0, 768)]
+        s["ldx"] = D(c, "Y", 1024, [], lambda g, T: g.sync.dma_start(T.xt[:], T.x[:]), "ld_x")
+        s["ld1"] = [D(c, "Y", 2048, [], lambda g, T, a=a: g.sync.dma_start(T.ct1[:, 1024 * a:1024 * a + 1024], T.c1[:, 1024 * a:1024 * a + 1024]), "ld_c1_%d" % a) for a in range(2)]
+        s["x1_0"] = QZ(c, 128, [s["ldx"]], quant(XQ(1), 0, 128, lambda T: T.xt[:]))
+        s["qc1"] = [QZ(c, 256, [s["ld1"][a]], quant(("cq1", "cp1"), 256 * a, 256, lambda T, a=a: T.ct1[:, 1024 * a:1024 * a + 1024])) for a in range(2)]
         s["neg"] = V(c, 512, [], lambda g, T: g.vector.memset(T.neg[:], -1e29))
-        s["ones"] = V(c, 516, [], lambda g, T: g.vector.memset(T.ones[:], 1.0), True)
+        s["ones"] = V(c, 258, [], lambda g, T: g.vector.memset(T.ones[:], 1.0))
         pi = G(c, 1, [], lambda g, T: g.iota(T.pi[:, 0:1], [[0, 1]], 0, 1))
         bm = G(c, 32, [], lambda g, T: g.iota(T.bm[:], [[0, 2], [1, 4], [0, 4]], 0, 0, allow_small_or_imprecise_dtypes=True))
-        p3 = V(c, 1, [pi], lambda g, T: g.vector.tensor_scalar(T.p3[:, 0:1], T.pi[:, 0:1], 3, None, A.bitwise_and))
-        s["acol"] = V(c, 1, [p3], lambda g, T: g.vector.tensor_copy(T.acol[:, 0:1], T.p3[:, 0:1]))
-        s["mask"] = V(c, 32, [bm, s["acol"]], lambda g, T: g.vector.tensor_scalar(T.mask[:], T.bm[:], T.acol[:, 0:1], None, A.is_equal))
-        s["aw"] = V(c, 1, [s["acol"]], lambda g, T: g.vector.tensor_scalar(T.aw[:, 0:1], T.acol[:, 0:1], float(CW), None, A.mult))
-        s["qc1"] = QZ(c, 512, [s["ldc1"]], lambda g, T: g.vector.quantize_mx(T.cq1[:], T.cp1[:], T.ct1[:]))
+        bits = [V(c, 1, [pi], lambda g, T, k=k, m=m: g.vector.tensor_scalar(T.pi[:, k:k + 1], T.pi[:, 0:1], m, None, A.bitwise_and)) for k, m in ((1, 3), (2, 28), (3, 32))]
+        s["acol"] = V(c, 1, [bits[0]], lambda g, T: g.vector.tensor_copy(T.pf[:, 0:1], T.pi[:, 1:2]))
+        s["mask"] = V(c, 32, [bm, s["acol"]], lambda g, T: g.vector.tensor_scalar(T.mask[:], T.bm[:], T.pf[:, 0:1], None, A.is_equal))
+        u = V(c, 1, [bits[1], s["acol"]], lambda g, T: g.vector.tensor_scalar(T.pf[:, 2:3], T.pi[:, 2:3], 2.0, T.pf[:, 0:1], A.mult, A.add))
+        s["step"] = [V(c, 1, [bits[2], u], lambda g, T: g.vector.tensor_scalar(T.step[:, 0:1], T.pi[:, 3:4], 0.125, T.pf[:, 2:3], A.mult, A.add))]
+        s["aw"] = [V(c, 1, [s["acol"]], lambda g, T, e=e, b=place(c, (c + e) % 2, 0): g.vector.tensor_scalar(
+            T.pf[64 * e:64 * e + 64, 1:2], T.pf[64 * e:64 * e + 64, 0:1], float(BW), float(b), A.mult, A.add)) for e in range(2)]
+        r1 = V(c, 192, [], lambda g, T: g.vector.memset(T.rs[:], 1.0))
+        s["rs"] = V(c, 48, [r1], lambda g, T: g.vector.memset(T.rs[:, 0::4], 0.0))
+        s["one"] = [V(c, 1, [], lambda g, T, k=k: g.vector.memset(T["dc%d" % k][:, 8:9], 1.0)) for k in (1, 2)]
+        s["z"] = [V(c, 128, [], lambda g, T, z=z: g.vector.memset(T.rt[:, z:z + 256], 0.0)) for z in (0, 768) if not FULL]
 
-    def spread(c, stage, h, q):
-        dst = [(c + i) % N for i in range(1, N)]
-        if h is None:
-            sem, a, n, k = "xa1_%d" % c, 0, 128, 0
-        else:
-            sem, n = "xa2_%d_%d" % (h, c), 64
-            a, k = own(c, h)
-        to = lambda d: 128 + 128 * chain(d).index(c) + 64 * k
-        s1 = send(c, [(dst, sem, lambda T: T["xq%d" % stage][:, a:a + n].bitcast(dt.uint8), lambda T, d: T["xq%d" % stage][:, to(d):to(d) + n].bitcast(dt.uint8))], [q])
-        s2 = send(c, [(dst, sem, lambda T: T["xp%d" % stage][:, a:a + n], lambda T, d: T["xp%d" % stage][:, to(d):to(d) + n])], [q])
-        for d in dst:
-            o = arrive(d, sem, [s1, s2], E["hopx"] if h is None else E["hopr"])
-            for e in ((0, 1) if h is None else (h,)):
-                st[d]["x%d_%d_%d" % (stage, e, c)] = o
+    def spread(c, stage, more):
+        sem = ("xa1_%d" if stage == 1 else "xa2_0_%d") % c
+        part = lambda l: [(sem, XQ(stage), 0, [((c - k) % N, XQ(stage), 128 * k) for k in l])]
+        w = send_mx(c, 128, part([k for l in SPREAD for k in l]), [st[c]["x%d_0" % stage]], more, (1,))
+        for l in SPREAD:
+            u = send_mx(c, 128, part(l), [st[c]["x%d_0" % stage]], 0.0, (4,))
+            for k in l:
+                st[(c - k) % N]["x%d_%d" % (stage, k)] = arrive((c - k) % N, sem, w + u)
 
     for c in R:
         s = st[c]
-        spread(c, 1, None, s["qx1"][0])
-        for h in range(2):
-            s["x1_%d_%d" % (h, c)] = s["qx1"][0 if left(c, h) else 1]
+        spread(c, 1, 0.0)
         s["zt"] = G(c, 516, [s["ones"]], lambda g, T: g.affine_select(T.zt[:], T.ones[:], [[-1, 516]], A.is_equal, 0.0, 4, 4))
-        late = [s["qx1"][0]]
-        s["wt"] = G(c, 6, late, lambda g, T: g.iota(T.wt[:, 0:N], [[-1, N]], 8, 0, allow_small_or_imprecise_dtypes=True))
-        for h in range(2):
-            m = min(c + 1, N - 1) if left(c, h) else max(c, 1)
-            s["sl%d" % h] = [G(c, z - a, late, lambda g, T, h=h, a=a, z=z, b=64 * place(c, h, a) - (0 if left(c, h) else 64): g.iota(
-                T.sl[:, 8 * h + a:8 * h + z], [[64, z - a]], b, 1, allow_small_or_imprecise_dtypes=True)) for a, z in ((0, m), (m, N))]
+        late = []
+        for e in range(2):
+            for q in range(1, N):
+                h = (c + e) % 2
+                s["step"].append(V(c, 1, [], lambda g, T, e=e, q=q, b=place(c, h, q) - place(c, h, q - 1): g.vector.memset(
+                    T.step[64 * e:64 * e + 64, q:q + 1], float(b))))
         s["q512"] = G(c, 6, late, lambda g, T: g.iota(T.q512[:, 0:N], [[K, N]], 0, 0, allow_small_or_imprecise_dtypes=True))
-        s["eq"] = [QZ(c, 128, [s["zt"]], lambda g, T, b=b: g.vector.quantize_mx(T.eq[:, 128 * b:128 * b + 128], T.ep[:, 128 * b:128 * b + 128], T.zt[:, 4 - b:516 - b])) for b in range(4)]
-        s["z"] = [V(c, 256, [], lambda g, T, h=h, z=(0 if left(c, h) else 256): g.vector.memset(T["rt%d" % h][:, z:z + 256], 0.0), True) for h in range(2)]
-        s["ldc2"] = D(c, "Y", [s["qc1"]], lambda g, T: g.sync.dma_start(T.ct2[:], T.c2[:]), "ld_c2", 16, 1.5)
-        s["qc2"] = QZ(c, 512, [s["ldc2"]], lambda g, T: g.vector.quantize_mx(T.cq2[:], T.cp2[:], T.ct2[:]))
+        s["eq"] = [QZ(c, 128, [s["zt"]], quant(("eq", "ep"), 128 * b, 128, lambda T, b=b: T.zt[:, 4 - b:516 - b])) for b in range(4)]
 
-    def spread_out(c, i, n, p, vals, deps):
-        sl = i if n == 1 else slice(i, i + n)
-        tr = []
-        for k in range(n):
-            m = X(c, 32, [deps[k], st[c]["mask"]], lambda g, T, k=k: g.vector.tensor_scalar(T.lx[p, i + k, :], T.mask[p, :], vals[k](T), None, A.mult),
-                  lambda g, T, k=k: g.scalar.activation(T.lx[p, i + k, :], T.mask[p, :], F.Copy, scale=vals[k](T)))
-            tr.append(V(c, 32, [m], lambda g, T, k=k: g.vector.transpose(T.lt[p, i + k, :], T.lx[p, i + k, :])))
-        y = V(c, 32 * n, tr, lambda g, T: g.vector.tensor_tensor(T.ly[p, sl, :], T.lt[p, sl, 0::2], T.lt[p, sl, 1::2], A.add))
-        return V(c, 16 * n, [y], lambda g, T: g.vector.tensor_tensor(T.lz[p, sl, :], T.ly[p, sl, 0::2], T.ly[p, sl, 1::2], A.add))
+    def listed(c, tag, vals, deps, out, fold, deps2, low):
+        n = 32 * len(vals)
+        lx, lt, ls = ["%s%s" % (b, tag) for b in ("lx", "lt", "ls")]
+        m = [copy(c, 32, [deps[k], st[c]["mask"]], lambda T, k=k: T[lx][:, 32 * k:32 * k + 32], lambda T: T.mask[:], vals[k]) for k in range(len(vals))]
+        t = V(c, n, m, lambda g, T: g.vector.transpose(T[lt][:, 0:n], T[lx][:, 0:n]))
+        z = V(c, n, [t, st[c]["rs"]], lambda g, T: g.vector.tensor_tensor_scan(T[ls][:, 0:n], T.rs[:, 0:n], T[lt][:, 0:n], 0.0, A.mult, A.add))
+        cv = [V(c, n // 4, [z] + deps2, lambda g, T, e=e: fold(g, T, out(T, e), T[ls][64 * e:64 * e + 64, 3:n:4], slice(64 * e, 64 * e + 64))) for e in range(2)]
+        q0 = V(c, n // 4, cv, lambda g, T: g.vector.tensor_copy(low(T, slice(0, 32), 1), low(T, slice(32, 64), 0)))
+        return [q0] + [V(c, n // 2, [q0], lambda g, T, a=a: g.vector.tensor_copy(low(T, slice(a, a + 32), None), low(T, slice(0, 32), None))) for a in (32, 64, 96)]
 
-    def word_list(c, i, n, vals, deps):
-        sl = slice(i, i + n)
-        z = spread_out(c, i, n, slice(0, 128), vals, deps)
-        half = []
-        for d in range(2):
-            for b in range(2):
-                for a in range(2):
-                    o, f = slice(64 * d + 32 * b, 64 * d + 32 * b + 32), slice(64 * d + 32 * a, 64 * d + 32 * a + 32)
-                    half.append(X(c, 8 * n, [z], lambda g, T, o=o, f=f, a=a: g.vector.tensor_copy(T.ls[o, sl, 8 * a:8 * a + 8], T.lz[f, sl, :]),
-                                  lambda g, T, o=o, f=f, a=a: g.scalar.activation(T.ls[o, sl, 8 * a:8 * a + 8], T.lz[f, sl, :], F.Copy)))
-        out = []
-        for h in range(2):
-            for d in range(2):
-                o, f = slice(64 * d, 64 * d + 64), slice(64 * h, 64 * h + 64)
-                out.append(V(c, 16 * n, half[4 * h:4 * h + 4] + [st[c]["acol"]], lambda g, T, o=o, f=f, h=h: g.vector.tensor_scalar(
-                    T.off[o, sl, 16 * h:16 * h + 16], T.ls[f, sl, :], 4.0, T.acol[f, 0:1], A.mult, A.add)))
-        return out
+    banks = [[None] * 8 for _ in R]
+    turn = [0] * N
+    pairs = {s: [[] for _ in R] for s in (1, 2)}
+    cands = {s: [[[] for _ in SENDS[s]] for _ in R] for s in (1, 2)}
 
-    scans = [[] for _ in R]
-    slot = [0] * N
-    pairs = {(s, h): [[] for _ in R] for s in (1, 2) for h in range(2)}
-    cands = {(s, h): [[] for _ in R] for s in (1, 2) for h in range(2)}
-
-    def search(c, stage, h):
+    def search(c, stage):
         s = st[c]
-        ch = chain(c)
-        ot = lands(c, h)[1]
-        tiles = [(192, (ch[0], ch[1])), (448, (ch[2], ch[3])), (704, (ch[4], c))]
-        if left(c, h):
-            tiles = [(320, (ch[1], ch[2])), (576, (ch[3], ch[4])), (64, (c, ch[0]))]
-        seq = [2, 0, 1]
-        nm = lambda k: "%d_%d_%d" % (stage, h, k)
-        wq, wp, sc_ = "wq%d_%d" % (stage, h), "wp%d_%d" % (stage, h), "sc%d_%d" % (stage, h)
+        rm, gt, ct = "rm%d" % stage, "gt%d" % stage, "ct%d" % stage
+        flat = [k for l in LISTS[stage] for k in l]
+        at = {k: 516 * i for i, k in enumerate(flat)}
         sg = {}
-        for k in seq:
-            col, who = tiles[k]
-            bank = len(scans[c]) % 4
-            prev = scans[c][-4] if len(scans[c]) >= 4 else None
-            m = MM(c, 512, [s["x%d_%d_%d" % (stage, h, r)] for r in who] + [s["qc%d" % stage], prev], lambda g, T, col=col, bank=bank: g.tensor.matmul_mx(
-                T.sb[:, 512 * bank:512 * bank + 512], T["xq%d" % stage][:, col:col + 128], T["xp%d" % stage][:, col:col + 128], T["cq%d" % stage][:], T["cp%d" % stage][:], True, True))
-            sc = V(c, 512, [m, s["neg"]], lambda g, T, k=k, bank=bank: g.vector.tensor_tensor_scan(
-                T["rm" + nm(k)][:, 0:512], T.sb[:, 512 * bank:512 * bank + 512], T.neg[:], -1e29, A.max, A.max))
-            scans[c].append(sc)
-            sg[k] = S(c, 512, [sc], lambda g, T, k=k: g.scalar.activation(
-                T["jk" + nm(k)][:], T["rm" + nm(k)][:, 0:512], F.Sign, bias=T["rm" + nm(k)][:, 511:512], scale=-1.0, accum_out=T["rm" + nm(k)][:, 512:513]))
-        o = send(c, [([r for r in tiles[k][1] if r != c], "pair%d_%d" % (stage, h), lambda T, k=k: T["rm" + nm(k)][:, 511:513],
-                      lambda T, d: T[sc_][:, 4 * c:4 * c + 2]) for k in range(3)], [sg[k] for k in range(3)])
+        for i, k in enumerate(flat):
+            if stage == 1 or FULL:
+                col, need = 128 * k, [s["x%d_%d" % (stage, k)]]
+            else:
+                col = 64 if k == "O" else 128 + 128 * TILES.index(k)
+                need = [s["x2_%d_%d" % (h, d)] for d, h in halves(k)]
+            bank = turn[c] % 4
+            turn[c] += 1
+            ps = lambda T, bank=bank: T.ps[:, 512 * bank:512 * bank + 512]
+            m = MM(c, 512, need + s["qc%d" % stage] + [banks[c][bank]], lambda g, T, col=col, ps=ps: g.tensor.matmul_mx(
+                ps(T), T["xq%d" % stage][:, col:col + 128], T["xp%d" % stage][:, col:col + 128], T["cq%d" % stage][:], T["cp%d" % stage][:], True, True))
+            a = at[k]
+            sc = V(c, 512, [m, s["neg"]], lambda g, T, a=a, ps=ps: g.vector.tensor_tensor_scan(T[rm][:, a:a + 512], ps(T), T.neg[:], -1e29, A.max, A.max))
+            banks[c][bank] = sc
+            s["scan%d_%d" % (stage, i)] = sc
+            sg[k] = S(c, 512, [sc], lambda g, T, a=a, i=i: g.scalar.activation(
+                T["jk%d" % stage][:, 512 * i:512 * i + 512], T[rm][:, a:a + 512], F.Sign, bias=T[rm][:, a + 511:a + 512], scale=-1.0, accum_out=T[rm][:, a + 512:a + 513]))
+        pair = lambda k, p=slice(0, 128): lambda T: T[rm][p, at[k] + 511:at[k] + 513]
+        land = lambda e, p=slice(0, 128): lambda T: T["sc%d" % stage][p, 4 * c + 2 * e:4 * c + 2 * e + 2]
+        if stage == 1 or FULL:
+            pp = [("pair%d" % stage, pair(k), [((c + k) % N, land(0))]) for k in flat if k]
+            s["own%d" % stage] = [copy(c, 2, [sg[0]], land(0), pair(0))]
+        else:
+            pp = [("pair2", pair(k), [((c + d) % N, land(side(c + d, h))) for d, h in halves(k)]) for k in flat if k != "O"]
+            s["own2"] = [copy(c, 2, [sg["O"]], land(e, slice(64 * e, 64 * e + 64)), pair("O", slice(64 * e, 64 * e + 64))) for e in range(2)]
+        o = send(c, 8, pp, [sg[k] for k in flat if k not in (0, "O")])
         for r in R:
             if r != c:
-                pairs[(stage, h)][r].append(o)
-        pb = slice(0, 64) if left(c, h) else slice(64, 128)
-        s["own%d_%d" % (stage, h)] = V(c, 2, [sg[2]], lambda g, T: g.vector.tensor_copy(T[sc_][pb, 4 * c:4 * c + 2], T["rm" + nm(2)][pb, 511:513]))
-        i0 = slot[c]
-        slot[c] += 3
-        ls = word_list(c, i0, 3, [lambda T, k=k: T["rm" + nm(k)][:, 512:513] for k in seq], [sg[k] for k in seq])
+                pairs[stage][r].append(o)
+        where = {}
+        for i, l in enumerate(LISTS[stage]):
+            off, n = "off%d_%d" % (stage, i), 16 * len(l)
+            ls = listed(c, "%d_%d" % (stage, i), [lambda T, k=k: T[rm][:, at[k] + 512:at[k] + 513] for k in l], [sg[k] for k in l],
+                        lambda T, e, off=off, n=n: T[off][0:64, n * e:n * e + n:2],
+                        lambda g, T, o, f, p: g.vector.tensor_scalar(o, f, 4.0, acol(T, p), A.mult, A.add), [s["acol"]],
+                        lambda T, p, e, off=off, n=n: T[off][p, 0:2 * n] if e is None else T[off][p, e:2 * n:2])
+            for j, k in enumerate(l):
+                where[k] = (off, n, j, ls)
         qs = {}
-        for j, k in enumerate(seq):
-            i = i0 + j
-            ga = [X(c, 256, ls,
-                    lambda g, T, k=k, i=i, e=e: g.vector.tensor_copy(T["gt" + nm(k)][:, 256 * e:256 * e + 256], T["ct%d" % stage][:, 0:4 * K].indirect(T.off[:, i, 16 * e:16 * e + 16])),
-                    lambda g, T, k=k, i=i, e=e: g.scalar.activation(T["gt" + nm(k)][:, 256 * e:256 * e + 256], T["ct%d" % stage][:, 0:4 * K].indirect(T.off[:, i, 16 * e:16 * e + 16]), F.Copy), True) for e in range(2)]
-            if k == 2:
-                qs[k] = QZ(c, 128, ga, lambda g, T: g.vector.quantize_mx(T[wq][:, ot:ot + 128], T[wp][:, ot:ot + 128], T["gt" + nm(2)][:]))
-                s["w%d_%d" % (stage, h)] = qs[k]
+        for i, t in enumerate(TILES):
+            ga = []
+            for d, h in halves(t):
+                e = side(c + d, h)
+                off, n, j, ls = where[d if stage == 1 or FULL else t]
+                o = n * e + 16 * j
+                ga.append(copy(c, 256, ls + s["ld%d" % stage], lambda T, a=512 * i + 256 * e: T[gt][:, a:a + 256],
+                               lambda T, off=off, o=o: T[ct][:, 0:4 * K].indirect(T[off][:, o:o + 16]), None, True))
+            qs[t] = QZ(c, 128, ga, quant(*((WQ(stage), 0) if i == 0 else (OQ(stage), 128 * i - 128)), 128, lambda T, i=i: T[gt][:, 512 * i:512 * i + 512]))
+        s["w%d" % stage] = qs[TILES[0]]
+        for i, l in enumerate(SENDS[stage]):
+            sem = "wa%d_%d" % (stage, i)
+            if FULL:
+                w = send_mx(c, 128, [(sem, OQ(stage), 128 * t - 128, [((c + t) % N, WQ(stage), 128 * t)]) for t in l], [qs[t] for t in l])
+            elif l == ["F"]:
+                w = send_mx(c, 128, [(sem, OQ(stage), 0, [((c + N // 2) % N, WQ(stage), 128)])], [qs["F"]])
             else:
-                qs[k] = QZ(c, 128, ga, lambda g, T, k=k: g.vector.quantize_mx(T["oq" + nm(k)][:], T["op" + nm(k)][:], T["gt" + nm(k)][:]))
-        sem = "wa%d_%d" % (stage, h)
-        to = lambda d: lands(d, h)[0] + 64 * ((c - d - 1) % N)
-        for part in ([2], [0, 1]):
-            pc, pp = [], []
-            for k in part:
-                for e, r in enumerate(tiles[k][1]):
-                    if r != c:
-                        a, bq, bp = (ot + 64 * e, wq, wp) if k == 2 else (64 * e, "oq" + nm(k), "op" + nm(k))
-                        pc.append(([r], sem, lambda T, bq=bq, a=a: T[bq][:, a:a + 64].bitcast(dt.uint8), lambda T, d: T[wq][:, to(d):to(d) + 64].bitcast(dt.uint8)))
-                        pp.append(([r], sem, lambda T, bp=bp, a=a: T[bp][:, a:a + 64], lambda T, d: T[wp][:, to(d):to(d) + 64]))
-            s1 = send(c, pc, [qs[k] for k in part])
-            s2 = send(c, pp, [qs[k] for k in part])
-            for p in pc:
-                cands[(stage, h)][p[0][0]] += [s1, s2]
+                pc = []
+                for t in l:
+                    for d, h in halves(t):
+                        r, e = (c + d) % N, side(c + d, h)
+                        to = 128 + 64 * e if t == "F" else 256 + 256 * h + 64 * slot(r, c)
+                        pc.append((sem, OQ(stage), 128 * TILES.index(t) - 128 + 64 * e, [(r, WQ(stage), to)]))
+                w = send_mx(c, 64, pc, [qs[t] for t in l])
+            for r in sorted(set((c + d) % N for t in l for d, _ in halves(t))):
+                cands[stage][r][i] += w
 
-    upd = [{} for _ in R]
-    joint = [{} for _ in R]
-
-    def finish(c, stage, h):
+    def finish(c, stage):
         s = st[c]
-        dc, sc, win = "dc%d" % stage, "sc%d_%d" % (stage, h), "win%d_%d" % (stage, h)
-        pb = slice(0, 64) if left(c, h) else slice(64, 128)
-        p0 = 0 if left(c, h) else 64
-        p1 = 64 - p0
-        pa = arrive(c, "pair%d_%d" % (stage, h), pairs[(stage, h)][c], E["hop"])
-        wa = arrive(c, "wa%d_%d" % (stage, h), cands[(stage, h)][c], E["hop"])
-        col = lambda T, k: T[dc][pb, k:k + 1]
-        ow = s["own%d_%d" % (stage, h)]
-        m = V(c, 6, [pa, ow], lambda g, T: g.vector.tensor_reduce(col(T, 0), T[sc][pb, 0::4], AxisListType.X, A.max))
-        e = V(c, 6, [m], lambda g, T: g.vector.tensor_scalar(T[dc][pb, 8:8 + N], T[sc][pb, 0::4], col(T, 0), None, A.is_equal))
-        w = V(c, 6, [e, s["wt"]], lambda g, T: g.vector.tensor_tensor(T[dc][pb, 16:16 + N], T[dc][pb, 8:8 + N], T.wt[pb, 0:N], A.mult))
-        k8 = V(c, 6, [w], lambda g, T: g.vector.tensor_reduce(col(T, 1), T[dc][pb, 16:16 + N], AxisListType.X, A.max))
-        oh = V(c, 6, [k8], lambda g, T: g.vector.tensor_scalar(T[dc][pb, 24:24 + N], T[dc][pb, 16:16 + N], col(T, 1), None, A.is_equal))
-        pv = V(c, 6, [oh] + s["sl%d" % h], lambda g, T: g.vector.tensor_tensor(T[dc][pb, 40:40 + N], T[dc][pb, 24:24 + N], T.sl[pb, 8 * h:8 * h + N], A.mult))
-        v = V(c, 6, [pv], lambda g, T: g.vector.tensor_reduce(col(T, 2), T[dc][pb, 40:40 + N], AxisListType.X, A.add))
-        i = slot[c]
-        slot[c] += 1
-        z = spread_out(c, i, 1, pb, [lambda T: col(T, 2)], [v])
-        near = []
-        for b in range(2):
-            for a in range(2):
-                o, f = slice(p0 + 32 * b, p0 + 32 * b + 32), slice(p0 + 32 * a, p0 + 32 * a + 32)
-                near.append(V(c, 8, [z, s["aw"]], lambda g, T, o=o, f=f, a=a: g.vector.tensor_scalar(T.off[o, i, 8 * a:8 * a + 8], T.lz[f, i, :], 1.0, T.aw[f, 0:1], A.mult, A.add)))
-        ls = [V(c, 16, near, lambda g, T: g.vector.tensor_copy(T.off[p1:p1 + 64, i, 0:16], T.off[pb, i, 0:16]))]
-        gn = V(c, 6, [pa, ow, s["q512"]], lambda g, T: g.vector.tensor_tensor(T[dc][pb, 32:32 + N], T[sc][pb, 1::4], T.q512[pb, 0:N], A.add))
-        joint[c].setdefault(stage, []).extend([m, oh, gn])
-        of, ot = lands(c, h)
-        cps = []
-        for mine in (True, False):
-            for b in range(4):
-                a, n = (ot, 128) if mine else (of, 320)
-                f, k, o = (p0, 64, 64 * place(c, h, c)) if mine else (0, 320, 64 * place(c, h, (c + 1) % N))
-                u = MM(c, n, [s["w%d_%d" % (stage, h)] if mine else wa, s["eq"][b], upd[c].get(b)], lambda g, T, b=b, a=a, n=n: g.tensor.matmul_mx(
-                    T.up[:, 512 * b:512 * b + n], T.eq[:, 128 * b:128 * b + 128], T.ep[:, 128 * b:128 * b + 128],
-                    T["wq%d_%d" % (stage, h)][:, a:a + n], T["wp%d_%d" % (stage, h)][:, a:a + n], True, True))
-                to = lambda T, b=b, o=o, k=k: T[win][:, CW * b + o:CW * b + o + k]
-                fr = lambda T, b=b, f=f, k=k: T.up[:, 512 * b + f:512 * b + f + k]
-                cp = X(c, k, [u], lambda g, T, to=to, fr=fr: g.vector.tensor_scalar(to(T), fr(T), -1.0, None, A.mult),
-                       lambda g, T, to=to, fr=fr: g.scalar.activation(to(T), fr(T), F.Copy, scale=-1.0))
-                upd[c][b] = cp
-                cps.append(cp)
-        half = 1 if left(c, h) else 0
-        if stage == 1:
-            r = V(c, 450, cps + ls + s["z"] + [s["ldx"]], lambda g, T: g.vector.tensor_tensor(
-                T["rt%d" % h][:, 256 * half:256 * half + 256], T[win][:, 0:4 * CW].indirect(T.off[:, i, 0:16]), T.xt[:, 256 * half:256 * half + 256], A.add))
-            s["r%d" % h] = r
-            a = 0 if left(c, h) else 768
-            q2 = QZ(c, 128, [r], lambda g, T: g.vector.quantize_mx(T.xq2[:, a:a + 128], T.xp2[:, a:a + 128], T["rt%d" % h][:]))
-            s["x2_%d_%d" % (h, c)] = q2
-            spread(c, 2, h, q2)
-        else:
-            for k in range(2):
-                y = V(c, 225, cps + ls + [s["r%d" % h]], lambda g, T, k=k: g.vector.tensor_tensor(
-                    T["yt%d" % h][:, 128 * k:128 * k + 128], T[win][:, 0:4 * CW].indirect(T.off[:, i, 8 * k:8 * k + 8]), T["rt%d" % h][:, 256 * half + 128 * k:256 * half + 128 * k + 128], A.add))
-                a = 256 * half + 128 * k
-                if k == 0:
-                    D(c, "Y", [y], lambda g, T, a=a, k=k: g.sync.dma_start(T.y[:, a:a + 128], T["yt%d" % h][:, 128 * k:128 * k + 128]), "st_y%d_%d" % (k, h))
-                else:
-                    D(c, "S", [y], lambda g, T, a=a, k=k: g.scalar.dma_start(T.y[:, a:a + 128], T["yt%d" % h][:, 128 * k:128 * k + 128]), "st_y%d_%d" % (k, h))
-
-    def numbers(c, stage):
-        dc = "dc%d" % stage
-        d = joint[c][stage]
-        pr = V(c, 6, d, lambda g, T: g.vector.tensor_tensor(T[dc][:, 48:48 + N], T[dc][:, 24:24 + N], T[dc][:, 32:32 + N], A.mult))
-        nu = V(c, 6, [pr], lambda g, T: g.vector.tensor_reduce(T[dc][:, 3:4], T[dc][:, 48:48 + N], AxisListType.X, A.add))
-        for row, cc in ((stage - 1, 3), (stage + 1, 0)):
+        dc, sc, win, of = "dc%d" % stage, "sc%d" % stage, "win%d" % stage, "of%d" % stage
+        pa = [arrive(c, "pair%d" % stage, pairs[stage][c])] + s["own%d" % stage]
+        sides = [(slice(0, 128), 0)] if stage == 1 or FULL else [(slice(0, 64), 0), (slice(64, 128), 2)]
+        rm = [V(c, 6, pa + [s["neg"]], lambda g, T, p=p, a=a: g.vector.tensor_tensor_scan(T[dc][p, 0:N], T[sc][p, a::4], T.neg[p, 0:N], -1e29, A.max, A.max)) for p, a in sides]
+        lt = V(c, 6, rm, lambda g, T: g.vector.tensor_scalar(T[dc][:, 9:9 + N], T[dc][:, 0:N], T[dc][:, N - 1:N], None, A.is_lt))
+        pv = V(c, 6, [lt] + s["one"] + s["step"], lambda g, T: g.vector.tensor_tensor(T[dc][:, 16:16 + N], T[dc][:, 8:8 + N], T.step[:, 0:N], A.mult))
+        v = V(c, 6, [pv], lambda g, T: g.vector.tensor_reduce(T[dc][:, 7:8], T[dc][:, 16:16 + N], AxisListType.X, A.add))
+        ls = listed(c, "%d_%d" % (stage, N), [lambda T: T[dc][:, 7:8]], [v], lambda T, e: T[of][0:64, e, 0:8],
+                    lambda g, T, o, f, p: g.vector.tensor_scalar(o, f, T.pf[p, 1:2], None, A.add), s["aw"],
+                    lambda T, p, e: T[of][p, :, :] if e is None else T[of][p, :, 8 * e:8 * e + 8])
+        gn = [V(c, 6, pa + [s["q512"]], lambda g, T, p=p, a=a: g.vector.tensor_tensor(T[dc][p, 24:24 + N], T[sc][p, a + 1::4], T.q512[p, 0:N], A.add)) for p, a in sides]
+        oh = V(c, 6, [lt] + s["one"], lambda g, T: g.vector.tensor_tensor(T[dc][:, 32:32 + N], T[dc][:, 8:8 + N], T[dc][:, 9:9 + N], A.subtract))
+        pr = V(c, 6, gn + [oh], lambda g, T: g.vector.tensor_tensor(T[dc][:, 40:40 + N], T[dc][:, 24:24 + N], T[dc][:, 32:32 + N], A.mult))
+        nu = V(c, 6, [pr], lambda g, T: g.vector.tensor_reduce(T[dc][:, 48:49], T[dc][:, 40:40 + N], AxisListType.X, A.add))
+        for row, cc, dep in ((stage - 1, 48, [nu]), (stage + 1, N - 1, rm)):
+            D(c, "Y", 4, dep, lambda g, T, row=row, cc=cc: g.sync.dma_start(T.no[row:row + 1, :], T[dc][:, cc:cc + 1]), "st")
+        runs = [(s["w%d" % stage], 0, 128, 0 if FULL else 4 * BW, (0, 1))]
+        for i, l in enumerate(SENDS[stage]):
+            wa = arrive(c, "wa%d_%d" % (stage, i), cands[stage][c][i])
+            if FULL:
+                for k in (l[:4], l[4:]):
+                    if k:
+                        runs.append((wa, 128 * k[0], 128 * len(k), 128 * k[0], (0, 1)))
+                continue
+            if "F" in l:
+                runs.append((wa, 128, 128, 4 * BW + 128, (0, 1)))
             for h in range(2):
-                f, o = (0, 64) if left(c, h) else (64, 0)
-                D(c, "Y", [nu] if cc == 3 else d, lambda g, T, row=row, cc=cc, f=f, o=o: g.sync.dma_start(T.no[row:row + 1, o:o + 64], T[dc][f:f + 64, cc:cc + 1]), "st_no", 128)
+                k = [t[1] for t in l if t != "F" and t[0] == h]
+                if k:
+                    runs.append((wa, 256 + 256 * h + 128 * min(k), 128 * len(k), 8 * BW * h + 128 * min(k), (h,)))
+        cps = [[], []]
+        for i, (dep, a, n, o, hs) in enumerate(runs):
+            for b in range(4):
+                bank = b + 4 * ((i + stage) % 2 if i else 1)
+                u = MM(c, n, [dep, s["eq"][b], banks[c][bank]], lambda g, T, b=b, a=a, n=n, bank=bank: g.tensor.matmul_mx(
+                    T.ps[:, 512 * bank:512 * bank + n], T.eq[:, 128 * b:128 * b + 128], T.ep[:, 128 * b:128 * b + 128],
+                    T["wq%d" % stage][:, a:a + n], T["wp%d" % stage][:, a:a + n], True, True))
+                cp = copy(c, n, [u], lambda T, b=b, o=o, n=n: T[win][:, BW * b + o:BW * b + o + n], lambda T, bank=bank, n=n: T.ps[:, 512 * bank:512 * bank + n], lambda T: -1.0)
+                banks[c][bank] = cp
+                for h in hs:
+                    cps[h].append(cp)
+        for h in range(2):
+            e = side(c, h)
+            w0, w1 = (0, 4 * BW) if FULL else (4 * BW * h, 4 * BW * h + 8 * BW)
+            pick = lambda T, a, n, e=e, w0=w0, w1=w1: T[win][:, w0:w1].indirect(T[of][:, e, a // 16:(a + n) // 16])
+            if stage == 1:
+                r = op(c, "V", 0.05 + 256 * E["sg"], cps[h] + ls + [s["ldx"]], lambda g, T, e=e, pick=pick: g.vector.tensor_tensor(
+                    T.rt[:, 256 + 256 * e:512 + 256 * e], pick(T, 0, 256), T.xt[:, 256 * e:256 * e + 256], A.add))
+                s["r%d" % h] = r
+                if FULL:
+                    if h == 1:
+                        s["x2_0"] = QZ(c, 128, [s["r0"], r], quant(XQ(2), 0, 128, lambda T: T.rt[:, 256:768]))
+                        spread(c, 2, 0.0)
+                    continue
+                q2 = QZ(c, 128, [r] + s["z"], quant(XQ(2), 128 * e, 128, lambda T, e=e: T.rt[:, 512 * e:512 * e + 512]))
+                s["x2_%d_0" % h] = q2
+                to = []
+                for i in ([5, 4, 2, 1, 3] if h == 0 else [3, 5, 4, 2, 1]):
+                    d = (c + i) % N
+                    t = "F" if i == N // 2 else (h, slot(c, d) // 2)
+                    to.append((d, XQ(2), 128 + 128 * TILES.index(t) + 64 * e))
+                w = send_mx(c, 64, [("xa2_%d_%d" % (h, c), XQ(2), 64 + 64 * e, to)], [q2])
+                for i in range(1, N):
+                    st[(c + i) % N]["x2_%d_%d" % (h, N - i)] = arrive((c + i) % N, "xa2_%d_%d" % (h, c), w)
+            else:
+                n = 256 // PIECES[h]
+                for k in range(PIECES[h]):
+                    a = 256 * e + n * k
+                    y = op(c, "V", 0.05 + n * E["sg"], cps[h] + ls + [s["r%d" % h]], lambda g, T, a=a, k=k, n=n, pick=pick: g.vector.tensor_tensor(
+                        T.yt[:, a:a + n], pick(T, n * k, n), T.rt[:, 256 + a:256 + a + n], A.add))
+                    if k % 2 == 0:
+                        D(c, "Y", 4 * n, [y], lambda g, T, a=a, n=n: g.sync.dma_start(T.y[:, a:a + n], T.yt[:, a:a + n]), "st")
+                    else:
+                        D(c, "S", 4 * n, [y], lambda g, T, a=a, n=n: g.scalar.dma_start(T.y[:, a:a + n], T.yt[:, a:a + n]), "st")
 
     for stage in (1, 2):
-        for h in range(2):
-            now[0] = h if stage == 1 else 1 + h
-            for c in R:
-                search(c, stage, h)
-            for c in R:
-                finish(c, stage, h)
         for c in R:
-            numbers(c, stage)
+            search(c, stage)
+            if stage == 1:
+                s = st[c]
+                s["ld2"] = [D(c, "Y", 4096, [s["scan1_1"]], lambda g, T: g.sync.dma_start(T.ct2[:], T.c2[:]), "ld_c2_0")]
+                s["qc2"] = [QZ(c, 512, s["ld2"], quant(("cq2", "cp2"), 0, 512, lambda T: T.ct2[:]))]
+        for c in R:
+            finish(c, stage)
     for o in arr:
-        ops[o]["sem"] = (ops[o]["sem"][0], got[(ops[o]["c"], ops[o]["sem"][0])])
-    return ops, sent
+        ops[o]["sem"] = (ops[o]["sem"], got[(ops[o]["c"], ops[o]["sem"])])
+    return ops, got
 
 
 def alike(ops):
     per = [[i for i, o in enumerate(ops) if o["c"] == c and o["kind"] != "a"] for c in range(N)]
-    calls = [[i for i in l if ops[i]["kind"] == "r"] for l in per]
     back = {}
-    for l in calls:
+    for l in per:
         for k, i in enumerate(l):
-            back[i] = calls[LEAD][k]
+            back[i] = per[LEAD][k]
     ids = per[LEAD] + [i for i, o in enumerate(ops) if o["c"] == LEAD and o["kind"] == "a"]
     at = {i: k for k, i in enumerate(ids)}
     return per, ids, [sorted(set(at[back.get(d, d)] for d in ops[i]["deps"])) for i in ids]
 
 
 def draw_up(topo, cores):
-    ops, sent = build(topo, cores, SETS[0])
+    ops, got = build(topo, cores, SETS[0])
     per, ids, deps = alike(ops)
     n = len(ids)
     R = range(n)
@@ -424,6 +445,7 @@ def draw_up(topo, cores):
     lead = [ops[i] for i in ids]
     alt = ["alt" in o for o in lead]
     home = [o["q"] for o in lead]
+    free_of_wake = [o["kind"] in "wa" for o in lead]
     succ = [[] for _ in R]
     for i in R:
         for d in deps[i]:
@@ -438,13 +460,12 @@ def draw_up(topo, cores):
     rank = [0.0] * n
     for j in reversed(top):
         rank[j] = min(sets[0][0][j].values()) + sets[0][1][j] + sets[0][2] + max([rank[k] for k in succ[j]] + [0.0])
-    rank = [rank[i] - lead[i]["bias"] for i in R]
 
     def order(nudge, pin, favour):
         dur, lat, wake = sets[0]
         todo = [len(d) for d in deps]
         at = [0.0] * n
-        ready = {q: [] for q in ("V", "S", "P", "G", "Y", None)}
+        ready = {q: [] for q in ("V", "S", "P", "G", "Y", "D", None)}
         free = {q: 0.0 for q in ready}
         seq = {q: [] for q in ready}
         qof = [None] * n
@@ -472,7 +493,7 @@ def draw_up(topo, cores):
             i, bp = -1, -1e9
             for j in ready[bq]:
                 if at[j] <= bt:
-                    p = pr[j] - (favour if bq == "V" and alt[j] else 0.0)
+                    p = -at[j] if bq == "D" else pr[j] - (favour if bq == "V" and alt[j] else 0.0)
                     if p > bp:
                         i, bp = j, p
             ready[bq].remove(i)
@@ -487,7 +508,7 @@ def draw_up(topo, cores):
             seq[bq].append(i)
             for k in succ[i]:
                 todo[k] -= 1
-                at[k] = max(at[k], e + lat[i] + (0.06 if bq == home[k] and not alt[k] else wake))
+                at[k] = max(at[k], e + lat[i] + (0.0 if free_of_wake[k] else wake))
                 if todo[k] == 0:
                     add(k)
         return seq, qof
@@ -515,7 +536,7 @@ def draw_up(topo, cores):
                         end = d
                     for k in succ[i]:
                         todo[k] -= 1
-                        a = d + (0.06 if q and qof[k] == q else wake)
+                        a = d + (0.0 if free_of_wake[k] else wake)
                         if a > at[k]:
                             at[k] = a
                         if todo[k] == 0 and qof[k] is None:
@@ -528,7 +549,7 @@ def draw_up(topo, cores):
         seed[0] = (seed[0] * 1103515245 + 12345) % (1 << 31)
         return (seed[0] >> 8) % m
 
-    work = [i for i in R if home[i] in ("V", "S")]
+    work = [i for i in R if home[i] in ("V", "S", "P", "G")]
     both = [i for i in work if alt[i]]
     cur = ([0.0] * n, [None] * n, 1.0)
     kept = order(*cur)
@@ -564,7 +585,206 @@ def draw_up(topo, cores):
             o = ops[per[c][k]]
             o["q"] = kept[1][k]
             o["emit"] = o["alt"][o["q"]][1]
-    return ops, sent, seq, [span(kept[0], kept[1], k) for k in range(len(SETS))]
+    return ops, got, seq, [span(kept[0], kept[1], k) for k in range(len(SETS))]
+
+
+def draw_up(topo, cores):
+    ops, got = build(topo, cores, SETS[0])
+    per, ids, deps = alike(ops)
+    n = len(ids)
+    R = range(n)
+    sets = []
+    for E in SETS:
+        full = build(topo, cores, E)[0]
+        lead = [full[i] for i in ids]
+        sets.append(([{q: v[0] for q, v in o["alt"].items()} if "alt" in o else {o["q"]: o["dur"]} for o in lead], [o["lat"] for o in lead], E["wake"]))
+    lead = [ops[i] for i in ids]
+    alt = ["alt" in o for o in lead]
+    home = [o["q"] for o in lead]
+    auto = [o["kind"] in "wa" for o in lead]
+    succ = [[] for _ in R]
+    for i in R:
+        for d in deps[i]:
+            succ[d].append(i)
+    count = [len(d) for d in deps]
+    cnt = list(count)
+    top = [i for i in R if cnt[i] == 0]
+    for i in top:
+        for j in succ[i]:
+            cnt[j] -= 1
+            if cnt[j] == 0:
+                top.append(j)
+    rank = [0.0] * n
+    for j in reversed(top):
+        rank[j] = min(sets[0][0][j].values()) + sets[0][1][j] + sets[0][2] + max([rank[x] for x in succ[j]] + [0.0])
+    above = [set() for _ in R]
+    for j in top:
+        for d in deps[j]:
+            above[j] |= above[d] | {d}
+    Q = "VSPGY"
+
+    def run(seq, which, pr=None, pin=None):
+        dur, lat, wake = sets[which]
+        todo = list(count)
+        at = [0.0] * n
+        start = [0.0] * n
+        free = dict.fromkeys(Q, 0.0)
+        pos = dict.fromkeys(Q, 0)
+        wire = end = total = 0.0
+        if pr:
+            ready = {q: [] for q in Q}
+            where = [[pin[i]] if pin[i] else list(dur[i]) for i in R]
+            for i in R:
+                if not count[i]:
+                    for q in where[i]:
+                        ready[q].append(i)
+        left = n
+        while left:
+            bt, bq, i = 1e9, None, -1
+            if pr:
+                for q in Q:
+                    if ready[q]:
+                        t = max(free[q], min([at[j] for j in ready[q]]))
+                        if t < bt:
+                            bt, bq = t, q
+                bp = -1e9
+                for j in ready[bq]:
+                    if at[j] <= bt + LOOK:
+                        p = pr[j] - (0.5 if bq == "V" and alt[j] else 0.0)
+                        if p > bp:
+                            i, bp = j, p
+                bt = max(bt, at[i])
+                for q in where[i]:
+                    ready[q].remove(i)
+                seq[bq].append(i)
+            else:
+                for q in Q:
+                    l = seq[q]
+                    p = pos[q]
+                    if p < len(l):
+                        j = l[p]
+                        if not todo[j]:
+                            t = at[j] if at[j] > free[q] else free[q]
+                            if t < bt:
+                                bt, bq, i = t, q, j
+                if bq is None:
+                    return None
+                pos[bq] += 1
+            start[i] = bt
+            e = free[bq] = bt + dur[i][bq]
+            total += e
+            done = [(i, e)]
+            while done:
+                j, e = done.pop()
+                left -= 1
+                if e > end:
+                    end = e
+                for x in succ[j]:
+                    todo[x] -= 1
+                    a = e if auto[x] else e + wake
+                    if a > at[x]:
+                        at[x] = a
+                    if not todo[x]:
+                        if home[x] == "D":
+                            wire = (at[x] if at[x] > wire else wire) + dur[x]["D"]
+                            start[x] = wire - dur[x]["D"]
+                            done.append((x, wire + lat[x]))
+                        elif auto[x]:
+                            done.append((x, at[x]))
+                        elif pr:
+                            for q in where[x]:
+                                ready[q].append(x)
+        return end, total / n, start
+
+    seed = [SEED]
+
+    def draw(m):
+        seed[0] = (seed[0] * 1103515245 + 12345) % (1 << 31)
+        return (seed[0] >> 8) % m
+
+    seq = {q: [] for q in Q}
+    run(seq, 0, rank, [None] * n)
+    base = [run(seq, x)[0] for x in range(len(SETS))]
+
+    def worth(seq):
+        v = 0.0
+        for x in range(len(SETS)):
+            r = run(seq, x)
+            if r is None:
+                return None, None
+            if x == 0:
+                start = r[2]
+            v += (r[0] + 0.1 * r[1]) / base[x]
+        return v / len(SETS), start
+    now, start = worth(seq)
+    best, kept = now, seq
+    work = [i for i in R if not auto[i]]
+    both = [i for i in work if alt[i]]
+    cur = (list(rank), [None] * n)
+    for step in range(DRAFTS):
+        pr, pin = list(cur[0]), list(cur[1])
+        x = draw(100)
+        if x < 35:
+            for _ in range(1 + draw(3)):
+                pr[work[draw(len(work))]] += (draw(41) - 20) / 10.0
+        elif x < 50:
+            a, d = draw(len(work)), (draw(41) - 20) / 10.0
+            for i in work[a:a + 3 + draw(30)]:
+                pr[i] += d
+        elif x < 75:
+            i, d, far = work[draw(len(work))], (draw(41) - 20) / 10.0, draw(50) / 10.0
+            for j in above[i] | {i}:
+                if rank[j] - rank[i] <= far:
+                    pr[j] += d
+        else:
+            for _ in range(1 + draw(3)):
+                pin[both[draw(len(both))]] = (None, "V", "S")[draw(3)]
+        new = {q: [] for q in Q}
+        run(new, 0, pr, pin)
+        v, s = worth(new)
+        if v <= now + 0.004 * max(0.0, 1.0 - step / (0.9 * DRAFTS)) * draw(1000) / 1000.0:
+            cur, now = (pr, pin), v
+            if v < best:
+                best, kept = v, new
+    seq = kept
+    now, start = worth(seq)
+    for step in range(STEPS):
+        i = work[draw(len(work))]
+        q = [x for x in Q if i in seq[x]][0]
+        to = ("S" if q == "V" else "V") if alt[i] and draw(3) == 0 else q
+        new = dict(seq)
+        new[q] = list(seq[q])
+        p = new[q].index(i)
+        if to != q:
+            new[q].pop(p)
+            new[to] = list(seq[to])
+            p = len([j for j in new[to] if start[j] < start[i]]) + draw(3) - 1
+            new[to].insert(max(0, p), i)
+        else:
+            m = 1 if draw(3) else 1 + draw(4)
+            piece = new[q][p:p + m]
+            del new[q][p:p + m]
+            d = 1 + draw(2 if draw(2) else 10)
+            p = max(0, p - d) if draw(2) else p + d
+            new[q][p:p] = piece
+        v, s = worth(new)
+        if v is not None and v <= now + 0.001 * max(0.0, 1.0 - step / (0.9 * STEPS)) * draw(1000) / 1000.0:
+            seq, now, start = new, v, s
+            if v < best:
+                best, kept = v, new
+    out = {}
+    start = run(kept, 0)[2]
+    kept = dict(kept)
+    kept["D"] = sorted([i for i in R if home[i] == "D"], key=lambda i: start[i])
+    for c in range(N):
+        for q, l in kept.items():
+            out[(c, q)] = [per[c][x] for x in l]
+            for x in l:
+                o = ops[per[c][x]]
+                if alt[x]:
+                    o["q"] = q
+                    o["emit"] = o["alt"][q][1]
+    return ops, got, out, [run(kept, x)[0] for x in range(len(SETS))]
 
 
 def plan(topo, cores):
@@ -577,10 +797,10 @@ def rank_program(g, core, T, topo):
     rank = T.rank_of(core)
     if rank is None:
         return
-    ops, sent, seq, _ = plan(topo, list(T.cores))
+    ops, got, seq, _ = plan(topo, list(T.cores))
     queues = {"V": g.vector, "S": g.scalar, "P": g.tensor, "G": g, "Y": g.sync}
     num = {}
-    tot = {"sent": sent[rank]}
+    tot = {k[1]: v for k, v in got.items() if k[0] == rank}
     for q in CSEM:
         k = 0
         for i in seq.get((rank, q), []):
@@ -592,11 +812,12 @@ def rank_program(g, core, T, topo):
     snap = {}
     pos = {q: 0 for q in queues}
     mine = sum(len(seq.get((rank, q), [])) for q in queues)
+    made = lambda d: ops[d]["by"] in snap if ops[d]["by"] is not None else (ops[d]["kind"] == "a" or d in snap)
     while mine:
         moved = False
         for q in queues:
             lst = seq.get((rank, q), [])
-            while pos[q] < len(lst) and all(ops[d]["kind"] in "ra" or d in snap for d in ops[lst[pos[q]]]["deps"]):
+            while pos[q] < len(lst) and all(made(d) for d in ops[lst[pos[q]]]["deps"]):
                 i = lst[pos[q]]
                 o = ops[i]
                 need = {}
@@ -615,16 +836,13 @@ def rank_program(g, core, T, topo):
                 if o["kind"] == "c":
                     ins.then_inc(T.sem[num[i][0]], 1)
                 elif o["kind"] == "d":
-                    ins.then_inc(T.sem[o["sem"][0]], 16)
+                    ins.then_inc(T.sem[o["sem"]], 16)
                 snap[i] = dict(known[q])
                 pos[q] += 1
                 mine -= 1
                 moved = True
         if not moved:
             raise ValueError("the plan does not close")
-    for o in ops:
-        if o["c"] == rank and o["kind"] in "da":
-            tot[o["sem"][0]] = o["sem"][1]
-    for name in SEMAPHORES:
+    for name in sorted(SEMAPHORES, key=lambda t: (t == "st", t in CSEM.values())):
         if tot.get(name, 0) > known["G"].get(name, 0):
             g.wait_ge(T.sem[name], tot[name])

@@ -12,7 +12,26 @@ SENDS = {1: [[(0, 0), (0, 1)], ["F"], [(1, 0), (1, 1)]], 2: [[(0, 0), (0, 1)], [
 PIECES = {0: 2, 1: 2}
 TILES = ["O", "F", (0, 0), (0, 1), (1, 0), (1, 1)]
 SPREAD = [[1, 2], [4, 5, 3]]
+HALVES = {s: [[[1, 2, 4, 5, 3]], [[3, 1, 2, 4, 5]]] for s in (1, 2)}
 FULL = False
+WHOLE = {1: True, 2: FULL}
+APART = False
+FAN = False
+PLANES = False
+RW, PW = (BW, 3 * BW) if PLANES else (4 * BW, BW)
+PIECES = {0: 1, 1: 2}
+SPLIT = {1: False, 2: False}
+SLOTS = [2, 4, 1, 5]
+FAR = [[(3, 0)], [(3, 1)]]
+CROSS = lambda h: [[[(2, h), (4, h)]], [[(1, h), (5, h)]]]
+SENDS = {s: [CROSS(0), [FAR], CROSS(1)] for s in (1, 2)}
+LISTS = {1: [[1, 5], [2, 4, 3]], 2: [[(0, 0), (0, 1)], ["F", (1, 0), (1, 1)]]}
+SLOTS = [1, 5, 2, 4]
+CROSS = lambda h: [[[(1, h)], [(5, h)]], [[(2, h)], [(4, h)]]]
+SENDS = {s: [CROSS(0), [FAR], CROSS(1)] for s in (1, 2)}
+BW = PW = 896
+RW = 4 * BW
+SPREAD = [[1, 5], [2, 4, 3]]
 if FULL:
     BW = 768
     LISTS = {1: [[0, 1, 2], [3, 4, 5]], 2: [[0, 1, 2], [3, 4, 5]]}
@@ -26,9 +45,9 @@ SCRATCH = {
     "eq": ("sbuf", [128, 512], "float8_e4m3fn_x4"),
     "ep": ("sbuf", [128, 512], "uint8"),
     "neg": ("sbuf", [128, 512], "float32"),
-    "bm": ("sbuf", [128, 32], "float32"),
-    "mask": ("sbuf", [128, 32], "float32"),
-    "rs": ("sbuf", [128, 192], "float32"),
+    "bm": ("sbuf", [128, 64], "float32"),
+    "mask": ("sbuf", [128, 64], "float32"),
+    "rs": ("sbuf", [128, 224], "float32"),
     "pi": ("sbuf", [128, 8], "int32"),
     "pf": ("sbuf", [128, 8], "float32"),
     "step": ("sbuf", [128, 8], "float32"),
@@ -49,32 +68,32 @@ for _s in (1, 2):
     SCRATCH["wp%d" % _s] = ("sbuf", [128, 768], "uint8")
     SCRATCH["oq%d" % _s] = ("sbuf", [128, 640], "float8_e4m3fn_x4")
     SCRATCH["op%d" % _s] = ("sbuf", [128, 640], "uint8")
-    SCRATCH["win%d" % _s] = ("sbuf", [128, 3072], "bfloat16")
+    SCRATCH["win"] = ("sbuf", [128, 7 * BW + 256], "bfloat16")
     SCRATCH["sc%d" % _s] = ("sbuf", [128, 4 * N], "float32")
     SCRATCH["gt%d" % _s] = ("sbuf", [128, N * 512], "bfloat16")
     SCRATCH["jk%d" % _s] = ("sbuf", [128, N * 512], "bfloat16")
     SCRATCH["rm%d" % _s] = ("sbuf", [128, N * 516], "float32")
-    SCRATCH["of%d" % _s] = ("sbuf", [128, 2, 16], "uint16")
+    SCRATCH["of%d" % _s] = ("sbuf", [128, 2, 4 if PLANES else 16], "uint16")
     for _i in list(range(len(LISTS[_s]))) + [N]:
         for _b in ("lx", "lt", "ls"):
             SCRATCH["%s%d_%d" % (_b, _s, _i)] = ("sbuf", [128, 192], "float32")
         if _i < N:
             SCRATCH["off%d_%d" % (_s, _i)] = ("sbuf", [128, 192], "uint16")
-    SEMAPHORES += ["pair%d" % _s] + ["wa%d_%d" % (_s, _i) for _i in range(len(SENDS[_s]))]
+    SEMAPHORES += ["pair%d_0" % _s, "pair%d_1" % _s] + ["wa%d_%d" % (_s, _i) for _i in range(len(SENDS[_s]))]
 for _r in range(N):
-    SEMAPHORES += ["xa1_%d" % _r, "xa2_0_%d" % _r, "xa2_1_%d" % _r]
+    SEMAPHORES += ["xa1_%d" % _r, "xa1_0_%d" % _r, "xa1_1_%d" % _r, "xa2_0_%d" % _r, "xa2_1_%d" % _r]
 
 CSEM = {"V": "cv", "S": "cs", "P": "cp", "G": "cg"}
 
 
-def estimate(f, wake, rem, row, rate, fix):
-    return {"v": 0.00083 * f, "s0": 0.024 * f, "s": 0.00083 * f, "sg": 0.00126 * f, "mm": 0.00076 * f, "g0": 0.13 * f,
+def estimate(f, wake, rem, row, rate, fix, call=0.0):
+    return {"call": call, "v": 0.00083 * f, "s0": 0.024 * f, "s": 0.00083 * f, "sg": 0.00126 * f, "mm": 0.00076 * f, "g0": 0.13 * f,
             "g": 0.0015 * f, "q": 0.00025 * f, "wake": wake, "rem": rem, "row": row, "byte": 1.0 / rate, "fix": fix, "dmai": 0.08}
 
 
-SETS = [estimate(1.2, 0.08, 0.3, 0.005, 16e3, 1.6), estimate(1.0, 0.06, 0.25, 0.003, 25e3, 1.6), estimate(1.5, 0.08, 0.3, 0.005, 16e3, 1.8),
-        estimate(1.2, 0.1, 0.6, 0.01, 12e3, 1.8)]
-DRAFTS, STEPS, LOOK, SEED = 6000, 25000, 0.15, 1
+SETS = [estimate(1.1, 0.08, 0.3, 0.005, 21e3, 1.45, 0.025), estimate(1.06, 0.15, 0.27, 0.004, 19e3, 1.1, 0.02),
+        estimate(1.4, 0.12, 0.45, 0.008, 13e3, 1.7, 0.035)]
+DRAFTS, STEPS, LOOK, SEED, AHEAD, HEAT = 3000, 30000, 0.15, 1, 0.0, 0.005
 LEAD = 2
 _memo = {}
 
@@ -101,8 +120,8 @@ def place(r, h, q):
     if FULL:
         return 128 * ((r - q) % N) + 64 * e
     if (q - r) % (N // 2) == 0:
-        return (4 * BW if h == 0 else 0) + (0 if q == r else 128) + 64 * e
-    return (0 if h == 0 else 4 * BW) + 64 * slot(r, q)
+        return 256 if q == r else 256 + K + 64 * e
+    return RW * h + 64 * SLOTS.index((r - q) % N)
 
 
 def shares(n, width):
@@ -119,7 +138,7 @@ def build(topo, cores, E):
     R = range(N)
 
     def op(c, q, dur, deps, emit, kind="c", sem=None, lat=0.0):
-        ops.append({"c": c, "q": q, "dur": dur, "deps": [d for d in deps if d is not None], "emit": emit, "kind": kind,
+        ops.append({"c": c, "q": q, "dur": dur + (E["call"] if q in ("V", "S") else 0.0), "deps": [d for d in deps if d is not None], "emit": emit, "kind": kind,
                     "sem": sem, "lat": lat, "by": None})
         return len(ops) - 1
 
@@ -134,7 +153,7 @@ def build(topo, cores, E):
         dv, ds = max(64, n) * E["v"], E["s0"] + max(64, n) * E["s"]
         if ind:
             dv, ds = 0.05 + n * E["sg"], 0.065 + n * E["sg"]
-        ops[i]["alt"] = {"V": (dv, ev), "S": (ds, es)}
+        ops[i]["alt"] = {"V": (dv + E["call"], ev), "S": (ds + E["call"], es)}
         return i
 
     def copy(c, n, deps, to, fr, by=None, ind=False):
@@ -163,8 +182,10 @@ def build(topo, cores, E):
     def QZ(c, n, deps, emit):
         return op(c, "V", 0.015 + 4 * n * E["q"], deps, emit)
 
-    def send(c, width, parts, deps, more=0.0):
+    def send(c, width, parts, deps, more=None):
         eng = topo.engines(cores[c], cores[parts[0][2][0][0]])
+        if more is not None:
+            eng = eng[more * len(eng) // 2:(more + 1) * len(eng) // 2]
         w = shares(len(parts), len(eng))
 
         def emit(g, T):
@@ -183,15 +204,21 @@ def build(topo, cores, E):
             for d, _ in to:
                 got[(d, sem)] = got.get((d, sem), 0) + w[i]
             got[(c, "sent")] = got.get((c, "sent"), 0) + w[i]
-        r = op(c, "G", E["rem"] + 0.06 * (len(parts) - 1) + more, deps, emit, "r")
-        t = max(128 * len(p[2]) / w[i] * (E["row"] + width * E["byte"]) for i, p in enumerate(parts))
+        r = op(c, "G", E["rem"] + 0.06 * (len(parts) - 1), deps, emit, "r")
+        t = max(128 * len(p[2]) / w[i] * (E["row"] + width * E["byte"]) for i, p in enumerate(parts)) / (1 if more is None else 2)
         return op(c, "D", t, [r], None, "w", None, E["fix"])
 
-    def send_mx(c, n, parts, deps, more=0.0, which=(1, 4)):
+    def after(w):
+        return [ops[i]["deps"][0] for i in w[-1:]]
+
+    def send_mx(c, n, parts, deps, more=None, which=(1, 4)):
         words = lambda b, a: lambda T: T[b[0]][:, a:a + n].bitcast(dt.uint8)
         plane = lambda b, a: lambda T: T[b[1]][:, a:a + n]
-        return [send(c, k * n, [(sem, f(b, a), [(d, f(b2, a2)) for d, b2, a2 in to]) for sem, b, a, to in parts], deps, more)
-                for k, f in ((1, plane), (4, words)) if k in which]
+        w = []
+        for k, f in ((4, words), (1, plane)):
+            if k in which:
+                w.append(send(c, k * n, [(sem, f(b, a), [(d, f(b2, a2)) for d, b2, a2 in to]) for sem, b, a, to in parts], deps + after(w), more))
+        return w
 
     XQ = lambda s: ("xq%d" % s, "xp%d" % s)
     WQ = lambda s: ("wq%d" % s, "wp%d" % s)
@@ -199,213 +226,269 @@ def build(topo, cores, E):
     quant = lambda b, a, n, fr: lambda g, T: g.vector.quantize_mx(T[b[0]][:, a:a + n], T[b[1]][:, a:a + n], fr(T))
     acol = lambda T, p: T.pf[p, 0:1]
     st = [{} for _ in R]
+
+    def fill(c, n, val, to, p=slice(0, 128), deps=()):
+        return S(c, n, [st[c]["ones"]] + list(deps), lambda g, T: g.scalar.activation(to(T, p), T.ones[p, 0:n], F.Copy, scale=float(val)))
+
     for c in R:
         s = st[c]
         s["ldx"] = D(c, "Y", 1024, [], lambda g, T: g.sync.dma_start(T.xt[:], T.x[:]), "ld_x")
         s["ld1"] = [D(c, "Y", 2048, [], lambda g, T, a=a: g.sync.dma_start(T.ct1[:, 1024 * a:1024 * a + 1024], T.c1[:, 1024 * a:1024 * a + 1024]), "ld_c1_%d" % a) for a in range(2)]
-        s["x1_0"] = QZ(c, 128, [s["ldx"]], quant(XQ(1), 0, 128, lambda T: T.xt[:]))
+        s["x1_0"] = s["x1_0_0"] = s["x1_1_0"] = QZ(c, 128, [s["ldx"]], quant(XQ(1), 0 if WHOLE[1] else 64, 128, lambda T: T.xt[:]))
         s["qc1"] = [QZ(c, 256, [s["ld1"][a]], quant(("cq1", "cp1"), 256 * a, 256, lambda T, a=a: T.ct1[:, 1024 * a:1024 * a + 1024])) for a in range(2)]
-        s["neg"] = V(c, 512, [], lambda g, T: g.vector.memset(T.neg[:], -1e29))
         s["ones"] = V(c, 258, [], lambda g, T: g.vector.memset(T.ones[:], 1.0))
+        s["neg"] = fill(c, 512, -1e29, lambda T, p: T.neg[:])
         pi = G(c, 1, [], lambda g, T: g.iota(T.pi[:, 0:1], [[0, 1]], 0, 1))
-        bm = G(c, 32, [], lambda g, T: g.iota(T.bm[:], [[0, 2], [1, 4], [0, 4]], 0, 0, allow_small_or_imprecise_dtypes=True))
+        bm = s["bm"] = G(c, 32, [], lambda g, T: g.iota(T.bm[:, 0:32], [[0, 2], [1, 4], [0, 4]], 0, 0, allow_small_or_imprecise_dtypes=True))
         bits = [V(c, 1, [pi], lambda g, T, k=k, m=m: g.vector.tensor_scalar(T.pi[:, k:k + 1], T.pi[:, 0:1], m, None, A.bitwise_and)) for k, m in ((1, 3), (2, 28), (3, 32))]
         s["acol"] = V(c, 1, [bits[0]], lambda g, T: g.vector.tensor_copy(T.pf[:, 0:1], T.pi[:, 1:2]))
-        s["mask"] = V(c, 32, [bm, s["acol"]], lambda g, T: g.vector.tensor_scalar(T.mask[:], T.bm[:], T.pf[:, 0:1], None, A.is_equal))
+        s["mask"] = V(c, 32, [bm, s["acol"]], lambda g, T: g.vector.tensor_scalar(T.mask[:, 0:32], T.bm[:, 0:32], T.pf[:, 0:1], None, A.is_equal))
         u = V(c, 1, [bits[1], s["acol"]], lambda g, T: g.vector.tensor_scalar(T.pf[:, 2:3], T.pi[:, 2:3], 2.0, T.pf[:, 0:1], A.mult, A.add))
-        s["step"] = [V(c, 1, [bits[2], u], lambda g, T: g.vector.tensor_scalar(T.step[:, 0:1], T.pi[:, 3:4], 0.125, T.pf[:, 2:3], A.mult, A.add))]
-        s["aw"] = [V(c, 1, [s["acol"]], lambda g, T, e=e, b=place(c, (c + e) % 2, 0): g.vector.tensor_scalar(
-            T.pf[64 * e:64 * e + 64, 1:2], T.pf[64 * e:64 * e + 64, 0:1], float(BW), float(b), A.mult, A.add)) for e in range(2)]
-        r1 = V(c, 192, [], lambda g, T: g.vector.memset(T.rs[:], 1.0))
-        s["rs"] = V(c, 48, [r1], lambda g, T: g.vector.memset(T.rs[:, 0::4], 0.0))
-        s["one"] = [V(c, 1, [], lambda g, T, k=k: g.vector.memset(T["dc%d" % k][:, 8:9], 1.0)) for k in (1, 2)]
-        s["z"] = [V(c, 128, [], lambda g, T, z=z: g.vector.memset(T.rt[:, z:z + 256], 0.0)) for z in (0, 768) if not FULL]
+        u = V(c, 1, [bits[2], u], lambda g, T: g.vector.tensor_scalar(T.pf[:, 3:4], T.pi[:, 3:4], 0.125, T.pf[:, 2:3], A.mult, A.add))
+        s["step"] = []
+        for e in range(2):
+            h = (c + e) % 2
+            for to, m, b in ((("step", 0), 1, place(c, h, 0)), (("pf", 4), -1 if c else 0, 256 - (place(c, h, c - 1) if c else 0)), (("pf", 5), 1, place(c, h, c + 1) - 256)):
+                s["step"].append(V(c, 1, [u], lambda g, T, to=to, m=m, b=b, p=slice(64 * e, 64 * e + 64): g.vector.tensor_scalar(
+                    T[to[0]][p, to[1]:to[1] + 1], T.pf[p, 3:4], float(m), float(b), A.mult, A.add)))
+        s["gap"] = [V(c, 320, [], lambda g, T, a=RW + BW * b: g.vector.memset(T.win[:, a + 256:a + BW], 0.0)) for b in range(3)]
+        r1 = fill(c, 224, 1.0, lambda T, p: T.rs[:])
+        s["rs"] = fill(c, 48, 0.0, lambda T, p: T.rs[:, 0:192:4], deps=[r1])
+        if PLANES:
+            b16 = G(c, 32, [], lambda g, T: g.iota(T.bm[:, 32:64], [[0, 2], [1, 16]], 0, 0, allow_small_or_imprecise_dtypes=True))
+            p16 = V(c, 1, [pi], lambda g, T: g.vector.tensor_scalar(T.pi[:, 4:5], T.pi[:, 0:1], 15, None, A.bitwise_and))
+            f16 = V(c, 1, [p16], lambda g, T: g.vector.tensor_copy(T.pf[:, 1:2], T.pi[:, 4:5]))
+            s["aw"] = [V(c, 32, [b16, f16], lambda g, T: g.vector.tensor_scalar(T.mask[:, 32:64], T.bm[:, 32:64], T.pf[:, 1:2], None, A.is_equal)),
+                       V(c, 2, [r1], lambda g, T: g.vector.memset(T.rs[:, 192:224:16], 0.0))]
+            s["mask16"], s["rs16"] = s["aw"]
+        else:
+            s["aw"] = [V(c, 1, [s["acol"]], lambda g, T: g.vector.tensor_scalar(T.pf[:, 1:2], T.pf[:, 0:1], float(BW), None, A.mult))]
+        s["one"] = [fill(c, 1, 1.0, lambda T, p, k=k: T["dc%d" % k][:, 8:9]) for k in (1, 2)]
+        s["z"] = [fill(c, 256, 0.0, lambda T, p, z=z: T.rt[:, z:z + 256]) for z in (0, 768)]
 
     def spread(c, stage, more):
         sem = ("xa1_%d" if stage == 1 else "xa2_0_%d") % c
         part = lambda l: [(sem, XQ(stage), 0, [((c - k) % N, XQ(stage), 128 * k) for k in l])]
-        w = send_mx(c, 128, part([k for l in SPREAD for k in l]), [st[c]["x%d_0" % stage]], more, (1,))
+        u = w = [] if APART else send_mx(c, 128, part([k for l in SPREAD for k in l]), [st[c]["x%d_0" % stage]], 0, (1,))
         for l in SPREAD:
-            u = send_mx(c, 128, part(l), [st[c]["x%d_0" % stage]], 0.0, (4,))
+            u = send_mx(c, 128, part(l), [st[c]["x%d_0" % stage]] + after(u), 1 if l == SPREAD[0] else None, (1, 4) if APART else (4,))
             for k in l:
                 st[(c - k) % N]["x%d_%d" % (stage, k)] = arrive((c - k) % N, sem, w + u)
 
+    def spread_half(c, stage, h):
+        sem, e = "xa%d_%d_%d" % (stage, h, c), side(c, h)
+        col = lambda k: 128 + 128 * TILES.index("F" if k == N // 2 else (h, slot(k, 0) // 2)) + 64 * e
+        part = lambda l: [(sem, XQ(stage), 64 + 64 * e, [((c - k) % N, XQ(stage), col(k)) for k in l])]
+        calls = HALVES[stage][h]
+        dep = [st[c]["x%d_%d_0" % (stage, h)]]
+        u = send_mx(c, 64, part(calls[0]), dep, None, (4,))
+        w = send_mx(c, 64, part([k for l in calls for k in l]), dep + after(u), None, (1,))
+        for l in calls:
+            if l != calls[0]:
+                u = send_mx(c, 64, part(l), dep + after(w), None, (4,))
+            for k in l:
+                st[(c - k) % N]["x%d_%d_%d" % (stage, h, k)] = arrive((c - k) % N, sem, w + u)
+
     for c in R:
         s = st[c]
-        spread(c, 1, 0.0)
-        s["zt"] = G(c, 516, [s["ones"]], lambda g, T: g.affine_select(T.zt[:], T.ones[:], [[-1, 516]], A.is_equal, 0.0, 4, 4))
-        late = []
+        s["q512"] = G(c, 6, [], lambda g, T: g.iota(T.q512[:, 0:N], [[K, N]], 0, 0, allow_small_or_imprecise_dtypes=True))
+        s["zt"] = G(c, 516, [s["ones"], s["q512"], s["bm"]], lambda g, T: g.affine_select(T.zt[:], T.ones[:], [[-1, 516]], A.is_equal, 0.0, 4, 4))
+        if WHOLE[1]:
+            spread(c, 1, 0.0)
+        else:
+            for h in range(2):
+                spread_half(c, 1, h)
         for e in range(2):
             for q in range(1, N):
                 h = (c + e) % 2
-                s["step"].append(V(c, 1, [], lambda g, T, e=e, q=q, b=place(c, h, q) - place(c, h, q - 1): g.vector.memset(
-                    T.step[64 * e:64 * e + 64, q:q + 1], float(b))))
-        s["q512"] = G(c, 6, late, lambda g, T: g.iota(T.q512[:, 0:N], [[K, N]], 0, 0, allow_small_or_imprecise_dtypes=True))
-        s["eq"] = [QZ(c, 128, [s["zt"]], quant(("eq", "ep"), 128 * b, 128, lambda T, b=b: T.zt[:, 4 - b:516 - b])) for b in range(4)]
+                s["step"].append(fill(c, 1, place(c, h, q) - place(c, h, q - 1), lambda T, p, q=q: T.step[p, q:q + 1], slice(64 * e, 64 * e + 64)))
+        s["eq"] = [QZ(c, 128, [s["zt"], s["x1_0"]], quant(("eq", "ep"), 128 * b, 128, lambda T, b=b: T.zt[:, 4 - b:516 - b])) for b in range(4)]
+        s["made"] = [s[k] for k in ("neg", "mask", "rs")] + s["aw"] + s["one"] + s["z"] + s["step"] + s["eq"] + s["gap"]
 
-    def listed(c, tag, vals, deps, out, fold, deps2, low):
+    def listed(c, tag, vals, deps, out, fold, deps2, low, es=(0, 1), w=4):
         n = 32 * len(vals)
+        p = slice(64 * es[0], 64 * es[-1] + 64)
+        m0, r0, mask, rs = (0, 0, "mask", "rs") if w == 4 else (32, 192, "mask16", "rs16")
         lx, lt, ls = ["%s%s" % (b, tag) for b in ("lx", "lt", "ls")]
-        m = [copy(c, 32, [deps[k], st[c]["mask"]], lambda T, k=k: T[lx][:, 32 * k:32 * k + 32], lambda T: T.mask[:], vals[k]) for k in range(len(vals))]
-        t = V(c, n, m, lambda g, T: g.vector.transpose(T[lt][:, 0:n], T[lx][:, 0:n]))
-        z = V(c, n, [t, st[c]["rs"]], lambda g, T: g.vector.tensor_tensor_scan(T[ls][:, 0:n], T.rs[:, 0:n], T[lt][:, 0:n], 0.0, A.mult, A.add))
-        cv = [V(c, n // 4, [z] + deps2, lambda g, T, e=e: fold(g, T, out(T, e), T[ls][64 * e:64 * e + 64, 3:n:4], slice(64 * e, 64 * e + 64))) for e in range(2)]
+        m = [copy(c, 32, [deps[k], st[c][mask]], lambda T, k=k: T[lx][p, 32 * k:32 * k + 32], lambda T: T.mask[p, m0:m0 + 32], vals[k]) for k in range(len(vals))]
+        t = V(c, n, m, lambda g, T: g.vector.transpose(T[lt][p, 0:n], T[lx][p, 0:n]))
+        z = V(c, n, [t, st[c][rs]], lambda g, T: g.vector.tensor_tensor_scan(T[ls][p, 0:n], T.rs[p, r0:r0 + n], T[lt][p, 0:n], 0.0, A.mult, A.add))
+        cv = [V(c, n // 4, [z] + deps2, lambda g, T, e=e: fold(g, T, out(T, e), T[ls][64 * e:64 * e + 64, w - 1:n:w], e)) for e in es]
         q0 = V(c, n // 4, cv, lambda g, T: g.vector.tensor_copy(low(T, slice(0, 32), 1), low(T, slice(32, 64), 0)))
-        return [q0] + [V(c, n // 2, [q0], lambda g, T, a=a: g.vector.tensor_copy(low(T, slice(a, a + 32), None), low(T, slice(0, 32), None))) for a in (32, 64, 96)]
+        if FAN:
+            return [q0] + [V(c, n // 2, [q0], lambda g, T, a=a: g.vector.tensor_copy(low(T, slice(a, a + 32), None), low(T, slice(0, 32), None))) for a in (32, 64, 96)]
+        q1 = V(c, n // 2, [q0], lambda g, T: g.vector.tensor_copy(low(T, slice(32, 64), None), low(T, slice(0, 32), None)))
+        return [V(c, n // 2, [q1], lambda g, T: g.vector.tensor_copy(low(T, slice(64, 128), None), low(T, slice(0, 64), None)))]
 
     banks = [[None] * 8 for _ in R]
     turn = [0] * N
-    pairs = {s: [[] for _ in R] for s in (1, 2)}
+    pairs = {s: [[[], []] for _ in R] for s in (1, 2)}
     cands = {s: [[[] for _ in SENDS[s]] for _ in R] for s in (1, 2)}
 
     def search(c, stage):
         s = st[c]
         rm, gt, ct = "rm%d" % stage, "gt%d" % stage, "ct%d" % stage
-        flat = [k for l in LISTS[stage] for k in l]
+        flat = [0 if WHOLE[stage] else "O"] + [k for l in LISTS[stage] for k in l]
         at = {k: 516 * i for i, k in enumerate(flat)}
         sg = {}
         for i, k in enumerate(flat):
-            if stage == 1 or FULL:
+            if WHOLE[stage]:
                 col, need = 128 * k, [s["x%d_%d" % (stage, k)]]
             else:
                 col = 64 if k == "O" else 128 + 128 * TILES.index(k)
-                need = [s["x2_%d_%d" % (h, d)] for d, h in halves(k)]
+                need = [s["x%d_%d_%d" % (stage, h, d)] for d, h in halves(k)]
             bank = turn[c] % 4
             turn[c] += 1
             ps = lambda T, bank=bank: T.ps[:, 512 * bank:512 * bank + 512]
             m = MM(c, 512, need + s["qc%d" % stage] + [banks[c][bank]], lambda g, T, col=col, ps=ps: g.tensor.matmul_mx(
                 ps(T), T["xq%d" % stage][:, col:col + 128], T["xp%d" % stage][:, col:col + 128], T["cq%d" % stage][:], T["cp%d" % stage][:], True, True))
             a = at[k]
-            sc = V(c, 512, [m, s["neg"]], lambda g, T, a=a, ps=ps: g.vector.tensor_tensor_scan(T[rm][:, a:a + 512], ps(T), T.neg[:], -1e29, A.max, A.max))
+            sc = V(c, 512, [m] + s["made"], lambda g, T, a=a, ps=ps: g.vector.tensor_tensor_scan(T[rm][:, a:a + 512], ps(T), T.neg[:], -1e29, A.max, A.max))
             banks[c][bank] = sc
             s["scan%d_%d" % (stage, i)] = sc
             sg[k] = S(c, 512, [sc], lambda g, T, a=a, i=i: g.scalar.activation(
                 T["jk%d" % stage][:, 512 * i:512 * i + 512], T[rm][:, a:a + 512], F.Sign, bias=T[rm][:, a + 511:a + 512], scale=-1.0, accum_out=T[rm][:, a + 512:a + 513]))
         pair = lambda k, p=slice(0, 128): lambda T: T[rm][p, at[k] + 511:at[k] + 513]
         land = lambda e, p=slice(0, 128): lambda T: T["sc%d" % stage][p, 4 * c + 2 * e:4 * c + 2 * e + 2]
-        if stage == 1 or FULL:
+        if WHOLE[stage]:
             pp = [("pair%d" % stage, pair(k), [((c + k) % N, land(0))]) for k in flat if k]
             s["own%d" % stage] = [copy(c, 2, [sg[0]], land(0), pair(0))]
         else:
-            pp = [("pair2", pair(k), [((c + d) % N, land(side(c + d, h))) for d, h in halves(k)]) for k in flat if k != "O"]
-            s["own2"] = [copy(c, 2, [sg["O"]], land(e, slice(64 * e, 64 * e + 64)), pair("O", slice(64 * e, 64 * e + 64))) for e in range(2)]
-        o = send(c, 8, pp, [sg[k] for k in flat if k not in (0, "O")])
-        for r in R:
-            if r != c:
-                pairs[stage][r].append(o)
+            pp = [("pair%d" % stage, pair(k), [((c + d) % N, land(side(c + d, h))) for d, h in halves(k)]) for k in flat if k != "O"]
+            s["own%d" % stage] = [copy(c, 2, [sg["O"]], land(e, slice(64 * e, 64 * e + 64)), pair("O", slice(64 * e, 64 * e + 64))) for e in range(2)]
+        word = lambda T: T[rm][:, 512:513]
+        s["hop%d" % stage] = [X(c, 1, [sg[flat[0]]] + s["step"] + s.get("pv", []),
+                                lambda g, T, k=k, m=m: g.vector.tensor_scalar(T.step[:, c + k:c + k + 1], word(T), m, T.pf[:, 4 + k:5 + k], A.mult, A.add),
+                                lambda g, T, k=k, m=m: g.scalar.activation(T.step[:, c + k:c + k + 1], word(T), F.Identity, bias=T.pf[:, 4 + k:5 + k], scale=m)) for k, m in ((0, 1.0), (1, -1.0))]
+        rest = [k for k in flat if k not in (0, "O")]
+        for h in range(2 if SPLIT[stage] else 1):
+            pick = [i for i, k in enumerate(rest) if not SPLIT[stage] or (k == "F" or k[0] == 0) == (h == 0)]
+            o = send(c, 8, [("pair%d_%d" % (stage, h),) + pp[i][1:] for i in pick], [sg[rest[i]] for i in pick])
+            for r in R:
+                if r != c:
+                    pairs[stage][r][h].append(o)
         where = {}
         for i, l in enumerate(LISTS[stage]):
             off, n = "off%d_%d" % (stage, i), 16 * len(l)
             ls = listed(c, "%d_%d" % (stage, i), [lambda T, k=k: T[rm][:, at[k] + 512:at[k] + 513] for k in l], [sg[k] for k in l],
                         lambda T, e, off=off, n=n: T[off][0:64, n * e:n * e + n:2],
-                        lambda g, T, o, f, p: g.vector.tensor_scalar(o, f, 4.0, acol(T, p), A.mult, A.add), [s["acol"]],
+                        lambda g, T, o, f, e: g.vector.tensor_scalar(o, f, 4.0, T.pf[64 * e:64 * e + 64, 0:1], A.mult, A.add), [s["acol"]],
                         lambda T, p, e, off=off, n=n: T[off][p, 0:2 * n] if e is None else T[off][p, e:2 * n:2])
             for j, k in enumerate(l):
                 where[k] = (off, n, j, ls)
-        qs = {}
-        for i, t in enumerate(TILES):
-            ga = []
-            for d, h in halves(t):
-                e = side(c + d, h)
-                off, n, j, ls = where[d if stage == 1 or FULL else t]
-                o = n * e + 16 * j
-                ga.append(copy(c, 256, ls + s["ld%d" % stage], lambda T, a=512 * i + 256 * e: T[gt][:, a:a + 256],
-                               lambda T, off=off, o=o: T[ct][:, 0:4 * K].indirect(T[off][:, o:o + 16]), None, True))
-            qs[t] = QZ(c, 128, ga, quant(*((WQ(stage), 0) if i == 0 else (OQ(stage), 128 * i - 128)), 128, lambda T, i=i: T[gt][:, 512 * i:512 * i + 512]))
-        s["w%d" % stage] = qs[TILES[0]]
+        of = {dh: (dh[0] if WHOLE[stage] else t) for t in TILES for dh in halves(t)}
+        col = [128]
+
+        def pack(groups, buf, a):
+            ga, got_, c0 = [], {}, col[0]
+            both = len(groups) == 2 and groups[0][0][0] == groups[1][0][0]
+            for i, l in enumerate(groups):
+                e = side(c + l[0][0], l[0][1])
+                off, n, j, ls = where[of[l[0]]]
+                o, m, x = n * e + 16 * j, len(l), (c0 + 64 * e if both else col[0])
+                ga.append(copy(c, 256 * m, ls + s["ld%d" % stage], lambda T, x=x, m=m: T[gt][:, 4 * x:4 * x + 256 * m],
+                               lambda T, off=off, o=o, m=m: T[ct][:, 0:4 * K].indirect(T[off][:, o:o + 16 * m]), None, True))
+                for k, dh in enumerate(l):
+                    got_[dh] = a + x - c0 + 64 * k
+                col[0] += 64 * m
+            n = col[0] - c0
+            return QZ(c, n, ga, quant(buf, a, n, lambda T: T[gt][:, 4 * c0:4 * c0 + 4 * n])), got_
         for i, l in enumerate(SENDS[stage]):
             sem = "wa%d_%d" % (stage, i)
-            if FULL:
-                w = send_mx(c, 128, [(sem, OQ(stage), 128 * t - 128, [((c + t) % N, WQ(stage), 128 * t)]) for t in l], [qs[t] for t in l])
-            elif l == ["F"]:
-                w = send_mx(c, 128, [(sem, OQ(stage), 0, [((c + N // 2) % N, WQ(stage), 128)])], [qs["F"]])
+            qs, cols = [], {}
+            for groups in l:
+                q, x = pack(groups, OQ(stage), col[0] - 128)
+                qs.append(q)
+                cols.update(x)
+            if l == [FAR]:
+                w = send_mx(c, 128, [(sem, OQ(stage), min(cols.values()), [((c + N // 2) % N, WQ(stage), 128)])], qs)
             else:
-                pc = []
-                for t in l:
-                    for d, h in halves(t):
-                        r, e = (c + d) % N, side(c + d, h)
-                        to = 128 + 64 * e if t == "F" else 256 + 256 * h + 64 * slot(r, c)
-                        pc.append((sem, OQ(stage), 128 * TILES.index(t) - 128 + 64 * e, [(r, WQ(stage), to)]))
-                w = send_mx(c, 64, pc, [qs[t] for t in l])
-            for r in sorted(set((c + d) % N for t in l for d, _ in halves(t))):
+                w = send_mx(c, 64, [(sem, OQ(stage), x, [((c + d) % N, WQ(stage), 128 + 64 * side(c + d, h) if d == N // 2 else 256 + 256 * h + 64 * SLOTS.index(d))])
+                                    for (d, h), x in cols.items()], qs)
+            for r in sorted(set((c + d) % N for d, _ in cols)):
                 cands[stage][r][i] += w
 
     def finish(c, stage):
         s = st[c]
-        dc, sc, win, of = "dc%d" % stage, "sc%d" % stage, "win%d" % stage, "of%d" % stage
-        pa = [arrive(c, "pair%d" % stage, pairs[stage][c])] + s["own%d" % stage]
-        sides = [(slice(0, 128), 0)] if stage == 1 or FULL else [(slice(0, 64), 0), (slice(64, 128), 2)]
-        rm = [V(c, 6, pa + [s["neg"]], lambda g, T, p=p, a=a: g.vector.tensor_tensor_scan(T[dc][p, 0:N], T[sc][p, a::4], T.neg[p, 0:N], -1e29, A.max, A.max)) for p, a in sides]
-        lt = V(c, 6, rm, lambda g, T: g.vector.tensor_scalar(T[dc][:, 9:9 + N], T[dc][:, 0:N], T[dc][:, N - 1:N], None, A.is_lt))
-        pv = V(c, 6, [lt] + s["one"] + s["step"], lambda g, T: g.vector.tensor_tensor(T[dc][:, 16:16 + N], T[dc][:, 8:8 + N], T.step[:, 0:N], A.mult))
-        v = V(c, 6, [pv], lambda g, T: g.vector.tensor_reduce(T[dc][:, 7:8], T[dc][:, 16:16 + N], AxisListType.X, A.add))
-        ls = listed(c, "%d_%d" % (stage, N), [lambda T: T[dc][:, 7:8]], [v], lambda T, e: T[of][0:64, e, 0:8],
-                    lambda g, T, o, f, p: g.vector.tensor_scalar(o, f, T.pf[p, 1:2], None, A.add), s["aw"],
-                    lambda T, p, e: T[of][p, :, :] if e is None else T[of][p, :, 8 * e:8 * e + 8])
+        dc, sc, win, of = "dc%d" % stage, "sc%d" % stage, "win", "of%d" % stage
+        pa = [arrive(c, "pair%d_%d" % (stage, h), pairs[stage][c][h]) for h in range(2 if SPLIT[stage] else 1)]
+        first = pa[:1] + s["own%d" % stage]
+        pa = pa + s["own%d" % stage]
+        sides = [(slice(0, 128), 0)] if WHOLE[stage] else [(slice(0, 64), 0), (slice(64, 128), 2)]
+        if SPLIT[stage]:
+            sides = [sides[side(c, h)] for h in range(2)]
+        rm = [V(c, 6, (first if SPLIT[stage] and h == 0 else pa) + [s["neg"]], lambda g, T, p=p, a=a: g.vector.tensor_tensor_scan(
+            T[dc][p, 0:N], T[sc][p, a::4], T.neg[p, 0:N], -1e29, A.max, A.max)) for h, (p, a) in enumerate(sides)]
+        lts, lss, u = [], [], (2 if PLANES else 8)
+        for h in range(2 if SPLIT[stage] else 1):
+            p, es, w = (sides[h][0], (side(c, h),), side(c, h)) if SPLIT[stage] else (slice(0, 128), (0, 1), slice(0, 2))
+            lt = V(c, 6, rm[h:h + 1] if SPLIT[stage] else rm, lambda g, T, p=p: g.vector.tensor_scalar(T[dc][p, 9:9 + N], T[dc][p, 0:N], T[dc][p, N - 1:N], None, A.is_lt))
+            pv = V(c, 6, [lt] + s["one"] + s["hop%d" % stage], lambda g, T, p=p: g.vector.tensor_tensor(T[dc][p, 16:16 + N], T[dc][p, 8:8 + N], T.step[p, 0:N], A.mult))
+            v = V(c, 6, [pv], lambda g, T, p=p: g.vector.tensor_reduce(T[dc][p, 7:8], T[dc][p, 16:16 + N], AxisListType.X, A.add))
+            lss.append(listed(c, "%d_%d" % (stage, N), [lambda T, p=p: T[dc][p, 7:8]], [v], lambda T, e: T[of][0:64, e, 0:u],
+                              lambda g, T, o, f, e: g.vector.tensor_scalar(o, f, float(place(c, (c + e) % 2, 0)) if PLANES else T.pf[64 * e:64 * e + 64, 1:2], None, A.add), s["aw"],
+                              lambda T, p, e, w=w: T[of][p, w, :] if e is None else T[of][p, w, u * e:u * e + u], es, 32 // u))
+            lts.append(lt)
+            s.setdefault("pv", []).append(pv)
         gn = [V(c, 6, pa + [s["q512"]], lambda g, T, p=p, a=a: g.vector.tensor_tensor(T[dc][p, 24:24 + N], T[sc][p, a + 1::4], T.q512[p, 0:N], A.add)) for p, a in sides]
-        oh = V(c, 6, [lt] + s["one"], lambda g, T: g.vector.tensor_tensor(T[dc][:, 32:32 + N], T[dc][:, 8:8 + N], T[dc][:, 9:9 + N], A.subtract))
+        oh = V(c, 6, lts + s["one"], lambda g, T: g.vector.tensor_tensor(T[dc][:, 32:32 + N], T[dc][:, 8:8 + N], T[dc][:, 9:9 + N], A.subtract))
         pr = V(c, 6, gn + [oh], lambda g, T: g.vector.tensor_tensor(T[dc][:, 40:40 + N], T[dc][:, 24:24 + N], T[dc][:, 32:32 + N], A.mult))
         nu = V(c, 6, [pr], lambda g, T: g.vector.tensor_reduce(T[dc][:, 48:49], T[dc][:, 40:40 + N], AxisListType.X, A.add))
-        for row, cc, dep in ((stage - 1, 48, [nu]), (stage + 1, N - 1, rm)):
-            D(c, "Y", 4, dep, lambda g, T, row=row, cc=cc: g.sync.dma_start(T.no[row:row + 1, :], T[dc][:, cc:cc + 1]), "st")
-        runs = [(s["w%d" % stage], 0, 128, 0 if FULL else 4 * BW, (0, 1))]
+        s["no%d" % stage] = [(dep, lambda g, T, row=row, cc=cc: g.sync.dma_start(T.no[row:row + 1, :], T[dc][:, cc:cc + 1])) for row, cc, dep in ((stage - 1, 48, [nu]), (stage + 1, N - 1, rm))]
+        n = K // len(s["qc%d" % stage])
+        runs = [(q, n * i, n, 256 + n * i, (0, 1)) for i, q in enumerate(s["qc%d" % stage])]
+        book = len(runs)
         for i, l in enumerate(SENDS[stage]):
             wa = arrive(c, "wa%d_%d" % (stage, i), cands[stage][c][i])
-            if FULL:
-                for k in (l[:4], l[4:]):
-                    if k:
-                        runs.append((wa, 128 * k[0], 128 * len(k), 128 * k[0], (0, 1)))
-                continue
-            if "F" in l:
-                runs.append((wa, 128, 128, 4 * BW + 128, (0, 1)))
+            if FAR in l:
+                runs.append((wa, 128, 128, 256 + K, (0, 1)))
             for h in range(2):
-                k = [t[1] for t in l if t != "F" and t[0] == h]
+                k = [SLOTS.index(d) for p in l if p != FAR for x in p for d, e in x if e == h]
                 if k:
-                    runs.append((wa, 256 + 256 * h + 128 * min(k), 128 * len(k), 8 * BW * h + 128 * min(k), (h,)))
-        cps = [[], []]
+                    runs.append((wa, 256 + 256 * h + 64 * min(k), 64 * len(k), RW * h + 64 * min(k), (0, 1)[h:]))
+        cps = [[[], [], [], []] for h in range(2)]
         for i, (dep, a, n, o, hs) in enumerate(runs):
             for b in range(4):
-                bank = b + 4 * ((i + stage) % 2 if i else 1)
-                u = MM(c, n, [dep, s["eq"][b], banks[c][bank]], lambda g, T, b=b, a=a, n=n, bank=bank: g.tensor.matmul_mx(
+                bank = b + 4 * ((i - book + 1 + stage) % 2 if i >= book else 1)
+                q = "w" if i >= book else "c"
+                mm = MM(c, n, [dep, s["eq"][b], banks[c][bank]], lambda g, T, b=b, a=a, n=n, bank=bank, q=q: g.tensor.matmul_mx(
                     T.ps[:, 512 * bank:512 * bank + n], T.eq[:, 128 * b:128 * b + 128], T.ep[:, 128 * b:128 * b + 128],
-                    T["wq%d" % stage][:, a:a + n], T["wp%d" % stage][:, a:a + n], True, True))
-                cp = copy(c, n, [u], lambda T, b=b, o=o, n=n: T[win][:, BW * b + o:BW * b + o + n], lambda T, bank=bank, n=n: T.ps[:, 512 * bank:512 * bank + n], lambda T: -1.0)
+                    T["%sq%d" % (q, stage)][:, a:a + n], T["%sp%d" % (q, stage)][:, a:a + n], True, True))
+                cp = copy(c, n, [mm] + (s["r0"] + s["r1"] if stage == 2 else []), lambda T, b=b, o=o, n=n: T[win][:, PW * b + o:PW * b + o + n], lambda T, bank=bank, n=n: T.ps[:, 512 * bank:512 * bank + n], lambda T: -1.0)
                 banks[c][bank] = cp
+                if b == 0:
+                    s["landed"] = mm
                 for h in hs:
-                    cps[h].append(cp)
+                    cps[h][b].append(cp)
         for h in range(2):
             e = side(c, h)
-            w0, w1 = (0, 4 * BW) if FULL else (4 * BW * h, 4 * BW * h + 8 * BW)
-            pick = lambda T, a, n, e=e, w0=w0, w1=w1: T[win][:, w0:w1].indirect(T[of][:, e, a // 16:(a + n) // 16])
+            ls = lss[h % len(lss)]
+            to, fr = (("rt", 256), ("xt", 0)) if stage == 1 else (("yt", 0), ("rt", 256))
+            cut = lambda T, v, b, e=e: T[v[0]][:, v[1] + 256 * e + b:v[1] + 256 * e + 256:4]
+            base = ls + ([s["ldx"]] if stage == 1 else s["r%d" % h])
+            if PLANES:
+                r = [op(c, "V", 0.05 + 64 * E["sg"], cps[h][b] + base, lambda g, T, b=b, h=h, e=e, to=to, fr=fr, cut=cut: g.vector.tensor_tensor(
+                    cut(T, to, b), T[win][:, BW * (3 * b + h):BW * (3 * b + h + 2)].indirect(T[of][:, e, :]), cut(T, fr, b), A.add)) for b in range(4)]
+            else:
+                n = 256 // (1 if stage == 1 else PIECES[h])
+                r = [op(c, "V", 0.05 + n * E["sg"], sum(cps[h], []) + base, lambda g, T, a=a, n=n, h=h, e=e, to=to, fr=fr: g.vector.tensor_tensor(
+                    T[to[0]][:, to[1] + 256 * e + a:to[1] + 256 * e + a + n], T[win][:, 0:(7 * BW + 256 if h else RW)].indirect(T[of][:, e, a // 16:(a + n) // 16]),
+                    T[fr[0]][:, fr[1] + 256 * e + a:fr[1] + 256 * e + a + n], A.add)) for a in range(0, 256, n)]
             if stage == 1:
-                r = op(c, "V", 0.05 + 256 * E["sg"], cps[h] + ls + [s["ldx"]], lambda g, T, e=e, pick=pick: g.vector.tensor_tensor(
-                    T.rt[:, 256 + 256 * e:512 + 256 * e], pick(T, 0, 256), T.xt[:, 256 * e:256 * e + 256], A.add))
                 s["r%d" % h] = r
-                if FULL:
-                    if h == 1:
-                        s["x2_0"] = QZ(c, 128, [s["r0"], r], quant(XQ(2), 0, 128, lambda T: T.rt[:, 256:768]))
-                        spread(c, 2, 0.0)
-                    continue
-                q2 = QZ(c, 128, [r] + s["z"], quant(XQ(2), 128 * e, 128, lambda T, e=e: T.rt[:, 512 * e:512 * e + 512]))
+                q2 = QZ(c, 128, r + s["z"], quant(XQ(2), 128 * e, 128, lambda T, e=e: T.rt[:, 512 * e:512 * e + 512]))
                 s["x2_%d_0" % h] = q2
-                to = []
-                for i in ([5, 4, 2, 1, 3] if h == 0 else [3, 5, 4, 2, 1]):
-                    d = (c + i) % N
-                    t = "F" if i == N // 2 else (h, slot(c, d) // 2)
-                    to.append((d, XQ(2), 128 + 128 * TILES.index(t) + 64 * e))
-                w = send_mx(c, 64, [("xa2_%d_%d" % (h, c), XQ(2), 64 + 64 * e, to)], [q2])
-                for i in range(1, N):
-                    st[(c + i) % N]["x2_%d_%d" % (h, N - i)] = arrive((c + i) % N, "xa2_%d_%d" % (h, c), w)
+                ops[q2]["ahead"] = h == 0
+                spread_half(c, 2, h)
             else:
                 n = 256 // PIECES[h]
                 for k in range(PIECES[h]):
                     a = 256 * e + n * k
-                    y = op(c, "V", 0.05 + n * E["sg"], cps[h] + ls + [s["r%d" % h]], lambda g, T, a=a, k=k, n=n, pick=pick: g.vector.tensor_tensor(
-                        T.yt[:, a:a + n], pick(T, n * k, n), T.rt[:, 256 + a:256 + a + n], A.add))
+                    y = r if PLANES else r[k:k + 1]
                     if k % 2 == 0:
-                        D(c, "Y", 4 * n, [y], lambda g, T, a=a, n=n: g.sync.dma_start(T.y[:, a:a + n], T.yt[:, a:a + n]), "st")
+                        D(c, "Y", 4 * n, y, lambda g, T, a=a, n=n: g.sync.dma_start(T.y[:, a:a + n], T.yt[:, a:a + n]), "st")
                     else:
-                        D(c, "S", 4 * n, [y], lambda g, T, a=a, n=n: g.scalar.dma_start(T.y[:, a:a + n], T.yt[:, a:a + n]), "st")
+                        D(c, "S", 4 * n, y, lambda g, T, a=a, n=n: g.scalar.dma_start(T.y[:, a:a + n], T.yt[:, a:a + n]), "st")
 
     for stage in (1, 2):
         for c in R:
@@ -416,6 +499,10 @@ def build(topo, cores, E):
                 s["qc2"] = [QZ(c, 512, s["ld2"], quant(("cq2", "cp2"), 0, 512, lambda T: T.ct2[:]))]
         for c in R:
             finish(c, stage)
+    for c in R:
+        for stage, when in ((1, "scan2_1"), (2, "landed")):
+            for dep, emit in st[c]["no%d" % stage]:
+                D(c, "Y", 4, dep + [st[c][when]], emit, "st")
     for o in arr:
         ops[o]["sem"] = (ops[o]["sem"], got[(ops[o]["c"], ops[o]["sem"])])
     return ops, got
@@ -621,6 +708,8 @@ def draw_up(topo, cores):
     for j in top:
         for d in deps[j]:
             above[j] |= above[d] | {d}
+    for j in set().union(*[above[i] | {i} for i in R if lead[i].get("ahead")]):
+        rank[j] += AHEAD
     Q = "VSPGY"
 
     def run(seq, which, pr=None, pin=None):
@@ -628,7 +717,9 @@ def draw_up(topo, cores):
         todo = list(count)
         at = [0.0] * n
         start = [0.0] * n
+        why = [-1] * n
         free = dict.fromkeys(Q, 0.0)
+        last = dict.fromkeys(Q + "D", -1)
         pos = dict.fromkeys(Q, 0)
         wire = end = total = 0.0
         if pr:
@@ -670,6 +761,9 @@ def draw_up(topo, cores):
                 if bq is None:
                     return None
                 pos[bq] += 1
+            if bt > at[i]:
+                why[i] = last[bq]
+            last[bq] = i
             start[i] = bt
             e = free[bq] = bt + dur[i][bq]
             total += e
@@ -678,14 +772,18 @@ def draw_up(topo, cores):
                 j, e = done.pop()
                 left -= 1
                 if e > end:
-                    end = e
+                    end, fin = e, j
                 for x in succ[j]:
                     todo[x] -= 1
                     a = e if auto[x] else e + wake
                     if a > at[x]:
                         at[x] = a
+                        why[x] = j
                     if not todo[x]:
                         if home[x] == "D":
+                            if wire > at[x]:
+                                why[x] = last["D"]
+                            last["D"] = x
                             wire = (at[x] if at[x] > wire else wire) + dur[x]["D"]
                             start[x] = wire - dur[x]["D"]
                             done.append((x, wire + lat[x]))
@@ -694,7 +792,7 @@ def draw_up(topo, cores):
                         elif pr:
                             for q in where[x]:
                                 ready[q].append(x)
-        return end, total / n, start
+        return end, total / n, start, why, fin
 
     seed = [SEED]
 
@@ -704,20 +802,21 @@ def draw_up(topo, cores):
 
     seq = {q: [] for q in Q}
     run(seq, 0, rank, [None] * n)
-    base = [run(seq, x)[0] for x in range(len(SETS))]
+    base = [run(seq, x)[0] * len(SETS) for x in range(len(SETS))]
 
-    def worth(seq):
-        v = 0.0
+    def worth(seq, was=None, room=0.0):
+        v, rs = [], []
         for x in range(len(SETS)):
             r = run(seq, x)
             if r is None:
                 return None, None
-            if x == 0:
-                start = r[2]
-            v += (r[0] + 0.1 * r[1]) / base[x]
-        return v / len(SETS), start
-    now, start = worth(seq)
-    best, kept = now, seq
+            rs.append(r)
+            v.append((r[0] + 0.1 * r[1]) / base[x])
+            if was and x == 0 and v[0] > was[0] + room + 0.001:
+                return None, None
+        return v, rs
+    now, rs = worth(seq)
+    best, kept = sum(now), seq
     work = [i for i in R if not auto[i]]
     both = [i for i in work if alt[i]]
     cur = (list(rank), [None] * n)
@@ -741,15 +840,27 @@ def draw_up(topo, cores):
                 pin[both[draw(len(both))]] = (None, "V", "S")[draw(3)]
         new = {q: [] for q in Q}
         run(new, 0, pr, pin)
-        v, s = worth(new)
-        if v <= now + 0.004 * max(0.0, 1.0 - step / (0.9 * DRAFTS)) * draw(1000) / 1000.0:
+        room = 0.004 * max(0.0, 1.0 - step / (0.9 * DRAFTS)) * draw(1000) / 1000.0
+        v, s = worth(new, now, room)
+        if v and sum(v) <= sum(now) + room:
             cur, now = (pr, pin), v
-            if v < best:
-                best, kept = v, new
+            if sum(v) < best:
+                best, kept = sum(v), new
     seq = kept
-    now, start = worth(seq)
+    now, rs = worth(seq)
+
+    def chain(r):
+        l, j = [], r[4]
+        while j >= 0:
+            if not auto[j]:
+                l.append(j)
+            j = r[3][j]
+        return l
+    crit = [chain(r) for r in rs]
     for step in range(STEPS):
-        i = work[draw(len(work))]
+        start = rs[0][2]
+        l = crit[draw(len(crit))] if draw(2) else work
+        i = l[draw(len(l))]
         q = [x for x in Q if i in seq[x]][0]
         to = ("S" if q == "V" else "V") if alt[i] and draw(3) == 0 else q
         new = dict(seq)
@@ -760,6 +871,11 @@ def draw_up(topo, cores):
             new[to] = list(seq[to])
             p = len([j for j in new[to] if start[j] < start[i]]) + draw(3) - 1
             new[to].insert(max(0, p), i)
+            near = [j for j in new[to][max(0, p - 3):p + 4] if alt[j] and j != i]
+            if near and draw(2):
+                j = near[draw(len(near))]
+                new[to].remove(j)
+                new[q].insert(len([x for x in new[q] if start[x] < start[j]]), j)
         else:
             m = 1 if draw(3) else 1 + draw(4)
             piece = new[q][p:p + m]
@@ -767,11 +883,13 @@ def draw_up(topo, cores):
             d = 1 + draw(2 if draw(2) else 10)
             p = max(0, p - d) if draw(2) else p + d
             new[q][p:p] = piece
-        v, s = worth(new)
-        if v is not None and v <= now + 0.001 * max(0.0, 1.0 - step / (0.9 * STEPS)) * draw(1000) / 1000.0:
-            seq, now, start = new, v, s
-            if v < best:
-                best, kept = v, new
+        room = HEAT * max(0.0, 1.0 - step / (0.9 * STEPS)) * draw(1000) / 1000.0
+        v, s = worth(new, now, room)
+        if v and sum(v) <= sum(now) + room:
+            seq, now, rs = new, v, s
+            crit = [chain(r) for r in rs]
+            if sum(v) < best:
+                best, kept = sum(v), new
     out = {}
     start = run(kept, 0)[2]
     kept = dict(kept)
@@ -822,6 +940,8 @@ def rank_program(g, core, T, topo):
                 o = ops[i]
                 need = {}
                 for d in o["deps"]:
+                    if ops[d]["kind"] == "r":
+                        continue
                     name, cnt = num[d] if ops[d]["kind"] == "c" else ops[d]["sem"]
                     if need.get(name, (0, None))[0] < cnt:
                         need[name] = (cnt, snap.get(d))

from concourse.bass import DstId, RemoteDMATransfer
from concourse.mybir import dt, AluOpType, AxisListType, ActivationFunctionType

N = 6
K = 512
A = AluOpType
F = ActivationFunctionType
BW = 256

LISTS = {1: [[0, 1, 2], [4, 5, 3]], 2: [["O", (0, 0), (0, 1)], ["F", (1, 0), (1, 1)]]}
SENDS = {1: [[(0, 0), (0, 1)], ["F"], [(1, 0), (1, 1)]], 2: [[(0, 0), (0, 1)], ["F"], [(1, 0), (1, 1)]]}
PIECES = {0: 2, 1: 2}
TILES = ["O", "F", (0, 0), (0, 1), (1, 0), (1, 1)]
SPREAD = [[1, 2], [4, 5, 3]]
HALVES = {s: [[[1, 2, 4, 5, 3]], [[3, 1, 2, 4, 5]]] for s in (1, 2)}
FULL = False
WHOLE = {1: True, 2: FULL}
APART = False
FAN = False
PLANES = False
RW, PW = (BW, 3 * BW) if PLANES else (4 * BW, BW)
PIECES = {0: 1, 1: 2}
SPLIT = {1: False, 2: False}
SLOTS = [2, 4, 1, 5]
FAR = [[(3, 0)], [(3, 1)]]
CROSS = lambda h: [[[(2, h), (4, h)]], [[(1, h), (5, h)]]]
SENDS = {s: [CROSS(0), [FAR], CROSS(1)] for s in (1, 2)}
LISTS = {1: [[1, 5], [2, 4, 3]], 2: [[(0, 0), (0, 1)], ["F", (1, 0), (1, 1)]]}
SLOTS = [1, 5, 2, 4]
CROSS = lambda h: [[[(1, h)], [(5, h)]], [[(2, h)], [(4, h)]]]
SENDS = {s: [CROSS(0), [FAR], CROSS(1)] for s in (1, 2)}
BW = PW = 896
RW = 4 * BW
SPREAD = [[1, 5], [2, 4, 3]]
if FULL:
    BW = 768
    LISTS = {1: [[0, 1, 2], [3, 4, 5]], 2: [[0, 1, 2], [3, 4, 5]]}
    SENDS = {1: [[1, 2], [3, 4, 5]], 2: [[1, 2], [3, 4, 5]]}
    TILES = list(range(N))

SCRATCH = {
    "xt": ("sbuf", [128, 512], "bfloat16"),
    "ones": ("sbuf", [128, 516], "bfloat16"),
    "zt": ("sbuf", [128, 516], "bfloat16"),
    "eq": ("sbuf", [128, 512], "float8_e4m3fn_x4"),
    "ep": ("sbuf", [128, 512], "uint8"),
    "neg": ("sbuf", [128, 512], "float32"),
    "bm": ("sbuf", [128, 64], "float32"),
    "mask": ("sbuf", [128, 64], "float32"),
    "rs": ("sbuf", [128, 224], "float32"),
    "pi": ("sbuf", [128, 8], "int32"),
    "pf": ("sbuf", [128, 8], "float32"),
    "step": ("sbuf", [128, 8], "float32"),
    "q512": ("sbuf", [128, 8], "float32"),
    "rt": ("sbuf", [128, 1024], "bfloat16"),
    "yt": ("sbuf", [128, 512], "float32"),
    "ps": ("psum", [128, 4096], "float32"),
}
SEMAPHORES = ["cv", "cs", "cp", "cg", "sent", "ld_x", "ld_c1_0", "ld_c1_1", "ld_c2_0", "st"]
for _s in (1, 2):
    SCRATCH["ct%d" % _s] = ("sbuf", [128, 4 * K], "bfloat16")
    SCRATCH["cq%d" % _s] = ("sbuf", [128, K], "float8_e4m3fn_x4")
    SCRATCH["cp%d" % _s] = ("sbuf", [128, K], "uint8")
    SCRATCH["xq%d" % _s] = ("sbuf", [128, 896], "float8_e4m3fn_x4")
    SCRATCH["xp%d" % _s] = ("sbuf", [128, 896], "uint8")
    SCRATCH["dc%d" % _s] = ("sbuf", [128, 64], "float32")
    SCRATCH["wq%d" % _s] = ("sbuf", [128, 768], "float8_e4m3fn_x4")
    SCRATCH["wp%d" % _s] = ("sbuf", [128, 768], "uint8")
    SCRATCH["oq%d" % _s] = ("sbuf", [128, 640], "float8_e4m3fn_x4")
    SCRATCH["op%d" % _s] = ("sbuf", [128, 640], "uint8")
    SCRATCH["win"] = ("sbuf", [128, 7 * BW + 256], "bfloat16")
    SCRATCH["sc%d" % _s] = ("sbuf", [128, 4 * N], "float32")
    SCRATCH["gt%d" % _s] = ("sbuf", [128, N * 512], "bfloat16")
    SCRATCH["jk%d" % _s] = ("sbuf", [128, N * 512], "bfloat16")
    SCRATCH["rm%d" % _s] = ("sbuf", [128, N * 516], "float32")
    SCRATCH["of%d" % _s] = ("sbuf", [128, 2, 4 if PLANES else 16], "uint16")
    for _i in list(range(len(LISTS[_s]))) + [N]:
        for _b in ("lx", "lt", "ls"):
            SCRATCH["%s%d_%d" % (_b, _s, _i)] = ("sbuf", [128, 192], "float32")
        if _i < N:
            SCRATCH["off%d_%d" % (_s, _i)] = ("sbuf", [128, 192], "uint16")
    SEMAPHORES += ["pair%d_0" % _s, "pair%d_1" % _s] + ["wa%d_%d" % (_s, _i) for _i in range(len(SENDS[_s]))]
for _r in range(N):
    SEMAPHORES += ["xa1_%d" % _r, "xa1_0_%d" % _r, "xa1_1_%d" % _r, "xa2_0_%d" % _r, "xa2_1_%d" % _r]

CSEM = {"V": "cv", "S": "cs", "P": "cp", "G": "cg"}


def estimate(f, wake, rem, row, rate, fix, call=0.0):
    return {"call": call, "v": 0.00083 * f, "s0": 0.024 * f, "s": 0.00083 * f, "sg": 0.00126 * f, "mm": 0.00076 * f, "g0": 0.13 * f,
            "g": 0.0015 * f, "q": 0.00025 * f, "wake": wake, "rem": rem, "row": row, "byte": 1.0 / rate, "fix": fix, "dmai": 0.08}


SETS = [estimate(1.1, 0.08, 0.3, 0.005, 21e3, 1.45, 0.025), estimate(1.06, 0.15, 0.27, 0.004, 19e3, 1.1, 0.02),
        estimate(1.4, 0.12, 0.45, 0.008, 13e3, 1.7, 0.035)]
DRAFTS, STEPS, LOOK, SEED, AHEAD, HEAT = 3000, 30000, 0.15, 1, 0.0, 0.005
LEAD = 2
_memo = {}


def side(r, h):
    return (r + h) % 2


def slot(r, c):
    k = (r - c) % N
    return k - 1 if k < N // 2 else k - 2


def halves(t):
    if FULL:
        return [(t, h) for h in range(2)]
    if t in ("O", "F"):
        return [(0 if t == "O" else N // 2, h) for h in range(2)]
    return [(3 * t[1] + 1, t[0]), (3 * t[1] + 2, t[0])]


def place(r, h, q):
    e = side(r, h)
    if FULL:
        return 128 * ((r - q) % N) + 64 * e
    if (q - r) % (N // 2) == 0:
        return 256 if q == r else 256 + K + 64 * e
    return RW * h + 64 * SLOTS.index((r - q) % N)


def shares(n, width):
    w = [width]
    while len(w) < n:
        w = sorted(w[1:] + [w[0] // 2] * 2, reverse=True)
    return w


def build(topo, cores, E):
    ops = []
    got = {}
    arr = []
    R = range(N)

    def op(c, q, dur, deps, emit, kind="c", sem=None, lat=0.0):
        ops.append({"c": c, "q": q, "dur": dur + (E["call"] if q in ("V", "S") else 0.0), "deps": [d for d in deps if d is not None], "emit": emit, "kind": kind,
                    "sem": sem, "lat": lat, "by": None})
        return len(ops) - 1

    def V(c, n, deps, emit):
        return op(c, "V", max(64, n) * E["v"], deps, emit)

    def S(c, n, deps, emit):
        return op(c, "S", E["s0"] + max(64, n) * E["s"], deps, emit)

    def X(c, n, deps, ev, es, ind=False):
        i = op(c, "V", 0.0, deps, None)
        dv, ds = max(64, n) * E["v"], E["s0"] + max(64, n) * E["s"]
        if ind:
            dv, ds = 0.05 + n * E["sg"], 0.065 + n * E["sg"]
        ops[i]["alt"] = {"V": (dv + E["call"], ev), "S": (ds + E["call"], es)}
        return i

    def copy(c, n, deps, to, fr, by=None, ind=False):
        if by is None:
            return X(c, n, deps, lambda g, T: g.vector.tensor_copy(to(T), fr(T)), lambda g, T: g.scalar.activation(to(T), fr(T), F.Copy), ind)
        return X(c, n, deps, lambda g, T: g.vector.tensor_scalar(to(T), fr(T), by(T), None, A.mult), lambda g, T: g.scalar.activation(to(T), fr(T), F.Copy, scale=by(T)))

    def G(c, n, deps, emit):
        return op(c, "G", E["g0"] + n * E["g"], deps, emit)

    def MM(c, n, deps, emit):
        return op(c, "P", (n + 16) * E["mm"], deps, emit)

    def arrive(c, sem, deps, by=None):
        o = op(c, None, 0.0, deps, None, "a", sem)
        ops[o]["by"] = by
        arr.append(o)
        return o

    def D(c, q, width, deps, emit, sem):
        d = op(c, q, E["dmai"], deps, emit, "d", sem)
        w = op(c, "D", 8 * (E["row"] + width * E["byte"]), [d], None, "w", None, E["fix"])
        got[(c, sem)] = got.get((c, sem), 0) + 16
        return arrive(c, sem, [w], d)

    def QZ(c, n, deps, emit):
        return op(c, "V", 0.015 + 4 * n * E["q"], deps, emit)

    def send(c, width, parts, deps, more=None):
        eng = topo.engines(cores[c], cores[parts[0][2][0][0]])
        if more is not None:
            eng = eng[more * len(eng) // 2:(more + 1) * len(eng) // 2]
        w = shares(len(parts), len(eng))

        def emit(g, T):
            ts = []
            for i, (sem, src, to) in enumerate(parts):
                m = 0
                for e in eng[sum(w[:i]):sum(w[:i + 1])]:
                    m |= 1 << e
                ids = []
                for d, _ in to:
                    rid, pid, _ = topo.addr(cores[d])
                    ids.append(DstId(rid=rid, pnc=pid))
                ts.append(RemoteDMATransfer(dst_ids=ids, dma_engine_mask=m, remote_sem=T.sem[sem], srcs=[src(T)], dsts=[land(T) for _, land in to], alu_op=0))
            return g.remote_dma_fused(ts, local_sem=T.sem.sent)
        for i, (sem, _, to) in enumerate(parts):
            for d, _ in to:
                got[(d, sem)] = got.get((d, sem), 0) + w[i]
            got[(c, "sent")] = got.get((c, "sent"), 0) + w[i]
        r = op(c, "G", E["rem"] + 0.06 * (len(parts) - 1), deps, emit, "r")
        t = max(128 * len(p[2]) / w[i] * (E["row"] + width * E["byte"]) for i, p in enumerate(parts)) / (1 if more is None else 2)
        return op(c, "D", t, [r], None, "w", None, E["fix"])

    def after(w):
        return [ops[i]["deps"][0] for i in w[-1:]]

    def send_mx(c, n, parts, deps, more=None, which=(1, 4)):
        words = lambda b, a: lambda T: T[b[0]][:, a:a + n].bitcast(dt.uint8)
        plane = lambda b, a: lambda T: T[b[1]][:, a:a + n]
        w = []
        for k, f in ((4, words), (1, plane)):
            if k in which:
                w.append(send(c, k * n, [(sem, f(b, a), [(d, f(b2, a2)) for d, b2, a2 in to]) for sem, b, a, to in parts], deps + after(w), more))
        return w

    XQ = lambda s: ("xq%d" % s, "xp%d" % s)
    WQ = lambda s: ("wq%d" % s, "wp%d" % s)
    OQ = lambda s: ("oq%d" % s, "op%d" % s)
    quant = lambda b, a, n, fr: lambda g, T: g.vector.quantize_mx(T[b[0]][:, a:a + n], T[b[1]][:, a:a + n], fr(T))
    acol = lambda T, p: T.pf[p, 0:1]
    st = [{} for _ in R]

    def fill(c, n, val, to, p=slice(0, 128), deps=()):
        return S(c, n, [st[c]["ones"]] + list(deps), lambda g, T: g.scalar.activation(to(T, p), T.ones[p, 0:n], F.Copy, scale=float(val)))

    for c in R:
        s = st[c]
        s["ldx"] = D(c, "Y", 1024, [], lambda g, T: g.sync.dma_start(T.xt[:], T.x[:]), "ld_x")
        s["ld1"] = [D(c, "Y", 2048, [], lambda g, T, a=a: g.sync.dma_start(T.ct1[:, 1024 * a:1024 * a + 1024], T.c1[:, 1024 * a:1024 * a + 1024]), "ld_c1_%d" % a) for a in range(2)]
        s["x1_0"] = s["x1_0_0"] = s["x1_1_0"] = QZ(c, 128, [s["ldx"]], quant(XQ(1), 0 if WHOLE[1] else 64, 128, lambda T: T.xt[:]))
        s["qc1"] = [QZ(c, 256, [s["ld1"][a]], quant(("cq1", "cp1"), 256 * a, 256, lambda T, a=a: T.ct1[:, 1024 * a:1024 * a + 1024])) for a in range(2)]
        s["ones"] = V(c, 258, [], lambda g, T: g.vector.memset(T.ones[:], 1.0))
        s["neg"] = fill(c, 512, -1e29, lambda T, p: T.neg[:])
        pi = G(c, 1, [], lambda g, T: g.iota(T.pi[:, 0:1], [[0, 1]], 0, 1))
        bm = s["bm"] = G(c, 32, [], lambda g, T: g.iota(T.bm[:, 0:32], [[0, 2], [1, 4], [0, 4]], 0, 0, allow_small_or_imprecise_dtypes=True))
        bits = [V(c, 1, [pi], lambda g, T, k=k, m=m: g.vector.tensor_scalar(T.pi[:, k:k + 1], T.pi[:, 0:1], m, None, A.bitwise_and)) for k, m in ((1, 3), (2, 28), (3, 32))]
        s["acol"] = V(c, 1, [bits[0]], lambda g, T: g.vector.tensor_copy(T.pf[:, 0:1], T.pi[:, 1:2]))
        s["mask"] = V(c, 32, [bm, s["acol"]], lambda g, T: g.vector.tensor_scalar(T.mask[:, 0:32], T.bm[:, 0:32], T.pf[:, 0:1], None, A.is_equal))
        u = V(c, 1, [bits[1], s["acol"]], lambda g, T: g.vector.tensor_scalar(T.pf[:, 2:3], T.pi[:, 2:3], 2.0, T.pf[:, 0:1], A.mult, A.add))
        u = V(c, 1, [bits[2], u], lambda g, T: g.vector.tensor_scalar(T.pf[:, 3:4], T.pi[:, 3:4], 0.125, T.pf[:, 2:3], A.mult, A.add))
        s["step"] = []
        for e in range(2):
            h = (c + e) % 2
            for to, m, b in ((("step", 0), 1, place(c, h, 0)), (("pf", 4), -1 if c else 0, 256 - (place(c, h, c - 1) if c else 0)), (("pf", 5), 1, place(c, h, c + 1) - 256)):
                s["step"].append(V(c, 1, [u], lambda g, T, to=to, m=m, b=b, p=slice(64 * e, 64 * e + 64): g.vector.tensor_scalar(
                    T[to[0]][p, to[1]:to[1] + 1], T.pf[p, 3:4], float(m), float(b), A.mult, A.add)))
        s["gap"] = [V(c, 320, [], lambda g, T, a=RW + BW * b: g.vector.memset(T.win[:, a + 256:a + BW], 0.0)) for b in range(3)]
        r1 = fill(c, 224, 1.0, lambda T, p: T.rs[:])
        s["rs"] = fill(c, 48, 0.0, lambda T, p: T.rs[:, 0:192:4], deps=[r1])
        if PLANES:
            b16 = G(c, 32, [], lambda g, T: g.iota(T.bm[:, 32:64], [[0, 2], [1, 16]], 0, 0, allow_small_or_imprecise_dtypes=True))
            p16 = V(c, 1, [pi], lambda g, T: g.vector.tensor_scalar(T.pi[:, 4:5], T.pi[:, 0:1], 15, None, A.bitwise_and))
            f16 = V(c, 1, [p16], lambda g, T: g.vector.tensor_copy(T.pf[:, 1:2], T.pi[:, 4:5]))
            s["aw"] = [V(c, 32, [b16, f16], lambda g, T: g.vector.tensor_scalar(T.mask[:, 32:64], T.bm[:, 32:64], T.pf[:, 1:2], None, A.is_equal)),
                       V(c, 2, [r1], lambda g, T: g.vector.memset(T.rs[:, 192:224:16], 0.0))]
            s["mask16"], s["rs16"] = s["aw"]
        else:
            s["aw"] = [V(c, 1, [s["acol"]], lambda g, T: g.vector.tensor_scalar(T.pf[:, 1:2], T.pf[:, 0:1], float(BW), None, A.mult))]
        s["one"] = [fill(c, 1, 1.0, lambda T, p, k=k: T["dc%d" % k][:, 8:9]) for k in (1, 2)]
        s["z"] = [fill(c, 256, 0.0, lambda T, p, z=z: T.rt[:, z:z + 256]) for z in (0, 768)]

    def spread(c, stage, more):
        sem = ("xa1_%d" if stage == 1 else "xa2_0_%d") % c
        part = lambda l: [(sem, XQ(stage), 0, [((c - k) % N, XQ(stage), 128 * k) for k in l])]
        u = w = [] if APART else send_mx(c, 128, part([k for l in SPREAD for k in l]), [st[c]["x%d_0" % stage]], 0, (1,))
        for l in SPREAD:
            u = send_mx(c, 128, part(l), [st[c]["x%d_0" % stage]] + after(u), 1 if l == SPREAD[0] else None, (1, 4) if APART else (4,))
            for k in l:
                st[(c - k) % N]["x%d_%d" % (stage, k)] = arrive((c - k) % N, sem, w + u)

    def spread_half(c, stage, h):
        sem, e = "xa%d_%d_%d" % (stage, h, c), side(c, h)
        col = lambda k: 128 + 128 * TILES.index("F" if k == N // 2 else (h, slot(k, 0) // 2)) + 64 * e
        part = lambda l: [(sem, XQ(stage), 64 + 64 * e, [((c - k) % N, XQ(stage), col(k)) for k in l])]
        calls = HALVES[stage][h]
        dep = [st[c]["x%d_%d_0" % (stage, h)]]
        u = send_mx(c, 64, part(calls[0]), dep, None, (4,))
        w = send_mx(c, 64, part([k for l in calls for k in l]), dep + after(u), None, (1,))
        for l in calls:
            if l != calls[0]:
                u = send_mx(c, 64, part(l), dep + after(w), None, (4,))
            for k in l:
                st[(c - k) % N]["x%d_%d_%d" % (stage, h, k)] = arrive((c - k) % N, sem, w + u)

    for c in R:
        s = st[c]
        s["q512"] = G(c, 6, [], lambda g, T: g.iota(T.q512[:, 0:N], [[K, N]], 0, 0, allow_small_or_imprecise_dtypes=True))
        s["zt"] = G(c, 516, [s["ones"], s["q512"], s["bm"]], lambda g, T: g.affine_select(T.zt[:], T.ones[:], [[-1, 516]], A.is_equal, 0.0, 4, 4))
        if WHOLE[1]:
            spread(c, 1, 0.0)
        else:
            for h in range(2):
                spread_half(c, 1, h)
        for e in range(2):
            for q in range(1, N):
                h = (c + e) % 2
                s["step"].append(fill(c, 1, place(c, h, q) - place(c, h, q - 1), lambda T, p, q=q: T.step[p, q:q + 1], slice(64 * e, 64 * e + 64)))
        s["eq"] = [QZ(c, 128, [s["zt"], s["x1_0"]], quant(("eq", "ep"), 128 * b, 128, lambda T, b=b: T.zt[:, 4 - b:516 - b])) for b in range(4)]
        s["made"] = [s[k] for k in ("neg", "mask", "rs")] + s["aw"] + s["one"] + s["z"] + s["step"] + s["eq"] + s["gap"]

    def listed(c, tag, vals, deps, out, fold, deps2, low, es=(0, 1), w=4):
        n = 32 * len(vals)
        p = slice(64 * es[0], 64 * es[-1] + 64)
        m0, r0, mask, rs = (0, 0, "mask", "rs") if w == 4 else (32, 192, "mask16", "rs16")
        lx, lt, ls = ["%s%s" % (b, tag) for b in ("lx", "lt", "ls")]
        m = [copy(c, 32, [deps[k], st[c][mask]], lambda T, k=k: T[lx][p, 32 * k:32 * k + 32], lambda T: T.mask[p, m0:m0 + 32], vals[k]) for k in range(len(vals))]
        t = V(c, n, m, lambda g, T: g.vector.transpose(T[lt][p, 0:n], T[lx][p, 0:n]))
        z = V(c, n, [t, st[c][rs]], lambda g, T: g.vector.tensor_tensor_scan(T[ls][p, 0:n], T.rs[p, r0:r0 + n], T[lt][p, 0:n], 0.0, A.mult, A.add))
        cv = [V(c, n // 4, [z] + deps2, lambda g, T, e=e: fold(g, T, out(T, e), T[ls][64 * e:64 * e + 64, w - 1:n:w], e)) for e in es]
        q0 = V(c, n // 4, cv, lambda g, T: g.vector.tensor_copy(low(T, slice(0, 32), 1), low(T, slice(32, 64), 0)))
        if FAN:
            return [q0] + [V(c, n // 2, [q0], lambda g, T, a=a: g.vector.tensor_copy(low(T, slice(a, a + 32), None), low(T, slice(0, 32), None))) for a in (32, 64, 96)]
        q1 = V(c, n // 2, [q0], lambda g, T: g.vector.tensor_copy(low(T, slice(32, 64), None), low(T, slice(0, 32), None)))
        return [V(c, n // 2, [q1], lambda g, T: g.vector.tensor_copy(low(T, slice(64, 128), None), low(T, slice(0, 64), None)))]

    banks = [[None] * 8 for _ in R]
    turn = [0] * N
    pairs = {s: [[[], []] for _ in R] for s in (1, 2)}
    cands = {s: [[[] for _ in SENDS[s]] for _ in R] for s in (1, 2)}

    def search(c, stage):
        s = st[c]
        rm, gt, ct = "rm%d" % stage, "gt%d" % stage, "ct%d" % stage
        flat = [0 if WHOLE[stage] else "O"] + [k for l in LISTS[stage] for k in l]
        at = {k: 516 * i for i, k in enumerate(flat)}
        sg = {}
        for i, k in enumerate(flat):
            if WHOLE[stage]:
                col, need = 128 * k, [s["x%d_%d" % (stage, k)]]
            else:
                col = 64 if k == "O" else 128 + 128 * TILES.index(k)
                need = [s["x%d_%d_%d" % (stage, h, d)] for d, h in halves(k)]
            bank = turn[c] % 4
            turn[c] += 1
            ps = lambda T, bank=bank: T.ps[:, 512 * bank:512 * bank + 512]
            m = MM(c, 512, need + s["qc%d" % stage] + [banks[c][bank]], lambda g, T, col=col, ps=ps: g.tensor.matmul_mx(
                ps(T), T["xq%d" % stage][:, col:col + 128], T["xp%d" % stage][:, col:col + 128], T["cq%d" % stage][:], T["cp%d" % stage][:], True, True))
            a = at[k]
            sc = V(c, 512, [m] + s["made"], lambda g, T, a=a, ps=ps: g.vector.tensor_tensor_scan(T[rm][:, a:a + 512], ps(T), T.neg[:], -1e29, A.max, A.max))
            banks[c][bank] = sc
            s["scan%d_%d" % (stage, i)] = sc
            sg[k] = S(c, 512, [sc], lambda g, T, a=a, i=i: g.scalar.activation(
                T["jk%d" % stage][:, 512 * i:512 * i + 512], T[rm][:, a:a + 512], F.Sign, bias=T[rm][:, a + 511:a + 512], scale=-1.0, accum_out=T[rm][:, a + 512:a + 513]))
        pair = lambda k, p=slice(0, 128): lambda T: T[rm][p, at[k] + 511:at[k] + 513]
        land = lambda e, p=slice(0, 128): lambda T: T["sc%d" % stage][p, 4 * c + 2 * e:4 * c + 2 * e + 2]
        if WHOLE[stage]:
            pp = [("pair%d" % stage, pair(k), [((c + k) % N, land(0))]) for k in flat if k]
            s["own%d" % stage] = [copy(c, 2, [sg[0]], land(0), pair(0))]
        else:
            pp = [("pair%d" % stage, pair(k), [((c + d) % N, land(side(c + d, h))) for d, h in halves(k)]) for k in flat if k != "O"]
            s["own%d" % stage] = [copy(c, 2, [sg["O"]], land(e, slice(64 * e, 64 * e + 64)), pair("O", slice(64 * e, 64 * e + 64))) for e in range(2)]
        word = lambda T: T[rm][:, 512:513]
        s["hop%d" % stage] = [X(c, 1, [sg[flat[0]]] + s["step"] + s.get("pv", []),
                                lambda g, T, k=k, m=m: g.vector.tensor_scalar(T.step[:, c + k:c + k + 1], word(T), m, T.pf[:, 4 + k:5 + k], A.mult, A.add),
                                lambda g, T, k=k, m=m: g.scalar.activation(T.step[:, c + k:c + k + 1], word(T), F.Identity, bias=T.pf[:, 4 + k:5 + k], scale=m)) for k, m in ((0, 1.0), (1, -1.0))]
        rest = [k for k in flat if k not in (0, "O")]
        for h in range(2 if SPLIT[stage] else 1):
            pick = [i for i, k in enumerate(rest) if not SPLIT[stage] or (k == "F" or k[0] == 0) == (h == 0)]
            o = send(c, 8, [("pair%d_%d" % (stage, h),) + pp[i][1:] for i in pick], [sg[rest[i]] for i in pick])
            for r in R:
                if r != c:
                    pairs[stage][r][h].append(o)
        where = {}
        for i, l in enumerate(LISTS[stage]):
            off, n = "off%d_%d" % (stage, i), 16 * len(l)
            ls = listed(c, "%d_%d" % (stage, i), [lambda T, k=k: T[rm][:, at[k] + 512:at[k] + 513] for k in l], [sg[k] for k in l],
                        lambda T, e, off=off, n=n: T[off][0:64, n * e:n * e + n:2],
                        lambda g, T, o, f, e: g.vector.tensor_scalar(o, f, 4.0, T.pf[64 * e:64 * e + 64, 0:1], A.mult, A.add), [s["acol"]],
                        lambda T, p, e, off=off, n=n: T[off][p, 0:2 * n] if e is None else T[off][p, e:2 * n:2])
            for j, k in enumerate(l):
                where[k] = (off, n, j, ls)
        of = {dh: (dh[0] if WHOLE[stage] else t) for t in TILES for dh in halves(t)}
        col = [128]

        def pack(groups, buf, a):
            ga, got_, c0 = [], {}, col[0]
            both = len(groups) == 2 and groups[0][0][0] == groups[1][0][0]
            for i, l in enumerate(groups):
                e = side(c + l[0][0], l[0][1])
                off, n, j, ls = where[of[l[0]]]
                o, m, x = n * e + 16 * j, len(l), (c0 + 64 * e if both else col[0])
                ga.append(copy(c, 256 * m, ls + s["ld%d" % stage], lambda T, x=x, m=m: T[gt][:, 4 * x:4 * x + 256 * m],
                               lambda T, off=off, o=o, m=m: T[ct][:, 0:4 * K].indirect(T[off][:, o:o + 16 * m]), None, True))
                for k, dh in enumerate(l):
                    got_[dh] = a + x - c0 + 64 * k
                col[0] += 64 * m
            n = col[0] - c0
            return QZ(c, n, ga, quant(buf, a, n, lambda T: T[gt][:, 4 * c0:4 * c0 + 4 * n])), got_
        for i, l in enumerate(SENDS[stage]):
            sem = "wa%d_%d" % (stage, i)
            qs, cols = [], {}
            for groups in l:
                q, x = pack(groups, OQ(stage), col[0] - 128)
                qs.append(q)
                cols.update(x)
            if l == [FAR]:
                w = send_mx(c, 128, [(sem, OQ(stage), min(cols.values()), [((c + N // 2) % N, WQ(stage), 128)])], qs)
            else:
                w = send_mx(c, 64, [(sem, OQ(stage), x, [((c + d) % N, WQ(stage), 128 + 64 * side(c + d, h) if d == N // 2 else 256 + 256 * h + 64 * SLOTS.index(d))])
                                    for (d, h), x in cols.items()], qs)
            for r in sorted(set((c + d) % N for d, _ in cols)):
                cands[stage][r][i] += w

    def finish(c, stage):
        s = st[c]
        dc, sc, win, of = "dc%d" % stage, "sc%d" % stage, "win", "of%d" % stage
        pa = [arrive(c, "pair%d_%d" % (stage, h), pairs[stage][c][h]) for h in range(2 if SPLIT[stage] else 1)]
        first = pa[:1] + s["own%d" % stage]
        pa = pa + s["own%d" % stage]
        sides = [(slice(0, 128), 0)] if WHOLE[stage] else [(slice(0, 64), 0), (slice(64, 128), 2)]
        if SPLIT[stage]:
            sides = [sides[side(c, h)] for h in range(2)]
        rm = [V(c, 6, (first if SPLIT[stage] and h == 0 else pa) + [s["neg"]], lambda g, T, p=p, a=a: g.vector.tensor_tensor_scan(
            T[dc][p, 0:N], T[sc][p, a::4], T.neg[p, 0:N], -1e29, A.max, A.max)) for h, (p, a) in enumerate(sides)]
        lts, lss, u = [], [], (2 if PLANES else 8)
        for h in range(2 if SPLIT[stage] else 1):
            p, es, w = (sides[h][0], (side(c, h),), side(c, h)) if SPLIT[stage] else (slice(0, 128), (0, 1), slice(0, 2))
            lt = V(c, 6, rm[h:h + 1] if SPLIT[stage] else rm, lambda g, T, p=p: g.vector.tensor_scalar(T[dc][p, 9:9 + N], T[dc][p, 0:N], T[dc][p, N - 1:N], None, A.is_lt))
            pv = V(c, 6, [lt] + s["one"] + s["hop%d" % stage], lambda g, T, p=p: g.vector.tensor_tensor(T[dc][p, 16:16 + N], T[dc][p, 8:8 + N], T.step[p, 0:N], A.mult))
            v = V(c, 6, [pv], lambda g, T, p=p: g.vector.tensor_reduce(T[dc][p, 7:8], T[dc][p, 16:16 + N], AxisListType.X, A.add))
            lss.append(listed(c, "%d_%d" % (stage, N), [lambda T, p=p: T[dc][p, 7:8]], [v], lambda T, e: T[of][0:64, e, 0:u],
                              lambda g, T, o, f, e: g.vector.tensor_scalar(o, f, float(place(c, (c + e) % 2, 0)) if PLANES else T.pf[64 * e:64 * e + 64, 1:2], None, A.add), s["aw"],
                              lambda T, p, e, w=w: T[of][p, w, :] if e is None else T[of][p, w, u * e:u * e + u], es, 32 // u))
            lts.append(lt)
            s.setdefault("pv", []).append(pv)
        gn = [V(c, 6, pa + [s["q512"]], lambda g, T, p=p, a=a: g.vector.tensor_tensor(T[dc][p, 24:24 + N], T[sc][p, a + 1::4], T.q512[p, 0:N], A.add)) for p, a in sides]
        oh = V(c, 6, lts + s["one"], lambda g, T: g.vector.tensor_tensor(T[dc][:, 32:32 + N], T[dc][:, 8:8 + N], T[dc][:, 9:9 + N], A.subtract))
        pr = V(c, 6, gn + [oh], lambda g, T: g.vector.tensor_tensor(T[dc][:, 40:40 + N], T[dc][:, 24:24 + N], T[dc][:, 32:32 + N], A.mult))
        nu = V(c, 6, [pr], lambda g, T: g.vector.tensor_reduce(T[dc][:, 48:49], T[dc][:, 40:40 + N], AxisListType.X, A.add))
        s["no%d" % stage] = [(dep, lambda g, T, row=row, cc=cc: g.sync.dma_start(T.no[row:row + 1, :], T[dc][:, cc:cc + 1])) for row, cc, dep in ((stage - 1, 48, [nu]), (stage + 1, N - 1, rm))]
        n = K // len(s["qc%d" % stage])
        runs = [(q, n * i, n, 256 + n * i, (0, 1)) for i, q in enumerate(s["qc%d" % stage])]
        book = len(runs)
        for i, l in enumerate(SENDS[stage]):
            wa = arrive(c, "wa%d_%d" % (stage, i), cands[stage][c][i])
            if FAR in l:
                runs.append((wa, 128, 128, 256 + K, (0, 1)))
            for h in range(2):
                k = [SLOTS.index(d) for p in l if p != FAR for x in p for d, e in x if e == h]
                if k:
                    runs.append((wa, 256 + 256 * h + 64 * min(k), 64 * len(k), RW * h + 64 * min(k), (0, 1)[h:]))
        cps = [[[], [], [], []] for h in range(2)]
        for i, (dep, a, n, o, hs) in enumerate(runs):
            for b in range(4):
                bank = b + 4 * ((i - book + 1 + stage) % 2 if i >= book else 1)
                q = "w" if i >= book else "c"
                mm = MM(c, n, [dep, s["eq"][b], banks[c][bank]], lambda g, T, b=b, a=a, n=n, bank=bank, q=q: g.tensor.matmul_mx(
                    T.ps[:, 512 * bank:512 * bank + n], T.eq[:, 128 * b:128 * b + 128], T.ep[:, 128 * b:128 * b + 128],
                    T["%sq%d" % (q, stage)][:, a:a + n], T["%sp%d" % (q, stage)][:, a:a + n], True, True))
                cp = copy(c, n, [mm] + (s["r0"] + s["r1"] if stage == 2 else []), lambda T, b=b, o=o, n=n: T[win][:, PW * b + o:PW * b + o + n], lambda T, bank=bank, n=n: T.ps[:, 512 * bank:512 * bank + n], lambda T: -1.0)
                banks[c][bank] = cp
                if b == 0:
                    s["landed"] = mm
                for h in hs:
                    cps[h][b].append(cp)
        for h in range(2):
            e = side(c, h)
            ls = lss[h % len(lss)]
            to, fr = (("rt", 256), ("xt", 0)) if stage == 1 else (("yt", 0), ("rt", 256))
            cut = lambda T, v, b, e=e: T[v[0]][:, v[1] + 256 * e + b:v[1] + 256 * e + 256:4]
            base = ls + ([s["ldx"]] if stage == 1 else s["r%d" % h])
            if PLANES:
                r = [op(c, "V", 0.05 + 64 * E["sg"], cps[h][b] + base, lambda g, T, b=b, h=h, e=e, to=to, fr=fr, cut=cut: g.vector.tensor_tensor(
                    cut(T, to, b), T[win][:, BW * (3 * b + h):BW * (3 * b + h + 2)].indirect(T[of][:, e, :]), cut(T, fr, b), A.add)) for b in range(4)]
            else:
                n = 256 // (1 if stage == 1 else PIECES[h])
                r = [op(c, "V", 0.05 + n * E["sg"], sum(cps[h], []) + base, lambda g, T, a=a, n=n, h=h, e=e, to=to, fr=fr: g.vector.tensor_tensor(
                    T[to[0]][:, to[1] + 256 * e + a:to[1] + 256 * e + a + n], T[win][:, 0:(7 * BW + 256 if h else RW)].indirect(T[of][:, e, a // 16:(a + n) // 16]),
                    T[fr[0]][:, fr[1] + 256 * e + a:fr[1] + 256 * e + a + n], A.add)) for a in range(0, 256, n)]
            if stage == 1:
                s["r%d" % h] = r
                q2 = QZ(c, 128, r + s["z"], quant(XQ(2), 128 * e, 128, lambda T, e=e: T.rt[:, 512 * e:512 * e + 512]))
                s["x2_%d_0" % h] = q2
                ops[q2]["ahead"] = h == 0
                spread_half(c, 2, h)
            else:
                n = 256 // PIECES[h]
                for k in range(PIECES[h]):
                    a = 256 * e + n * k
                    y = r if PLANES else r[k:k + 1]
                    if k % 2 == 0:
                        D(c, "Y", 4 * n, y, lambda g, T, a=a, n=n: g.sync.dma_start(T.y[:, a:a + n], T.yt[:, a:a + n]), "st")
                    else:
                        D(c, "S", 4 * n, y, lambda g, T, a=a, n=n: g.scalar.dma_start(T.y[:, a:a + n], T.yt[:, a:a + n]), "st")

    for stage in (1, 2):
        for c in R:
            search(c, stage)
            if stage == 1:
                s = st[c]
                s["ld2"] = [D(c, "Y", 4096, [s["scan1_1"]], lambda g, T: g.sync.dma_start(T.ct2[:], T.c2[:]), "ld_c2_0")]
                s["qc2"] = [QZ(c, 512, s["ld2"], quant(("cq2", "cp2"), 0, 512, lambda T: T.ct2[:]))]
        for c in R:
            finish(c, stage)
    for c in R:
        for stage, when in ((1, "scan2_1"), (2, "landed")):
            for dep, emit in st[c]["no%d" % stage]:
                D(c, "Y", 4, dep + [st[c][when]], emit, "st")
    for o in arr:
        ops[o]["sem"] = (ops[o]["sem"], got[(ops[o]["c"], ops[o]["sem"])])
    return ops, got


def alike(ops):
    per = [[i for i, o in enumerate(ops) if o["c"] == c and o["kind"] != "a"] for c in range(N)]
    back = {}
    for l in per:
        for k, i in enumerate(l):
            back[i] = per[LEAD][k]
    ids = per[LEAD] + [i for i, o in enumerate(ops) if o["c"] == LEAD and o["kind"] == "a"]
    at = {i: k for k, i in enumerate(ids)}
    return per, ids, [sorted(set(at[back.get(d, d)] for d in ops[i]["deps"])) for i in ids]


def draw_up(topo, cores):
    ops, got = build(topo, cores, SETS[0])
    per, ids, deps = alike(ops)
    n = len(ids)
    R = range(n)
    sets = []
    for E in SETS:
        full = build(topo, cores, E)[0]
        lead = [full[i] for i in ids]
        sets.append(([{q: v[0] for q, v in o["alt"].items()} if "alt" in o else {o["q"]: o["dur"]} for o in lead], [o["lat"] for o in lead], E["wake"]))
    lead = [ops[i] for i in ids]
    alt = ["alt" in o for o in lead]
    home = [o["q"] for o in lead]
    free_of_wake = [o["kind"] in "wa" for o in lead]
    succ = [[] for _ in R]
    for i in R:
        for d in deps[i]:
            succ[d].append(i)
    cnt = [len(d) for d in deps]
    top = [i for i in R if cnt[i] == 0]
    for i in top:
        for j in succ[i]:
            cnt[j] -= 1
            if cnt[j] == 0:
                top.append(j)
    rank = [0.0] * n
    for j in reversed(top):
        rank[j] = min(sets[0][0][j].values()) + sets[0][1][j] + sets[0][2] + max([rank[k] for k in succ[j]] + [0.0])

    def order(nudge, pin, favour):
        dur, lat, wake = sets[0]
        todo = [len(d) for d in deps]
        at = [0.0] * n
        ready = {q: [] for q in ("V", "S", "P", "G", "Y", "D", None)}
        free = {q: 0.0 for q in ready}
        seq = {q: [] for q in ready}
        qof = [None] * n
        pr = [rank[i] + nudge[i] for i in R]

        def add(i):
            if not alt[i]:
                ready[home[i]].append(i)
                return
            for q in ("V", "S"):
                if pin[i] in (None, q):
                    ready[q].append(i)
        for i in R:
            if todo[i] == 0:
                add(i)
        for _ in R:
            bt, bq = 1e9, None
            for q, l in ready.items():
                if l:
                    t = min([at[i] for i in l])
                    if q and free[q] > t:
                        t = free[q]
                    if t < bt:
                        bt, bq = t, q
            i, bp = -1, -1e9
            for j in ready[bq]:
                if at[j] <= bt:
                    p = -at[j] if bq == "D" else pr[j] - (favour if bq == "V" and alt[j] else 0.0)
                    if p > bp:
                        i, bp = j, p
            ready[bq].remove(i)
            if alt[i]:
                o = "S" if bq == "V" else "V"
                if i in ready[o]:
                    ready[o].remove(i)
            qof[i] = bq
            e = bt + dur[i][bq]
            if bq:
                free[bq] = e
            seq[bq].append(i)
            for k in succ[i]:
                todo[k] -= 1
                at[k] = max(at[k], e + lat[i] + (0.0 if free_of_wake[k] else wake))
                if todo[k] == 0:
                    add(k)
        return seq, qof

    def span(seq, qof, which):
        dur, lat, wake = sets[which]
        todo = [len(d) for d in deps]
        at = [0.0] * n
        pos = {q: 0 for q in seq}
        free = {q: 0.0 for q in seq}
        end = 0.0
        land = [i for i in R if qof[i] is None and todo[i] == 0]
        moved = True
        while moved:
            moved = False
            for q, l in seq.items():
                while (land if q is None else pos[q] < len(l) and todo[l[pos[q]]] == 0):
                    i = land.pop() if q is None else l[pos[q]]
                    pos[q] += 1
                    e = at[i] if q is None else max(at[i], free[q]) + dur[i][q]
                    free[q] = e
                    moved = True
                    d = e + lat[i]
                    if d > end:
                        end = d
                    for k in succ[i]:
                        todo[k] -= 1
                        a = d + (0.0 if free_of_wake[k] else wake)
                        if a > at[k]:
                            at[k] = a
                        if todo[k] == 0 and qof[k] is None:
                            land.append(k)
        return end

    seed = [12345]

    def draw(m):
        seed[0] = (seed[0] * 1103515245 + 12345) % (1 << 31)
        return (seed[0] >> 8) % m

    work = [i for i in R if home[i] in ("V", "S", "P", "G")]
    both = [i for i in work if alt[i]]
    cur = ([0.0] * n, [None] * n, 1.0)
    kept = order(*cur)
    base = [span(kept[0], kept[1], k) for k in range(len(SETS))]
    now = best = 1.0
    for step in range(STEPS):
        nudge, pin, favour = list(cur[0]), list(cur[1]), cur[2]
        k = draw(100)
        if k < 60:
            for _ in range(1 + draw(3)):
                nudge[work[draw(len(work))]] = (draw(61) - 30) / 10.0 if draw(10) < 7 else 0.0
        elif k < 75:
            a, d = draw(len(work)), (draw(51) - 25) / 10.0
            for i in work[a:a + 3 + draw(38)]:
                nudge[i] += d
        elif k < 97:
            for _ in range(1 + draw(3)):
                pin[both[draw(len(both))]] = (None, "V", "S")[draw(3)]
        else:
            favour = (0.0, 0.5, 1.0, 1.5, 2.0, 3.0)[draw(6)]
        so = order(nudge, pin, favour)
        v = sum(span(so[0], so[1], k) / base[k] for k in range(len(SETS))) / len(SETS)
        if v <= now + 0.003 * max(0.0, 1.0 - step / (0.9 * STEPS)) * draw(1000) / 1000.0:
            cur, now = (nudge, pin, favour), v
            if v < best:
                best, kept = v, so
    seq = {}
    for c in range(N):
        for q, l in kept[0].items():
            if q:
                seq[(c, q)] = [per[c][k] for k in l]
        for k in both:
            o = ops[per[c][k]]
            o["q"] = kept[1][k]
            o["emit"] = o["alt"][o["q"]][1]
    return ops, got, seq, [span(kept[0], kept[1], k) for k in range(len(SETS))]


def draw_up(topo, cores):
    ops, got = build(topo, cores, SETS[0])
    per, ids, deps = alike(ops)
    n = len(ids)
    R = range(n)
    sets = []
    for E in SETS:
        full = build(topo, cores, E)[0]
        lead = [full[i] for i in ids]
        sets.append(([{q: v[0] for q, v in o["alt"].items()} if "alt" in o else {o["q"]: o["dur"]} for o in lead], [o["lat"] for o in lead], E["wake"]))
    lead = [ops[i] for i in ids]
    alt = ["alt" in o for o in lead]
    home = [o["q"] for o in lead]
    auto = [o["kind"] in "wa" for o in lead]
    succ = [[] for _ in R]
    for i in R:
        for d in deps[i]:
            succ[d].append(i)
    count = [len(d) for d in deps]
    cnt = list(count)
    top = [i for i in R if cnt[i] == 0]
    for i in top:
        for j in succ[i]:
            cnt[j] -= 1
            if cnt[j] == 0:
                top.append(j)
    rank = [0.0] * n
    for j in reversed(top):
        rank[j] = min(sets[0][0][j].values()) + sets[0][1][j] + sets[0][2] + max([rank[x] for x in succ[j]] + [0.0])
    above = [set() for _ in R]
    for j in top:
        for d in deps[j]:
            above[j] |= above[d] | {d}
    for j in set().union(*[above[i] | {i} for i in R if lead[i].get("ahead")]):
        rank[j] += AHEAD
    Q = "VSPGY"

    def run(seq, which, pr=None, pin=None):
        dur, lat, wake = sets[which]
        todo = list(count)
        at = [0.0] * n
        start = [0.0] * n
        why = [-1] * n
        free = dict.fromkeys(Q, 0.0)
        last = dict.fromkeys(Q + "D", -1)
        pos = dict.fromkeys(Q, 0)
        wire = end = total = 0.0
        if pr:
            ready = {q: [] for q in Q}
            where = [[pin[i]] if pin[i] else list(dur[i]) for i in R]
            for i in R:
                if not count[i]:
                    for q in where[i]:
                        ready[q].append(i)
        left = n
        while left:
            bt, bq, i = 1e9, None, -1
            if pr:
                for q in Q:
                    if ready[q]:
                        t = max(free[q], min([at[j] for j in ready[q]]))
                        if t < bt:
                            bt, bq = t, q
                bp = -1e9
                for j in ready[bq]:
                    if at[j] <= bt + LOOK:
                        p = pr[j] - (0.5 if bq == "V" and alt[j] else 0.0)
                        if p > bp:
                            i, bp = j, p
                bt = max(bt, at[i])
                for q in where[i]:
                    ready[q].remove(i)
                seq[bq].append(i)
            else:
                for q in Q:
                    l = seq[q]
                    p = pos[q]
                    if p < len(l):
                        j = l[p]
                        if not todo[j]:
                            t = at[j] if at[j] > free[q] else free[q]
                            if t < bt:
                                bt, bq, i = t, q, j
                if bq is None:
                    return None
                pos[bq] += 1
            if bt > at[i]:
                why[i] = last[bq]
            last[bq] = i
            start[i] = bt
            e = free[bq] = bt + dur[i][bq]
            total += e
            done = [(i, e)]
            while done:
                j, e = done.pop()
                left -= 1
                if e > end:
                    end, fin = e, j
                for x in succ[j]:
                    todo[x] -= 1
                    a = e if auto[x] else e + wake
                    if a > at[x]:
                        at[x] = a
                        why[x] = j
                    if not todo[x]:
                        if home[x] == "D":
                            if wire > at[x]:
                                why[x] = last["D"]
                            last["D"] = x
                            wire = (at[x] if at[x] > wire else wire) + dur[x]["D"]
                            start[x] = wire - dur[x]["D"]
                            done.append((x, wire + lat[x]))
                        elif auto[x]:
                            done.append((x, at[x]))
                        elif pr:
                            for q in where[x]:
                                ready[q].append(x)
        return end, total / n, start, why, fin

    seed = [SEED]

    def draw(m):
        seed[0] = (seed[0] * 1103515245 + 12345) % (1 << 31)
        return (seed[0] >> 8) % m

    seq = {q: [] for q in Q}
    run(seq, 0, rank, [None] * n)
    base = [run(seq, x)[0] * len(SETS) for x in range(len(SETS))]

    def worth(seq, was=None, room=0.0):
        v, rs = [], []
        for x in range(len(SETS)):
            r = run(seq, x)
            if r is None:
                return None, None
            rs.append(r)
            v.append((r[0] + 0.1 * r[1]) / base[x])
            if was and x == 0 and v[0] > was[0] + room + 0.001:
                return None, None
        return v, rs
    now, rs = worth(seq)
    best, kept = sum(now), seq
    work = [i for i in R if not auto[i]]
    both = [i for i in work if alt[i]]
    cur = (list(rank), [None] * n)
    for step in range(DRAFTS):
        pr, pin = list(cur[0]), list(cur[1])
        x = draw(100)
        if x < 35:
            for _ in range(1 + draw(3)):
                pr[work[draw(len(work))]] += (draw(41) - 20) / 10.0
        elif x < 50:
            a, d = draw(len(work)), (draw(41) - 20) / 10.0
            for i in work[a:a + 3 + draw(30)]:
                pr[i] += d
        elif x < 75:
            i, d, far = work[draw(len(work))], (draw(41) - 20) / 10.0, draw(50) / 10.0
            for j in above[i] | {i}:
                if rank[j] - rank[i] <= far:
                    pr[j] += d
        else:
            for _ in range(1 + draw(3)):
                pin[both[draw(len(both))]] = (None, "V", "S")[draw(3)]
        new = {q: [] for q in Q}
        run(new, 0, pr, pin)
        room = 0.004 * max(0.0, 1.0 - step / (0.9 * DRAFTS)) * draw(1000) / 1000.0
        v, s = worth(new, now, room)
        if v and sum(v) <= sum(now) + room:
            cur, now = (pr, pin), v
            if sum(v) < best:
                best, kept = sum(v), new
    seq = kept
    now, rs = worth(seq)

    def chain(r):
        l, j = [], r[4]
        while j >= 0:
            if not auto[j]:
                l.append(j)
            j = r[3][j]
        return l
    crit = [chain(r) for r in rs]
    for step in range(STEPS):
        start = rs[0][2]
        l = crit[draw(len(crit))] if draw(2) else work
        i = l[draw(len(l))]
        q = [x for x in Q if i in seq[x]][0]
        to = ("S" if q == "V" else "V") if alt[i] and draw(3) == 0 else q
        new = dict(seq)
        new[q] = list(seq[q])
        p = new[q].index(i)
        if to != q:
            new[q].pop(p)
            new[to] = list(seq[to])
            p = len([j for j in new[to] if start[j] < start[i]]) + draw(3) - 1
            new[to].insert(max(0, p), i)
            near = [j for j in new[to][max(0, p - 3):p + 4] if alt[j] and j != i]
            if near and draw(2):
                j = near[draw(len(near))]
                new[to].remove(j)
                new[q].insert(len([x for x in new[q] if start[x] < start[j]]), j)
        else:
            m = 1 if draw(3) else 1 + draw(4)
            piece = new[q][p:p + m]
            del new[q][p:p + m]
            d = 1 + draw(2 if draw(2) else 10)
            p = max(0, p - d) if draw(2) else p + d
            new[q][p:p] = piece
        room = HEAT * max(0.0, 1.0 - step / (0.9 * STEPS)) * draw(1000) / 1000.0
        v, s = worth(new, now, room)
        if v and sum(v) <= sum(now) + room:
            seq, now, rs = new, v, s
            crit = [chain(r) for r in rs]
            if sum(v) < best:
                best, kept = sum(v), new
    out = {}
    start = run(kept, 0)[2]
    kept = dict(kept)
    kept["D"] = sorted([i for i in R if home[i] == "D"], key=lambda i: start[i])
    for c in range(N):
        for q, l in kept.items():
            out[(c, q)] = [per[c][x] for x in l]
            for x in l:
                o = ops[per[c][x]]
                if alt[x]:
                    o["q"] = q
                    o["emit"] = o["alt"][q][1]
    return ops, got, out, [run(kept, x)[0] for x in range(len(SETS))]


def plan(topo, cores):
    if "plan" not in _memo:
        _memo["plan"] = draw_up(topo, cores)
    return _memo["plan"]


def rank_program(g, core, T, topo):
    rank = T.rank_of(core)
    if rank is None:
        return
    ops, got, seq, _ = plan(topo, list(T.cores))
    queues = {"V": g.vector, "S": g.scalar, "P": g.tensor, "G": g, "Y": g.sync}
    num = {}
    tot = {k[1]: v for k, v in got.items() if k[0] == rank}
    for q in CSEM:
        k = 0
        for i in seq.get((rank, q), []):
            if ops[i]["kind"] == "c":
                k += 1
                num[i] = (CSEM[q], k)
        tot[CSEM[q]] = k
    known = {q: {} for q in queues}
    snap = {}
    pos = {q: 0 for q in queues}
    mine = sum(len(seq.get((rank, q), [])) for q in queues)
    made = lambda d: ops[d]["by"] in snap if ops[d]["by"] is not None else (ops[d]["kind"] == "a" or d in snap)
    while mine:
        moved = False
        for q in queues:
            lst = seq.get((rank, q), [])
            while pos[q] < len(lst) and all(made(d) for d in ops[lst[pos[q]]]["deps"]):
                i = lst[pos[q]]
                o = ops[i]
                need = {}
                for d in o["deps"]:
                    if ops[d]["kind"] == "r":
                        continue
                    name, cnt = num[d] if ops[d]["kind"] == "c" else ops[d]["sem"]
                    if need.get(name, (0, None))[0] < cnt:
                        need[name] = (cnt, snap.get(d))
                for name in sorted(need, key=lambda t: -len(need[t][1] or {})):
                    cnt, sn = need[name]
                    if known[q].get(name, 0) < cnt:
                        queues[q].wait_ge(T.sem[name], cnt)
                        known[q][name] = cnt
                        for k2, v2 in (sn or {}).items():
                            known[q][k2] = max(known[q].get(k2, 0), v2)
                ins = o["emit"](g, T)
                if o["kind"] == "c":
                    ins.then_inc(T.sem[num[i][0]], 1)
                elif o["kind"] == "d":
                    ins.then_inc(T.sem[o["sem"]], 16)
                snap[i] = dict(known[q])
                pos[q] += 1
                mine -= 1
                moved = True
        if not moved:
            raise ValueError("the plan does not close")
    for name in sorted(SEMAPHORES, key=lambda t: (t == "st", t in CSEM.values())):
        if tot.get(name, 0) > known["G"].get(name, 0):
            g.wait_ge(T.sem[name], tot[name])
